import numpy as np
import ml_dtypes


def mxq(x, axis, fmt="e4m3"):
    dtype, down = {"e4m3": (ml_dtypes.float8_e4m3fn, 7), "e5m2": (ml_dtypes.float8_e5m2, 14)}[fmt]
    v = np.moveaxis(np.asarray(x, np.float32).astype(ml_dtypes.bfloat16).astype(np.float64), axis, -1)
    blocks = v.reshape(v.shape[:-1] + (-1, 32))
    amax = np.abs(blocks).max(-1, keepdims=True)
    byte = np.maximum(np.where(amax > 0, np.frexp(amax)[1] - 1 + 127, 0) - down, 1)
    scale = np.exp2(byte - 127.0)
    codes = (blocks / scale).astype(np.float32).astype(dtype).astype(np.float64)
    return np.moveaxis((codes * scale).reshape(v.shape), -1, axis)


WIDE = False


def mx_kscale(k):
    if not WIDE:
        return np.ones(k)
    levels = np.array([10, -10, 5, -5, 0])
    if k % 512:
        return np.exp2(np.random.permutation(np.resize(levels, k // 32))).repeat(32)
    a = np.empty((k // 512, 16))
    for p in range(k // 512):
        a[p, :8] = np.random.permutation(np.resize(levels, 8))
        for g in range(8):
            far = levels[np.abs(levels - a[p, g]) >= 10]
            a[p, g + 8] = far[np.random.randint(len(far))]
    return np.exp2(a.ravel()).repeat(32)


def f64(x):
    return np.asarray(x).astype(np.float64)


def striped(idx):
    return np.tile(idx.reshape(-1, 16).T, (8, 1)).astype(np.uint16)


def unstriped(offs):
    return offs[:16].T.reshape(-1).astype(np.int64)


def pack_weight(w):
    k, n = w.shape
    w = f64(np.asarray(w, np.float32).astype(ml_dtypes.bfloat16)).reshape(k // 32, 32, n)
    amax = np.abs(w).max(1)
    byte = np.clip(np.where(amax > 0, np.frexp(amax)[1] - 1 + 127 - 7, 1), 1, 254)
    scaled = (w * np.exp2(127.0 - byte)[:, None, :]).reshape(k, n).astype(np.float32)
    words = np.ascontiguousarray(scaled.reshape(k // 512, 128, 4, n).transpose(0, 1, 3, 2)).astype(ml_dtypes.float8_e4m3fn).view(np.uint8)
    return words, np.ascontiguousarray(byte.astype(np.uint8).reshape(k // 512, 16, n))


def unpack_weight(words, scales):
    g, p, n, _ = words.shape
    vals = np.ascontiguousarray(words).view(ml_dtypes.float8_e4m3fn).astype(np.float64) * np.repeat(np.exp2(scales.astype(np.float64) - 127.0), 8, axis=1)[..., None]
    return vals.transpose(0, 1, 3, 2).reshape(g * 512, n)


def relu(v):
    return np.maximum(v, 0.0)


K, T, S, V, H, N = 1024, 2048, 1024, 512, 512, 256


def setup_inputs():
    n = np.random.standard_normal
    s = mx_kscale(K)[:, None]
    u = mx_kscale(H)
    packed_xT = pack_weight(n((K, T)) * s)
    return {
        "x_words": packed_xT[0],
        "x_scales": packed_xT[1],
        "w1": (n((K, H)) / np.sqrt(2 * K) / s * u).astype(np.float32),
        "w2": (n((K, H)) / np.sqrt(2 * K) / s * u).astype(np.float32),
        "w3": (n((H, N)) / np.sqrt(H) / u[:, None]).astype(np.float32),
        "offs": striped(np.random.permutation(T)[:S]),
        "cen": striped(np.random.permutation(S)[:V]),
        "pos1": striped(np.random.permutation(S)[:V]),
        "pos2": striped(np.random.permutation(S)[:V]),
    }


def reference(x_words, x_scales, w1, w2, w3, offs, cen, pos1, pos2):
    xq = unpack_weight(x_words, x_scales)[:, unstriped(offs)]
    y = mxq(f64(w1), 0, "e4m3").T @ xq
    yc = y[:, unstriped(cen)]
    e = mxq(f64(w2), 0, "e4m3").T @ xq
    z = np.maximum(relu(yc + e[:, unstriped(pos1)]), relu(yc + e[:, unstriped(pos2)]))
    return mxq(f64(w3), 0, "e4m3").T @ mxq(z, 0, "e4m3")

@@ -1,0 +1,252 @@
+from contextlib import ExitStack
+
+import concourse.mybir as mybir
+
+K, T, S, V, H, N = 1024, 2048, 1024, 512, 512, 256
+FLOPS = 2 * (2 * K * H * S + H * N * V)
+
+F32 = mybir.dt.float32
+BF16 = mybir.dt.bfloat16
+I32 = mybir.dt.int32
+U32 = mybir.dt.uint32
+U16 = mybir.dt.uint16
+U8 = mybir.dt.uint8
+FP8X4 = mybir.dt.float8_e4m3fn_x4
+ACT = mybir.ActivationFunctionType
+ALU = mybir.AluOpType
+
+P = 128
+PACK = 4
+K_PASS = P * PACK
+PASSES = K // K_PASS
+BANK = 512
+HALVES = S // BANK
+LIST_ROWS = 16
+CHUNKS = (256, 128, 128)
+
+
+def tile_picked_edgecv_relu_p_kernel(
+    tc, x_words, x_scales, w1, w2, w3, offs, cen, pos1, pos2, out
+):
+    nc = tc.nc
+    with ExitStack() as ctx:
+        keep = ctx.enter_context(tc.tile_pool(name="keep", bufs=1))
+        psum = ctx.enter_context(tc.psum_pool(name="psum", bufs=1))
+
+        def load_list(name, src):
+            lst = keep.tile(list(src.shape), U16, name=name)
+            nc.sync.dma_start(lst[:], src)
+            return lst
+
+        def load_words(z):
+            table = keep.tile([P, T], U32, name=f"x_table{z}")
+            nc.sync.dma_start(
+                table[:].bitcast(I32), x_words[z].rearrange("p c r -> p (c r)").bitcast(I32)
+            )
+            return table
+
+        def load_weight(name, w, z):
+            raw = keep.tile([P, PACK, H], F32, name=f"{name}_raw{z}")
+            nc.sync.dma_start(
+                raw[:], w[z * K_PASS : (z + 1) * K_PASS, :].rearrange("(p j) c -> p j c", j=PACK)
+            )
+            return raw
+
+        scale_table = keep.tile([P, T], U8, name="scale_table")
+        nc.vector.memset(scale_table[:].bitcast(I32), 0)
+        offs_t = load_list("offs_t", offs)
+        x_table = [load_words(0)]
+        for q in range(4):
+            nc.sync.dma_start(
+                scale_table[32 * q : 32 * q + 4 * PASSES, :].bitcast(I32),
+                x_scales[:, 4 * q : 4 * q + 4, :].bitcast(I32),
+            )
+        w2_raw = [load_weight("w2", w2, 0)]
+        x_table.append(load_words(1))
+        w2_raw.append(load_weight("w2", w2, 1))
+        pos1_t = load_list("pos1_t", pos1)
+        pos2_t = load_list("pos2_t", pos2)
+        w1_raw = [load_weight("w1", w1, z) for z in range(PASSES)]
+        cen_t = load_list("cen_t", cen)
+        w3_raw = keep.tile([P, PACK, N], F32, name="w3_raw")
+        w3_rows = w3.rearrange("(a t i) n -> t a i n", t=PACK, i=4)
+        for t in range(PACK):
+            nc.sync.dma_start(w3_raw[:, t, :], w3_rows[t])
+
+        def pick_words(z):
+            picked = keep.tile([P, S], U32, name=f"x_code{z}", align_bytes=64)
+            nc.vector.tensor_copy(picked[:], x_table[z][:].indirect(offs_t[:]))
+            return picked
+
+        x_code = [pick_words(0)]
+
+        def pick_scales(h, tag):
+            picked = keep.tile([P, BANK], U8, name=f"x_scale{h}", tag=tag, align_bytes=64)
+            cols = BANK // LIST_ROWS
+            nc.vector.tensor_copy(picked[:], scale_table[:].indirect(offs_t[:, h * cols : (h + 1) * cols]))
+            return picked
+
+        x_scale = [pick_scales(0, "x_scale0")]
+
+        def interleave(on_vector, dst, src, func):
+            if on_vector:
+                if func == "relu":
+                    nc.vector.tensor_scalar_max(dst, src, 0.0)
+                else:
+                    nc.vector.tensor_copy(dst, src)
+            else:
+                nc.scalar.activation(dst, src, ACT.Relu if func == "relu" else ACT.Copy)
+
+        def cast_weight(name, raw, t, on_vector, tag=None):
+            grouped = keep.tile(
+                [P, K_PASS], BF16, name=f"{name}_bf{t}", tag=tag or f"{name}_bf{t}", align_bytes=64
+            )
+            interleave(
+                on_vector,
+                grouped[:].rearrange("p (a i j) -> p a j i", i=4, j=PACK),
+                raw[:].rearrange("p j (a t i) -> p t a j i", t=PACK, i=4)[:, t],
+                "copy",
+            )
+            return grouped
+
+        def quantize(name, grouped, tag=None):
+            width = grouped.shape[1] // PACK
+            codes = keep.tile([P, width], U32, name=f"{name}_code", tag=tag or f"{name}_code", align_bytes=64)
+            scales = keep.tile([P, width], U8, name=f"{name}_scale", tag=f"{name}_scale", align_bytes=64)
+            nc.vector.quantize_mx(out=codes[:].bitcast(FP8X4), scales=scales[:], in_=grouped[:])
+            return codes, scales
+
+        def open_banks(name, t):
+            return [
+                psum.tile([P, BANK], F32, name=f"{name}_acc{t}{h}", tag=f"bank{HALVES * t + h}")
+                for h in range(HALVES)
+            ]
+
+        def multiply(banks, wq, z):
+            codes, scales = wq
+            for h in range(HALVES):
+                cols = slice(h * BANK, (h + 1) * BANK)
+                nc.tensor.matmul_mx(
+                    out=banks[h][:],
+                    lhsT=codes[:].bitcast(FP8X4),
+                    lhsT_scale=scales[:],
+                    rhs=x_code[z][:, cols].bitcast(FP8X4),
+                    rhs_scale=x_scale[h][4 * z : P, :],
+                    start=(z == 0),
+                    stop=(z == PASSES - 1),
+                )
+
+        def evacuate(name, banks, last_on_vector=False):
+            rows = keep.tile([P, S], F32, name=name)
+            for h in range(HALVES):
+                cols = slice(h * BANK, (h + 1) * BANK)
+                if last_on_vector and h == HALVES - 1:
+                    nc.vector.tensor_copy(rows[:, cols], banks[h][:])
+                else:
+                    nc.scalar.activation(rows[:, cols], banks[h][:], ACT.Copy)
+            return rows
+
+        def neighbour_max(t, e_rows):
+            g1 = keep.tile([P, V], F32, name=f"g1_{t}")
+            g2 = keep.tile([P, V], F32, name=f"g2_{t}")
+            nc.vector.tensor_copy(g1[:], e_rows[:].indirect(pos1_t[:]))
+            nc.vector.tensor_copy(g2[:], e_rows[:].indirect(pos2_t[:]))
+            cut = CHUNKS[0] if t == PACK - 1 else V
+            head = keep.tile([P, cut], F32, name=f"best{t}", tag=f"best{t}", align_bytes=64)
+            nc.vector.tensor_tensor(head[:], g1[:, :cut], g2[:, :cut], ALU.max)
+            if cut == V:
+                return lambda a, b: head[:, a:b]
+            rest = keep.tile([P, V - cut], F32, name=f"best{t}_rest")
+            nc.vector.tensor_tensor(rest[:], g1[:, cut:], g2[:, cut:], ALU.max)
+            return lambda a, b: head[:, a:b] if b <= cut else rest[:, a - cut : b - cut]
+
+        e_banks = [open_banks("e", t) for t in range(PACK)]
+        first = [cast_weight("w2p0", w2_raw[0], t, False) for t in range(PACK)]
+        wq = quantize("w2p0t0", first[0])
+        x_scale.append(pick_scales(1, "w2p0_bf0"))
+        multiply(e_banks[0], wq, 0)
+        for t in (1, 2):
+            multiply(e_banks[t], quantize(f"w2p0t{t}", first[t]), 0)
+        x_code.append(pick_words(1))
+        g0 = cast_weight("w2p1", w2_raw[1], 0, False)
+        g1 = cast_weight("w2p1", w2_raw[1], 1, False)
+        multiply(e_banks[0], quantize("w2p1t0", g0), 1)
+        g2 = cast_weight("w2p1", w2_raw[1], 2, True, tag="w2p1_bf0")
+        multiply(e_banks[3], quantize("w2p0t3", first[3], tag="w2p0t2_code"), 0)
+        multiply(e_banks[1], quantize("w2p1t1", g1), 1)
+        g3 = cast_weight("w2p1", w2_raw[1], 3, True, tag="w2p1_bf1")
+        multiply(e_banks[2], quantize("w2p1t2", g2), 1)
+        multiply(e_banks[3], quantize("w2p1t3", g3), 1)
+
+        best = []
+        e0 = evacuate("e0", e_banks[0])
+        best.append(neighbour_max(0, e0))
+        e1 = evacuate("e1", e_banks[1])
+        best.append(neighbour_max(1, e1))
+        behind = ("w2p1t1_code", "w2p1t2_code", "w2p1t3_code", "w2p1t3_scale")
+        w1q0 = [
+            quantize(f"w1p0t{t}", cast_weight("w1p0", w1_raw[0], t, False, tag=behind[t]))
+            for t in range(PACK)
+        ]
+        e2 = evacuate("e2", e_banks[2])
+        best.append(neighbour_max(2, e2))
+        w1q1 = [
+            quantize(f"w1p1t{t}", cast_weight("w1p1", w1_raw[1], t, False, tag=behind[t]))
+            for t in range(PACK)
+        ]
+        e3 = evacuate("e3", e_banks[3])
+        best.append(neighbour_max(3, e3))
+
+        w3_bf = keep.tile([P, N * PACK], BF16, name="w3_bf", tag=behind[3], align_bytes=64)
+        interleave(
+            False,
+            w3_bf[:].rearrange("p (c i t) -> p c t i", i=4, t=PACK),
+            w3_raw[:].rearrange("p t (c i) -> p c t i", i=4),
+            "copy",
+        )
+        w3_code, w3_scale = quantize("w3", w3_bf)
+
+        y_rows = []
+        for t in range(PACK):
+            banks = open_banks("y", t)
+            multiply(banks, w1q0[t], 0)
+            multiply(banks, w1q1[t], 1)
+            y_rows.append(evacuate(f"y{t}", banks))
+
+        out_view = out.rearrange("(u p) v -> p u v", p=P)
+        v0 = 0
+        for c, n in enumerate(CHUNKS):
+            edge = keep.tile(
+                [P, PACK, n], F32, name=f"edge{c}", tag=("edge0", "best3", "z_bf0")[c], align_bytes=64
+            )
+            centres = cen_t[:, v0 // LIST_ROWS : (v0 + n) // LIST_ROWS]
+            for t in range(PACK):
+                nc.vector.tensor_tensor(
+                    edge[:, t, :], y_rows[t][:].indirect(centres), best[t](v0, v0 + n), ALU.add
+                )
+            z_bf = keep.tile(
+                [P, n * PACK], BF16, name=f"z_bf{c}", tag=("z_bf0", "z_bf1", "z_bf1")[c], align_bytes=64
+            )
+            interleave(
+                c == len(CHUNKS) - 1,
+                z_bf[:].rearrange("p (c i t) -> p c t i", i=4, t=PACK),
+                edge[:].rearrange("p t (c i) -> p c t i", i=4),
+                "relu",
+            )
+            z_code, z_scale = quantize(f"z{c}", z_bf)
+            acc = psum.tile([P, N // P, n], F32, name=f"out_acc{c}", tag=f"bank{c}")
+            for u in range(N // P):
+                cols = slice(u * P, (u + 1) * P)
+                nc.tensor.matmul_mx(
+                    out=acc[:, u, :],
+                    lhsT=w3_code[:, cols].bitcast(FP8X4),
+                    lhsT_scale=w3_scale[:, cols],
+                    rhs=z_code[:].bitcast(FP8X4),
+                    rhs_scale=z_scale[:],
+                    start=True,
+                    stop=True,
+                )
+            result = keep.tile([P, N // P, n], F32, name=f"result{c}")
+            nc.scalar.activation(result[:], acc[:], ACT.Copy)
+            nc.sync.dma_start(out_view[:, :, v0 : v0 + n], result[:])
+            v0 = v0 + n

@@ -73,20 +73,14 @@ def tile_picked_edgecv_relu_p_kernel(
         for t in range(PACK):
             nc.sync.dma_start(w3_raw[:, t, :], w3_rows[t])
 
-        def pick_words(z):
-            picked = keep.tile([P, S], U32, name=f"x_code{z}", align_bytes=64)
+        def pick_words(z, tag):
+            picked = keep.tile([P, S], U32, name=f"x_code{z}", tag=tag, align_bytes=64)
             nc.vector.tensor_copy(picked[:], x_table[z][:].indirect(offs_t[:]))
             return picked
 
-        x_code = [pick_words(0)]
-
-        def pick_scales(h, tag):
-            picked = keep.tile([P, BANK], U8, name=f"x_scale{h}", tag=tag, align_bytes=64)
-            cols = BANK // LIST_ROWS
-            nc.vector.tensor_copy(picked[:], scale_table[:].indirect(offs_t[:, h * cols : (h + 1) * cols]))
-            return picked
-
-        x_scale = [pick_scales(0, "x_scale0")]
+        x_code = [pick_words(0, "x_code0")]
+        x_scale = keep.tile([P, S], U8, name="x_scale", align_bytes=64)
+        nc.vector.tensor_copy(x_scale[:], scale_table[:].indirect(offs_t[:]))
 
         def interleave(on_vector, dst, src, func):
             if on_vector:
@@ -97,16 +91,17 @@ def tile_picked_edgecv_relu_p_kernel(
             else:
                 nc.scalar.activation(dst, src, ACT.Relu if func == "relu" else ACT.Copy)
 
-        def cast_weight(name, raw, t, on_vector, tag=None):
+        def cast_weight(name, raw, tiles, on_vector=False, tag=None):
             grouped = keep.tile(
-                [P, K_PASS], BF16, name=f"{name}_bf{t}", tag=tag or f"{name}_bf{t}", align_bytes=64
+                [P, len(tiles) * K_PASS], BF16, name=f"{name}_bf", tag=tag or f"{name}_bf", align_bytes=64
             )
-            interleave(
-                on_vector,
-                grouped[:].rearrange("p (a i j) -> p a j i", i=4, j=PACK),
-                raw[:].rearrange("p j (a t i) -> p t a j i", t=PACK, i=4)[:, t],
-                "copy",
-            )
+            for s, t in enumerate(tiles):
+                interleave(
+                    on_vector,
+                    grouped[:, s * K_PASS : (s + 1) * K_PASS].rearrange("p (a i j) -> p a j i", i=4, j=PACK),
+                    raw[:].rearrange("p j (a t i) -> p t a j i", t=PACK, i=4)[:, t],
+                    "copy",
+                )
             return grouped
 
         def quantize(name, grouped, tag=None):
@@ -122,16 +117,17 @@ def tile_picked_edgecv_relu_p_kernel(
                 for h in range(HALVES)
             ]
 
-        def multiply(banks, wq, z):
+        def multiply(banks, wq, z, s=0):
             codes, scales = wq
+            stat = slice(s * P, (s + 1) * P)
             for h in range(HALVES):
                 cols = slice(h * BANK, (h + 1) * BANK)
                 nc.tensor.matmul_mx(
                     out=banks[h][:],
-                    lhsT=codes[:].bitcast(FP8X4),
-                    lhsT_scale=scales[:],
+                    lhsT=codes[:, stat].bitcast(FP8X4),
+                    lhsT_scale=scales[:, stat],
                     rhs=x_code[z][:, cols].bitcast(FP8X4),
-                    rhs_scale=x_scale[h][4 * z : P, :],
+                    rhs_scale=x_scale[4 * z : P, cols],
                     start=(z == 0),
                     stop=(z == PASSES - 1),
                 )
@@ -161,43 +157,36 @@ def tile_picked_edgecv_relu_p_kernel(
             return lambda a, b: head[:, a:b] if b <= cut else rest[:, a - cut : b - cut]
 
         e_banks = [open_banks("e", t) for t in range(PACK)]
-        first = [cast_weight("w2p0", w2_raw[0], t, False) for t in range(PACK)]
-        wq = quantize("w2p0t0", first[0])
-        x_scale.append(pick_scales(1, "w2p0_bf0"))
-        multiply(e_banks[0], wq, 0)
-        for t in (1, 2):
+        first = [cast_weight(f"w2p0t{t}", w2_raw[0], (t,)) for t in (0, 1)]
+        late = cast_weight("w2p0t23", w2_raw[0], (2, 3))
+        for t in (0, 1):
             multiply(e_banks[t], quantize(f"w2p0t{t}", first[t]), 0)
-        x_code.append(pick_words(1))
-        g0 = cast_weight("w2p1", w2_raw[1], 0, False)
-        g1 = cast_weight("w2p1", w2_raw[1], 1, False)
+        x_code.append(pick_words(1, "w2p0t1_bf"))
+        g0 = cast_weight("w2p1t0", w2_raw[1], (0,))
+        g1 = cast_weight("w2p1t1", w2_raw[1], (1,))
         multiply(e_banks[0], quantize("w2p1t0", g0), 1)
-        g2 = cast_weight("w2p1", w2_raw[1], 2, True, tag="w2p1_bf0")
-        multiply(e_banks[3], quantize("w2p0t3", first[3], tag="w2p0t2_code"), 0)
+        late_q = quantize("w2p0t23", late, tag="w2p1t0_bf")
         multiply(e_banks[1], quantize("w2p1t1", g1), 1)
-        g3 = cast_weight("w2p1", w2_raw[1], 3, True, tag="w2p1_bf1")
+        multiply(e_banks[2], late_q, 0, 0)
+        multiply(e_banks[3], late_q, 0, 1)
+        g2 = cast_weight("w2p1t2", w2_raw[1], (2,), on_vector=True, tag="w2p0t23_bf")
         multiply(e_banks[2], quantize("w2p1t2", g2), 1)
-        multiply(e_banks[3], quantize("w2p1t3", g3), 1)
 
         best = []
         e0 = evacuate("e0", e_banks[0])
+        g3 = cast_weight("w2p1t3", w2_raw[1], (3,), tag="w2p1t0_scale")
+        multiply(e_banks[3], quantize("w2p1t3", g3), 1)
         best.append(neighbour_max(0, e0))
         e1 = evacuate("e1", e_banks[1])
         best.append(neighbour_max(1, e1))
-        behind = ("w2p1t1_code", "w2p1t2_code", "w2p1t3_code", "w2p1t3_scale")
-        w1q0 = [
-            quantize(f"w1p0t{t}", cast_weight("w1p0", w1_raw[0], t, False, tag=behind[t]))
-            for t in range(PACK)
-        ]
+        w1q0 = quantize("w1p0", cast_weight("w1p0", w1_raw[0], range(PACK), tag="w2p1t2_code"))
         e2 = evacuate("e2", e_banks[2])
         best.append(neighbour_max(2, e2))
-        w1q1 = [
-            quantize(f"w1p1t{t}", cast_weight("w1p1", w1_raw[1], t, False, tag=behind[t]))
-            for t in range(PACK)
-        ]
+        w1q1 = quantize("w1p1", cast_weight("w1p1", w1_raw[1], range(PACK), tag="w2p1t2_code"))
         e3 = evacuate("e3", e_banks[3])
         best.append(neighbour_max(3, e3))
 
-        w3_bf = keep.tile([P, N * PACK], BF16, name="w3_bf", tag=behind[3], align_bytes=64)
+        w3_bf = keep.tile([P, N * PACK], BF16, name="w3_bf", tag="w2p1t2_code", align_bytes=64)
         interleave(
             False,
             w3_bf[:].rearrange("p (c i t) -> p c t i", i=4, t=PACK),
@@ -209,8 +198,8 @@ def tile_picked_edgecv_relu_p_kernel(
         y_rows = []
         for t in range(PACK):
             banks = open_banks("y", t)
-            multiply(banks, w1q0[t], 0)
-            multiply(banks, w1q1[t], 1)
+            multiply(banks, w1q0, 0, t)
+            multiply(banks, w1q1, 1, t)
             y_rows.append(evacuate(f"y{t}", banks))
 
         out_view = out.rearrange("(u p) v -> p u v", p=P)

@@ -46,7 +46,7 @@ def tile_picked_edgecv_relu_p_kernel(
             return table
 
         def load_weight(name, w, z):
-            raw = keep.tile([P, PACK, H], F32, name=f"{name}_raw{z}")
+            raw = keep.tile([P, PACK, H], F32, name=f"{name}_raw{z}", tag=f"{name}_raw{z}", align_bytes=64)
             nc.sync.dma_start(
                 raw[:], w[z * K_PASS : (z + 1) * K_PASS, :].rearrange("(p j) c -> p j c", j=PACK)
             )
@@ -57,7 +57,7 @@ def tile_picked_edgecv_relu_p_kernel(
         offs_t = load_list("offs_t", offs)
         x_table = [load_words(0)]
         for q in range(4):
-            nc.sync.dma_start(
+            nc.gpsimd.dma_start(
                 scale_table[32 * q : 32 * q + 4 * PASSES, :].bitcast(I32),
                 x_scales[:, 4 * q : 4 * q + 4, :].bitcast(I32),
             )
@@ -68,7 +68,7 @@ def tile_picked_edgecv_relu_p_kernel(
         pos2_t = load_list("pos2_t", pos2)
         w1_raw = [load_weight("w1", w1, z) for z in range(PASSES)]
         cen_t = load_list("cen_t", cen)
-        w3_raw = keep.tile([P, PACK, N], F32, name="w3_raw")
+        w3_raw = keep.tile([P, PACK, N], F32, name="w3_raw", tag="w3_raw", align_bytes=64)
         w3_rows = w3.rearrange("(a t i) n -> t a i n", t=PACK, i=4)
         for t in range(PACK):
             nc.sync.dma_start(w3_raw[:, t, :], w3_rows[t])
@@ -142,26 +142,25 @@ def tile_picked_edgecv_relu_p_kernel(
                     nc.scalar.activation(rows[:, cols], banks[h][:], ACT.Copy)
             return rows
 
-        def neighbour_max(t, e_rows):
+        def neighbours(t, e_rows):
             g1 = keep.tile([P, V], F32, name=f"g1_{t}")
             g2 = keep.tile([P, V], F32, name=f"g2_{t}")
             nc.vector.tensor_copy(g1[:], e_rows[:].indirect(pos1_t[:]))
             nc.vector.tensor_copy(g2[:], e_rows[:].indirect(pos2_t[:]))
-            cut = CHUNKS[0] if t == PACK - 1 else V
-            head = keep.tile([P, cut], F32, name=f"best{t}", tag=f"best{t}", align_bytes=64)
-            nc.vector.tensor_tensor(head[:], g1[:, :cut], g2[:, :cut], ALU.max)
-            if cut == V:
-                return lambda a, b: head[:, a:b]
-            rest = keep.tile([P, V - cut], F32, name=f"best{t}_rest")
-            nc.vector.tensor_tensor(rest[:], g1[:, cut:], g2[:, cut:], ALU.max)
-            return lambda a, b: head[:, a:b] if b <= cut else rest[:, a - cut : b - cut]
+            return g1, g2
+
+        def larger(name, pair, a, b, tag):
+            g1, g2 = pair
+            best = keep.tile([P, b - a], F32, name=name, tag=tag, align_bytes=64)
+            nc.vector.tensor_tensor(best[:], g1[:, a:b], g2[:, a:b], ALU.max)
+            return best
 
         e_banks = [open_banks("e", t) for t in range(PACK)]
         first = [cast_weight(f"w2p0t{t}", w2_raw[0], (t,)) for t in (0, 1)]
         late = cast_weight("w2p0t23", w2_raw[0], (2, 3))
         for t in (0, 1):
             multiply(e_banks[t], quantize(f"w2p0t{t}", first[t]), 0)
-        x_code.append(pick_words(1, "w2p0t1_bf"))
+        x_code.append(pick_words(1, "w2_raw0"))
         g0 = cast_weight("w2p1t0", w2_raw[1], (0,))
         g1 = cast_weight("w2p1t1", w2_raw[1], (1,))
         multiply(e_banks[0], quantize("w2p1t0", g0), 1)
@@ -172,28 +171,26 @@ def tile_picked_edgecv_relu_p_kernel(
         g2 = cast_weight("w2p1t2", w2_raw[1], (2,), on_vector=True, tag="w2p0t23_bf")
         multiply(e_banks[2], quantize("w2p1t2", g2), 1)
 
-        best = []
-        e0 = evacuate("e0", e_banks[0])
+        pair = neighbours(0, evacuate("e0", e_banks[0]))
         g3 = cast_weight("w2p1t3", w2_raw[1], (3,), tag="w2p1t0_scale")
         multiply(e_banks[3], quantize("w2p1t3", g3), 1)
-        best.append(neighbour_max(0, e0))
-        e1 = evacuate("e1", e_banks[1])
-        best.append(neighbour_max(1, e1))
+        best = [larger("best0", pair, 0, V, "w2_raw1")]
+        pair = neighbours(1, evacuate("e1", e_banks[1]))
         w1q0 = quantize("w1p0", cast_weight("w1p0", w1_raw[0], range(PACK), tag="w2p1t2_code"))
-        e2 = evacuate("e2", e_banks[2])
-        best.append(neighbour_max(2, e2))
+        best.append(larger("best1", pair, 0, V, "w1_raw0"))
+        pair = neighbours(2, evacuate("e2", e_banks[2]))
         w1q1 = quantize("w1p1", cast_weight("w1p1", w1_raw[1], range(PACK), tag="w2p1t2_code"))
-        e3 = evacuate("e3", e_banks[3])
-        best.append(neighbour_max(3, e3))
+        best.append(larger("best2", pair, 0, V, "w1_raw1"))
+        pair = neighbours(3, evacuate("e3", e_banks[3]))
+        best3_head = larger("best3_head", pair, 0, CHUNKS[0], "best3_head")
+        best3_rest = larger("best3_rest", pair, CHUNKS[0], V, "w1p1_scale")
 
-        w3_bf = keep.tile([P, N * PACK], BF16, name="w3_bf", tag="w2p1t2_code", align_bytes=64)
-        interleave(
-            False,
-            w3_bf[:].rearrange("p (c i t) -> p c t i", i=4, t=PACK),
-            w3_raw[:].rearrange("p t (c i) -> p c t i", i=4),
-            "copy",
-        )
-        w3_code, w3_scale = quantize("w3", w3_bf)
+        def best_cols(t, a, b):
+            if t < PACK - 1:
+                return best[t][:, a:b]
+            if a == 0:
+                return best3_head[:]
+            return best3_rest[:, a - CHUNKS[0] : b - CHUNKS[0]]
 
         y_rows = []
         for t in range(PACK):
@@ -202,19 +199,28 @@ def tile_picked_edgecv_relu_p_kernel(
             multiply(banks, w1q1, 1, t)
             y_rows.append(evacuate(f"y{t}", banks))
 
+        w3_bf = keep.tile([P, N * PACK], BF16, name="w3_bf", tag="w1p1_code", align_bytes=64)
+        interleave(
+            False,
+            w3_bf[:].rearrange("p (c i t) -> p c t i", i=4, t=PACK),
+            w3_raw[:].rearrange("p t (c i) -> p c t i", i=4),
+            "copy",
+        )
+        w3_code, w3_scale = quantize("w3", w3_bf)
+
         out_view = out.rearrange("(u p) v -> p u v", p=P)
         v0 = 0
         for c, n in enumerate(CHUNKS):
             edge = keep.tile(
-                [P, PACK, n], F32, name=f"edge{c}", tag=("edge0", "best3", "z_bf0")[c], align_bytes=64
+                [P, PACK, n], F32, name=f"edge{c}", tag=("edge0", "best3_head", "edge0")[c], align_bytes=64
             )
             centres = cen_t[:, v0 // LIST_ROWS : (v0 + n) // LIST_ROWS]
             for t in range(PACK):
                 nc.vector.tensor_tensor(
-                    edge[:, t, :], y_rows[t][:].indirect(centres), best[t](v0, v0 + n), ALU.add
+                    edge[:, t, :], y_rows[t][:].indirect(centres), best_cols(t, v0, v0 + n), ALU.add
                 )
             z_bf = keep.tile(
-                [P, n * PACK], BF16, name=f"z_bf{c}", tag=("z_bf0", "z_bf1", "z_bf1")[c], align_bytes=64
+                [P, n * PACK], BF16, name=f"z_bf{c}", tag=("z_bf0", "z_bf1", "best3_head")[c], align_bytes=64
             )
             interleave(
                 c == len(CHUNKS) - 1,

@@ -57,7 +57,7 @@ def tile_picked_edgecv_relu_p_kernel(
         offs_t = load_list("offs_t", offs)
         x_table = [load_words(0)]
         for q in range(4):
-            nc.gpsimd.dma_start(
+            nc.sync.dma_start(
                 scale_table[32 * q : 32 * q + 4 * PASSES, :].bitcast(I32),
                 x_scales[:, 4 * q : 4 * q + 4, :].bitcast(I32),
             )
@@ -178,28 +178,21 @@ def tile_picked_edgecv_relu_p_kernel(
         pair = neighbours(1, evacuate("e1", e_banks[1]))
         w1q0 = quantize("w1p0", cast_weight("w1p0", w1_raw[0], range(PACK), tag="w2p1t2_code"))
         best.append(larger("best1", pair, 0, V, "w1_raw0"))
+        w1q1 = [quantize("w1p1a", cast_weight("w1p1a", w1_raw[1], (0, 1), tag="w2p1t3_code"))]
         pair = neighbours(2, evacuate("e2", e_banks[2]))
-        w1q1 = quantize("w1p1", cast_weight("w1p1", w1_raw[1], range(PACK), tag="w2p1t2_code"))
+        w1q1.append(quantize("w1p1b", cast_weight("w1p1b", w1_raw[1], (2, 3), tag="w2p1t3_scale")))
         best.append(larger("best2", pair, 0, V, "w1_raw1"))
         pair = neighbours(3, evacuate("e3", e_banks[3]))
-        best3_head = larger("best3_head", pair, 0, CHUNKS[0], "best3_head")
-        best3_rest = larger("best3_rest", pair, CHUNKS[0], V, "w1p1_scale")
-
-        def best_cols(t, a, b):
-            if t < PACK - 1:
-                return best[t][:, a:b]
-            if a == 0:
-                return best3_head[:]
-            return best3_rest[:, a - CHUNKS[0] : b - CHUNKS[0]]
+        best.append(larger("best3", pair, 0, V, "best3"))
 
         y_rows = []
         for t in range(PACK):
             banks = open_banks("y", t)
             multiply(banks, w1q0, 0, t)
-            multiply(banks, w1q1, 1, t)
+            multiply(banks, w1q1[t // 2], 1, t % 2)
             y_rows.append(evacuate(f"y{t}", banks))
 
-        w3_bf = keep.tile([P, N * PACK], BF16, name="w3_bf", tag="w1p1_code", align_bytes=64)
+        w3_bf = keep.tile([P, N * PACK], BF16, name="w3_bf", tag="w1p1b_code", align_bytes=64)
         interleave(
             False,
             w3_bf[:].rearrange("p (c i t) -> p c t i", i=4, t=PACK),
@@ -212,15 +205,15 @@ def tile_picked_edgecv_relu_p_kernel(
         v0 = 0
         for c, n in enumerate(CHUNKS):
             edge = keep.tile(
-                [P, PACK, n], F32, name=f"edge{c}", tag=("edge0", "best3_head", "edge0")[c], align_bytes=64
+                [P, PACK, n], F32, name=f"edge{c}", tag=("edge0", "w3_raw", "edge0")[c], align_bytes=64
             )
             centres = cen_t[:, v0 // LIST_ROWS : (v0 + n) // LIST_ROWS]
             for t in range(PACK):
                 nc.vector.tensor_tensor(
-                    edge[:, t, :], y_rows[t][:].indirect(centres), best_cols(t, v0, v0 + n), ALU.add
+                    edge[:, t, :], y_rows[t][:].indirect(centres), best[t][:, v0 : v0 + n], ALU.add
                 )
             z_bf = keep.tile(
-                [P, n * PACK], BF16, name=f"z_bf{c}", tag=("z_bf0", "z_bf1", "best3_head")[c], align_bytes=64
+                [P, n * PACK], BF16, name=f"z_bf{c}", tag=("z_bf0", "z_bf1", "w3_raw")[c], align_bytes=64
             )
             interleave(
                 c == len(CHUNKS) - 1,

@@ -104,6 +104,19 @@ def tile_picked_edgecv_relu_p_kernel(
                 )
             return grouped
 
+        def cast_weight_gpsimd(name, raw):
+            grouped = keep.tile([P, PACK * K_PASS], BF16, name=f"{name}_bf", tag=f"{name}_bf", align_bytes=64)
+            for t in range(PACK):
+                nc.gpsimd.tensor_scalar(
+                    grouped[:, t * K_PASS : (t + 1) * K_PASS].rearrange("p (a i j) -> p a j i", i=4, j=PACK),
+                    raw[:].rearrange("p j (a t i) -> p t a j i", t=PACK, i=4)[:, t],
+                    1.0,
+                    0.0,
+                    ALU.mult,
+                    ALU.add,
+                )
+            return grouped
+
         def quantize(name, grouped, tag=None):
             width = grouped.shape[1] // PACK
             codes = keep.tile([P, width], U32, name=f"{name}_code", tag=tag or f"{name}_code", align_bytes=64)
@@ -133,7 +146,7 @@ def tile_picked_edgecv_relu_p_kernel(
                 )
 
         def evacuate(name, banks, last_on_vector=False):
-            rows = keep.tile([P, S], F32, name=name)
+            rows = keep.tile([P, S], F32, name=name, tag=name, align_bytes=64)
             for h in range(HALVES):
                 cols = slice(h * BANK, (h + 1) * BANK)
                 if last_on_vector and h == HALVES - 1:
@@ -148,12 +161,6 @@ def tile_picked_edgecv_relu_p_kernel(
             nc.vector.tensor_copy(g1[:], e_rows[:].indirect(pos1_t[:]))
             nc.vector.tensor_copy(g2[:], e_rows[:].indirect(pos2_t[:]))
             return g1, g2
-
-        def larger(name, pair, a, b, tag):
-            g1, g2 = pair
-            best = keep.tile([P, b - a], F32, name=name, tag=tag, align_bytes=64)
-            nc.vector.tensor_tensor(best[:], g1[:, a:b], g2[:, a:b], ALU.max)
-            return best
 
         e_banks = [open_banks("e", t) for t in range(PACK)]
         first = [cast_weight(f"w2p0t{t}", w2_raw[0], (t,)) for t in (0, 1)]
@@ -174,25 +181,32 @@ def tile_picked_edgecv_relu_p_kernel(
         pair = neighbours(0, evacuate("e0", e_banks[0]))
         g3 = cast_weight("w2p1t3", w2_raw[1], (3,), tag="w2p1t0_scale")
         multiply(e_banks[3], quantize("w2p1t3", g3), 1)
-        best = [larger("best0", pair, 0, V, "w2_raw1")]
-        pair = neighbours(1, evacuate("e1", e_banks[1]))
-        w1q0 = quantize("w1p0", cast_weight("w1p0", w1_raw[0], range(PACK), tag="w2p1t2_code"))
-        best.append(larger("best1", pair, 0, V, "w1_raw0"))
-        w1q1 = [quantize("w1p1a", cast_weight("w1p1a", w1_raw[1], (0, 1), tag="w2p1t3_code"))]
-        pair = neighbours(2, evacuate("e2", e_banks[2]))
-        w1q1.append(quantize("w1p1b", cast_weight("w1p1b", w1_raw[1], (2, 3), tag="w2p1t3_scale")))
-        best.append(larger("best2", pair, 0, V, "w1_raw1"))
-        pair = neighbours(3, evacuate("e3", e_banks[3]))
-        best.append(larger("best3", pair, 0, V, "best3"))
+        pairs = [pair]
+        w1_bf = [cast_weight_gpsimd(f"w1p{z}", w1_raw[z]) for z in range(PASSES)]
+        pairs.append(neighbours(1, evacuate("e1", e_banks[1])))
+        pairs.append(neighbours(2, evacuate("e2", e_banks[2])))
+        e3 = evacuate("e3", e_banks[3])
+        g1 = keep.tile([P, V], F32, name="g1_3")
+        g2 = keep.tile([P, V], F32, name="g2_3")
+        nc.vector.tensor_copy(g1[:], e3[:].indirect(pos1_t[:]))
+        w1q0 = quantize("w1p0", w1_bf[0], tag="e2")
+        w1q1 = quantize("w1p1", w1_bf[1], tag="e1")
+        nc.vector.tensor_copy(g2[:], e3[:].indirect(pos2_t[:]))
+        pairs.append((g1, g2))
+        best_all = keep.tile([P, PACK, V], F32, name="best_all", tag="w1p1_bf", align_bytes=64)
+        best = []
+        for t in range(PACK):
+            nc.vector.tensor_tensor(best_all[:, t, :], pairs[t][0][:], pairs[t][1][:], ALU.max)
+            best.append(best_all[:, t, :])
 
         y_rows = []
         for t in range(PACK):
             banks = open_banks("y", t)
             multiply(banks, w1q0, 0, t)
-            multiply(banks, w1q1[t // 2], 1, t % 2)
+            multiply(banks, w1q1, 1, t)
             y_rows.append(evacuate(f"y{t}", banks))
 
-        w3_bf = keep.tile([P, N * PACK], BF16, name="w3_bf", tag="w1p1b_code", align_bytes=64)
+        w3_bf = keep.tile([P, N * PACK], BF16, name="w3_bf", tag="w1p1_scale", align_bytes=64)
         interleave(
             False,
             w3_bf[:].rearrange("p (c i t) -> p c t i", i=4, t=PACK),

@@ -1,6 +1,7 @@
 from contextlib import ExitStack
 
 import concourse.mybir as mybir
+from concourse.masks import make_identity
 
 K, T, S, V, H, N = 1024, 2048, 1024, 512, 512, 256
 FLOPS = 2 * (2 * K * H * S + H * N * V)
@@ -22,7 +23,8 @@ PASSES = K // K_PASS
 BANK = 512
 HALVES = S // BANK
 LIST_ROWS = 16
-CHUNKS = (256, 128, 128)
+TILES = H // P
+BLOCKS = V // P
 
 
 def tile_picked_edgecv_relu_p_kernel(
@@ -45,15 +47,20 @@ def tile_picked_edgecv_relu_p_kernel(
             )
             return table
 
-        def load_weight(name, w, z):
-            raw = keep.tile([P, PACK, H], F32, name=f"{name}_raw{z}", tag=f"{name}_raw{z}", align_bytes=64)
-            nc.sync.dma_start(
-                raw[:], w[z * K_PASS : (z + 1) * K_PASS, :].rearrange("(p j) c -> p j c", j=PACK)
-            )
-            return raw
+        raw = {}
+
+        def load_weight(name, w, z, first, count):
+            tag = f"{name}_raw{z}{first}"
+            tile = keep.tile([P, PACK, count * P], F32, name=tag, tag=tag, align_bytes=64)
+            rows = w[z * K_PASS : (z + 1) * K_PASS, first * P : (first + count) * P]
+            nc.sync.dma_start(tile[:], rows.rearrange("(p j) c -> p j c", j=PACK))
+            raw[name, first, z] = tile
 
         scale_table = keep.tile([P, T], U8, name="scale_table")
         nc.vector.memset(scale_table[:].bitcast(I32), 0)
+        identity = keep.tile([P, P], F32, name="identity")
+        make_identity(nc, identity[:])
+
         offs_t = load_list("offs_t", offs)
         x_table = [load_words(0)]
         for q in range(4):
@@ -61,182 +68,228 @@ def tile_picked_edgecv_relu_p_kernel(
                 scale_table[32 * q : 32 * q + 4 * PASSES, :].bitcast(I32),
                 x_scales[:, 4 * q : 4 * q + 4, :].bitcast(I32),
             )
-        w2_raw = [load_weight("w2", w2, 0)]
+        load_weight("w2", w2, 0, 0, 1)
         x_table.append(load_words(1))
-        w2_raw.append(load_weight("w2", w2, 1))
+        load_weight("w2", w2, 1, 0, 1)
         pos1_t = load_list("pos1_t", pos1)
         pos2_t = load_list("pos2_t", pos2)
-        w1_raw = [load_weight("w1", w1, z) for z in range(PASSES)]
+        for z in range(PASSES):
+            load_weight("w2", w2, z, 1, 1)
+        for z in range(PASSES):
+            load_weight("w2", w2, z, 2, 2)
+        for first in (0, 2):
+            for z in range(PASSES):
+                load_weight("w1", w1, z, first, 2)
         cen_t = load_list("cen_t", cen)
         w3_raw = keep.tile([P, PACK, N], F32, name="w3_raw", tag="w3_raw", align_bytes=64)
-        w3_rows = w3.rearrange("(a t i) n -> t a i n", t=PACK, i=4)
-        for t in range(PACK):
-            nc.sync.dma_start(w3_raw[:, t, :], w3_rows[t])
+        nc.sync.dma_start(w3_raw[:], w3.rearrange("(p j) n -> p j n", j=PACK))
 
-        def pick_words(z, tag):
-            picked = keep.tile([P, S], U32, name=f"x_code{z}", tag=tag, align_bytes=64)
-            nc.vector.tensor_copy(picked[:], x_table[z][:].indirect(offs_t[:]))
-            return picked
+        def stage(name, width, tag=None):
+            return keep.tile([P, width], BF16, name=f"{name}_bf", tag=tag or f"{name}_bf", align_bytes=64)
 
-        x_code = [pick_words(0, "x_code0")]
-        x_scale = keep.tile([P, S], U8, name="x_scale", align_bytes=64)
-        nc.vector.tensor_copy(x_scale[:], scale_table[:].indirect(offs_t[:]))
-
-        def interleave(on_vector, dst, src, func):
-            if on_vector:
-                if func == "relu":
-                    nc.vector.tensor_scalar_max(dst, src, 0.0)
-                else:
-                    nc.vector.tensor_copy(dst, src)
-            else:
-                nc.scalar.activation(dst, src, ACT.Relu if func == "relu" else ACT.Copy)
-
-        def cast_weight(name, raw, tiles, on_vector=False, tag=None):
-            grouped = keep.tile(
-                [P, len(tiles) * K_PASS], BF16, name=f"{name}_bf", tag=tag or f"{name}_bf", align_bytes=64
-            )
-            for s, t in enumerate(tiles):
-                interleave(
-                    on_vector,
-                    grouped[:, s * K_PASS : (s + 1) * K_PASS].rearrange("p (a i j) -> p a j i", i=4, j=PACK),
-                    raw[:].rearrange("p j (a t i) -> p t a j i", t=PACK, i=4)[:, t],
-                    "copy",
-                )
-            return grouped
-
-        def cast_weight_gpsimd(name, raw):
-            grouped = keep.tile([P, PACK * K_PASS], BF16, name=f"{name}_bf", tag=f"{name}_bf", align_bytes=64)
-            for t in range(PACK):
+        def cast(engine, grouped, src):
+            if engine == "gpsimd":
                 nc.gpsimd.tensor_scalar(
-                    grouped[:, t * K_PASS : (t + 1) * K_PASS].rearrange("p (a i j) -> p a j i", i=4, j=PACK),
-                    raw[:].rearrange("p j (a t i) -> p t a j i", t=PACK, i=4)[:, t],
+                    grouped.rearrange("p (c j) -> p c j", j=PACK),
+                    src.rearrange("p j c -> p c j"),
                     1.0,
                     0.0,
                     ALU.mult,
                     ALU.add,
                 )
-            return grouped
+            else:
+                dst = grouped.rearrange("p (a i j) -> p a j i", i=4, j=PACK)
+                view = src.rearrange("p j (a i) -> p a j i", i=4)
+                if engine == "vector":
+                    nc.vector.tensor_copy(dst, view)
+                else:
+                    nc.scalar.activation(dst, view, ACT.Copy)
 
         def quantize(name, grouped, tag=None):
             width = grouped.shape[1] // PACK
             codes = keep.tile([P, width], U32, name=f"{name}_code", tag=tag or f"{name}_code", align_bytes=64)
-            scales = keep.tile([P, width], U8, name=f"{name}_scale", tag=f"{name}_scale", align_bytes=64)
+            scales = keep.tile([P, width], U8, name=f"{name}_scale", align_bytes=64)
             nc.vector.quantize_mx(out=codes[:].bitcast(FP8X4), scales=scales[:], in_=grouped[:])
             return codes, scales
 
-        def open_banks(name, t):
+        def open_banks(k):
             return [
-                psum.tile([P, BANK], F32, name=f"{name}_acc{t}{h}", tag=f"bank{HALVES * t + h}")
+                psum.tile([P, BANK], F32, name=f"acc{k}{h}", tag=f"bank{HALVES * (k % 2) + h}")
                 for h in range(HALVES)
             ]
 
-        def multiply(banks, wq, z, s=0):
+        x_code = {}
+
+        def pick_words(z, h, tag=None):
+            picked = keep.tile([P, BANK], U32, name=f"x_code{z}{h}", tag=tag or f"x_code{z}{h}", align_bytes=64)
+            cols = slice(h * BANK // LIST_ROWS, (h + 1) * BANK // LIST_ROWS)
+            nc.vector.tensor_copy(picked[:], x_table[z][:].indirect(offs_t[:, cols]))
+            x_code[z, h] = picked
+
+        def multiply(banks, wq, z, halves=range(HALVES), s=0):
             codes, scales = wq
             stat = slice(s * P, (s + 1) * P)
-            for h in range(HALVES):
-                cols = slice(h * BANK, (h + 1) * BANK)
+            for h in halves:
                 nc.tensor.matmul_mx(
                     out=banks[h][:],
                     lhsT=codes[:, stat].bitcast(FP8X4),
                     lhsT_scale=scales[:, stat],
-                    rhs=x_code[z][:, cols].bitcast(FP8X4),
-                    rhs_scale=x_scale[4 * z : P, cols],
+                    rhs=x_code[z, h][:].bitcast(FP8X4),
+                    rhs_scale=x_scale[4 * z : P, h * BANK : (h + 1) * BANK],
                     start=(z == 0),
                     stop=(z == PASSES - 1),
                 )
 
-        def evacuate(name, banks, last_on_vector=False):
-            rows = keep.tile([P, S], F32, name=name, tag=name, align_bytes=64)
+        def evacuate(name, banks, tag):
+            rows = keep.tile([P, S], F32, name=name, tag=tag or name, align_bytes=64)
             for h in range(HALVES):
-                cols = slice(h * BANK, (h + 1) * BANK)
-                if last_on_vector and h == HALVES - 1:
-                    nc.vector.tensor_copy(rows[:, cols], banks[h][:])
-                else:
-                    nc.scalar.activation(rows[:, cols], banks[h][:], ACT.Copy)
+                nc.scalar.activation(rows[:, h * BANK : (h + 1) * BANK], banks[h][:], ACT.Copy)
             return rows
 
-        def neighbours(t, e_rows):
-            g1 = keep.tile([P, V], F32, name=f"g1_{t}")
-            g2 = keep.tile([P, V], F32, name=f"g2_{t}")
-            nc.vector.tensor_copy(g1[:], e_rows[:].indirect(pos1_t[:]))
-            nc.vector.tensor_copy(g2[:], e_rows[:].indirect(pos2_t[:]))
-            return g1, g2
+        def fetch(name, rows, lst, tag=None):
+            got = keep.tile([P, lst.shape[1] * LIST_ROWS], F32, name=name, tag=tag or name, align_bytes=64)
+            nc.vector.tensor_copy(got[:], rows[:].indirect(lst))
+            return got
 
-        e_banks = [open_banks("e", t) for t in range(PACK)]
-        first = [cast_weight(f"w2p0t{t}", w2_raw[0], (t,)) for t in (0, 1)]
-        late = cast_weight("w2p0t23", w2_raw[0], (2, 3))
-        for t in (0, 1):
-            multiply(e_banks[t], quantize(f"w2p0t{t}", first[t]), 0)
-        x_code.append(pick_words(1, "w2_raw0"))
-        g0 = cast_weight("w2p1t0", w2_raw[1], (0,))
-        g1 = cast_weight("w2p1t1", w2_raw[1], (1,))
-        multiply(e_banks[0], quantize("w2p1t0", g0), 1)
-        late_q = quantize("w2p0t23", late, tag="w2p1t0_bf")
-        multiply(e_banks[1], quantize("w2p1t1", g1), 1)
-        multiply(e_banks[2], late_q, 0, 0)
-        multiply(e_banks[3], late_q, 0, 1)
-        g2 = cast_weight("w2p1t2", w2_raw[1], (2,), on_vector=True, tag="w2p0t23_bf")
-        multiply(e_banks[2], quantize("w2p1t2", g2), 1)
+        edge = [psum.tile([P, H], F32, name=f"edge{b}", tag=f"bank{4 + b}") for b in range(BLOCKS)]
 
-        pair = neighbours(0, evacuate("e0", e_banks[0]))
-        g3 = cast_weight("w2p1t3", w2_raw[1], (3,), tag="w2p1t0_scale")
-        multiply(e_banks[3], quantize("w2p1t3", g3), 1)
-        pairs = [pair]
-        w1_bf = [cast_weight_gpsimd(f"w1p{z}", w1_raw[z]) for z in range(PASSES)]
-        pairs.append(neighbours(1, evacuate("e1", e_banks[1])))
-        pairs.append(neighbours(2, evacuate("e2", e_banks[2])))
-        e3 = evacuate("e3", e_banks[3])
-        g1 = keep.tile([P, V], F32, name="g1_3")
-        g2 = keep.tile([P, V], F32, name="g2_3")
-        nc.vector.tensor_copy(g1[:], e3[:].indirect(pos1_t[:]))
-        w1q0 = quantize("w1p0", w1_bf[0], tag="e2")
-        w1q1 = quantize("w1p1", w1_bf[1], tag="e1")
-        nc.vector.tensor_copy(g2[:], e3[:].indirect(pos2_t[:]))
-        pairs.append((g1, g2))
-        best_all = keep.tile([P, PACK, V], F32, name="best_all", tag="w1p1_bf", align_bytes=64)
-        best = []
-        for t in range(PACK):
-            nc.vector.tensor_tensor(best_all[:, t, :], pairs[t][0][:], pairs[t][1][:], ALU.max)
-            best.append(best_all[:, t, :])
+        def add_turned(values, u, b, start=False, stop=False):
+            nc.tensor.matmul(
+                edge[b][:, u * P : (u + 1) * P],
+                lhsT=values,
+                rhs=identity[:],
+                start=start,
+                stop=stop,
+                is_transpose=True,
+            )
 
-        y_rows = []
-        for t in range(PACK):
-            banks = open_banks("y", t)
-            multiply(banks, w1q0, 0, t)
-            multiply(banks, w1q1, 1, t)
-            y_rows.append(evacuate(f"y{t}", banks))
+        def add_turned_all(values, u, start=False):
+            for b in range(BLOCKS):
+                add_turned(values[:, b * P : (b + 1) * P], u, b, start=start)
 
-        w3_bf = keep.tile([P, N * PACK], BF16, name="w3_bf", tag="w1p1_scale", align_bytes=64)
-        interleave(
-            False,
-            w3_bf[:].rearrange("p (c i t) -> p c t i", i=4, t=PACK),
-            w3_raw[:].rearrange("p t (c i) -> p c t i", i=4),
-            "copy",
-        )
+        first, second, gap, rows, banks = {}, {}, {}, {}, {}
+
+        def cast_group(name, start, engines, tag=None):
+            width = raw[name, start, 0].shape[2] * PACK
+            grouped = stage(f"{name}_{start}", PASSES * width, tag)
+            for z in range(PASSES):
+                cast(engines[z], grouped[:, z * width : (z + 1) * width], raw[name, start, z][:])
+            return grouped
+
+        def products(k, grouped):
+            wq = quantize(f"k{k}", grouped)
+            count = grouped.shape[1] // (PASSES * K_PASS)
+            for u in range(count):
+                banks[k + u] = open_banks(k + u)
+                for h in range(HALVES):
+                    for z in range(PASSES):
+                        multiply(banks[k + u], wq, z, (h,), s=z * count + u)
+
+        def empty(k, tag=None):
+            rows[k] = evacuate(f"rows{k}", banks[k], tag)
+
+        def fetch_second(u, tag=None):
+            second[u] = fetch(f"second{u}", rows[u], pos2_t[:], tag)
+            add_turned_all(second[u], u, start=(u == 0))
+
+        def add_lift(u, tag):
+            lift = keep.tile([P, V], F32, name=f"lift{u}", tag=tag, align_bytes=64)
+            nc.scalar.activation(lift[:], gap[u][:], ACT.Relu)
+            add_turned_all(lift, u)
+
+        def fetch_centre(u, tag):
+            add_turned_all(fetch(f"centre{u}", rows[TILES + u], cen_t[:], tag), u)
+
+        def head_pass(z):
+            grouped = stage(f"k0p{z}", K_PASS)
+            cast("scalar", grouped[:], raw["w2", 0, z][:])
+            return quantize(f"k0p{z}", grouped)
+
+        for h in range(HALVES):
+            pick_words(0, h)
+        x_scale = keep.tile([P, S], U8, name="x_scale", align_bytes=64)
+        nc.vector.tensor_copy(x_scale[:], scale_table[:].indirect(offs_t[:]))
+        banks[0] = open_banks(0)
+        multiply(banks[0], head_pass(0), 0)
+        pick_words(1, 0)
+        wq = head_pass(1)
+        multiply(banks[0], wq, 1, (0,))
+        pick_words(1, 1, tag="w2_raw10")
+        multiply(banks[0], wq, 1, (1,))
+        empty(0)
+        products(1, cast_group("w2", 1, ("vector", "vector")))
+
+        def gather_first(u):
+            first[u] = fetch(f"first{u}", rows[u], pos1_t[:])
+
+        def subtract(u, tag):
+            gap[u] = keep.tile([P, V], F32, name=f"gap{u}", tag=tag, align_bytes=64)
+            nc.gpsimd.tensor_tensor(gap[u][:], first[u][:], second[u][:], ALU.subtract)
+
+        grouped = cast_group("w2", 2, ("gpsimd", "scalar"), "stage")
+        fetch_second(0, tag="w2_1_bf")
+        gather_first(0)
+        empty(1, "w2_raw12")
+        products(2, grouped)
+        subtract(0, "stage")
+        grouped = cast_group("w1", 0, ("gpsimd", "scalar"), "first0")
+        fetch_second(1, tag="w2_raw02")
+        gather_first(1)
+        empty(2, "w1_raw10")
+        products(4, grouped)
+        subtract(1, "first0")
+        grouped = cast_group("w1", 2, ("gpsimd", "scalar"), "first1")
+        empty(3, "w1_raw12")
+        fetch_second(2, tag="w1_raw00")
+        gather_first(2)
+        empty(4)
+        empty(5)
+        products(6, grouped)
+        subtract(2, "first1")
+        w3_bf = stage("w3", N * PACK, "first2")
+        cast("gpsimd", w3_bf[:], w3_raw[:])
+        fetch_second(3, tag="w1_raw02")
+        gather_first(3)
         w3_code, w3_scale = quantize("w3", w3_bf)
+        subtract(3, "gap3")
+        empty(6)
+        empty(7)
+        add_lift(0, "k2_code")
+        add_lift(1, "k4_code")
+        fetch_centre(0, "w3_raw")
+        add_lift(2, "k6_code")
+        fetch_centre(1, "w1_raw12")
+        add_lift(3, "lift3")
 
         out_view = out.rearrange("(u p) v -> p u v", p=P)
-        v0 = 0
-        for c, n in enumerate(CHUNKS):
-            edge = keep.tile(
-                [P, PACK, n], F32, name=f"edge{c}", tag=("edge0", "w3_raw", "edge0")[c], align_bytes=64
+        z_bf = {}
+
+        def gather_block(b):
+            centres = cen_t[:, b * P // LIST_ROWS : (b + 1) * P // LIST_ROWS]
+            for u in (2, 3):
+                got = fetch(f"centre{u}{b}", rows[TILES + u], centres, tag=f"piece{(2 * b + u) % 3}")
+                add_turned(got[:], u, b, stop=(u == 3))
+
+        def turn_back(b):
+            z_rows = keep.tile([P, H], BF16, name=f"z_rows{b}")
+            nc.scalar.activation(
+                z_rows[:].rearrange("v (g p e) -> v g p e", g=2, e=2),
+                edge[b][:].rearrange("v (p g e) -> v g p e", g=2, e=2),
+                ACT.Relu,
             )
-            centres = cen_t[:, v0 // LIST_ROWS : (v0 + n) // LIST_ROWS]
-            for t in range(PACK):
-                nc.vector.tensor_tensor(
-                    edge[:, t, :], y_rows[t][:].indirect(centres), best[t][:, v0 : v0 + n], ALU.add
-                )
-            z_bf = keep.tile(
-                [P, n * PACK], BF16, name=f"z_bf{c}", tag=("z_bf0", "z_bf1", "w3_raw")[c], align_bytes=64
+            words = z_rows[:].bitcast(F32)
+            turned = psum.tile([P, 2, P], F32, name=f"turned{b}", tag=f"bank{b % 2}")
+            for g in range(2):
+                nc.tensor.transpose(turned[:, g, :], words[:, g * P : (g + 1) * P], identity[:])
+            z_bf[b] = keep.tile([P, P * PACK], BF16, name=f"z_bf{b}", align_bytes=64)
+            nc.vector.tensor_copy(
+                z_bf[b][:].bitcast(F32).rearrange("p (v g) -> p v g", g=2),
+                turned[:].rearrange("p g v -> p v g"),
             )
-            interleave(
-                c == len(CHUNKS) - 1,
-                z_bf[:].rearrange("p (c i t) -> p c t i", i=4, t=PACK),
-                edge[:].rearrange("p t (c i) -> p c t i", i=4),
-                "relu",
-            )
-            z_code, z_scale = quantize(f"z{c}", z_bf)
-            acc = psum.tile([P, N // P, n], F32, name=f"out_acc{c}", tag=f"bank{c}")
+
+        def project(b):
+            z_code, z_scale = quantize(f"z{b}", z_bf[b])
+            acc = psum.tile([P, N // P, P], F32, name=f"out_acc{b}", tag=f"bank{2 + b % 2}")
             for u in range(N // P):
                 cols = slice(u * P, (u + 1) * P)
                 nc.tensor.matmul_mx(
@@ -248,7 +301,14 @@ def tile_picked_edgecv_relu_p_kernel(
                     start=True,
                     stop=True,
                 )
-            result = keep.tile([P, N // P, n], F32, name=f"result{c}")
+            result = keep.tile([P, N // P, P], F32, name=f"result{b}")
             nc.scalar.activation(result[:], acc[:], ACT.Copy)
-            nc.sync.dma_start(out_view[:, :, v0 : v0 + n], result[:])
-            v0 = v0 + n
+            nc.sync.dma_start(out_view[:, :, b * P : (b + 1) * P], result[:])
+
+        for b in range(BLOCKS + 2):
+            if b < BLOCKS:
+                gather_block(b)
+            if 0 < b <= BLOCKS:
+                turn_back(b - 1)
+            if b > 1:
+                project(b - 2)

@@ -25,6 +25,7 @@ HALVES = S // BANK
 LIST_ROWS = 16
 TILES = H // P
 BLOCKS = V // P
+GROUPS = ((0, 2), (2, 1), (3, 1))
 
 
 def tile_picked_edgecv_relu_p_kernel(
@@ -108,7 +109,7 @@ def tile_picked_edgecv_relu_p_kernel(
         def quantize(name, grouped, tag=None):
             width = grouped.shape[1] // PACK
             codes = keep.tile([P, width], U32, name=f"{name}_code", tag=tag or f"{name}_code", align_bytes=64)
-            scales = keep.tile([P, width], U8, name=f"{name}_scale", align_bytes=64)
+            scales = keep.tile([P, width], U8, name=f"{name}_scale", tag=f"{name}_scale", align_bytes=64)
             nc.vector.quantize_mx(out=codes[:].bitcast(FP8X4), scales=scales[:], in_=grouped[:])
             return codes, scales
 
@@ -153,9 +154,18 @@ def tile_picked_edgecv_relu_p_kernel(
 
         edge = [psum.tile([P, H], F32, name=f"edge{b}", tag=f"bank{4 + b}") for b in range(BLOCKS)]
 
+        last = {}
+
         def add_turned(values, u, b, start=False, stop=False):
+            if (u, b) == (TILES - 1, BLOCKS - 1):
+                start = not last
+                if start:
+                    last["edge"] = psum.tile([P, P], F32, name="edge_last", tag="bank1")
+                dst = last["edge"][:]
+            else:
+                dst = edge[b][:, u * P : (u + 1) * P]
             nc.tensor.matmul(
-                edge[b][:, u * P : (u + 1) * P],
+                dst,
                 lhsT=values,
                 rhs=identity[:],
                 start=start,
@@ -169,21 +179,21 @@ def tile_picked_edgecv_relu_p_kernel(
 
         first, second, gap, rows, banks = {}, {}, {}, {}, {}
 
-        def cast_group(name, start, engines, tag=None):
-            width = raw[name, start, 0].shape[2] * PACK
-            grouped = stage(f"{name}_{start}", PASSES * width, tag)
-            for z in range(PASSES):
-                cast(engines[z], grouped[:, z * width : (z + 1) * width], raw[name, start, z][:])
+        def cast_group(name, start, engines, tags):
+            grouped = []
+            for z, engine in enumerate(engines):
+                src = raw[name, start, z]
+                grouped.append(stage(f"{name}_{start}{z}", src.shape[2] * PACK, tags[z]))
+                cast(engine, grouped[z][:], src[:])
             return grouped
 
-        def products(k, grouped):
-            wq = quantize(f"k{k}", grouped)
-            count = grouped.shape[1] // (PASSES * K_PASS)
-            for u in range(count):
+        def products(k, grouped, tag=None):
+            wq = [quantize(f"k{k}p0", grouped[0], tag), quantize(f"k{k}p1", grouped[1])]
+            for u in range(2):
                 banks[k + u] = open_banks(k + u)
                 for h in range(HALVES):
                     for z in range(PASSES):
-                        multiply(banks[k + u], wq, z, (h,), s=z * count + u)
+                        multiply(banks[k + u], wq[z], z, (h,), s=u)
 
         def empty(k, tag=None):
             rows[k] = evacuate(f"rows{k}", banks[k], tag)
@@ -194,102 +204,108 @@ def tile_picked_edgecv_relu_p_kernel(
 
         def add_lift(u, tag):
             lift = keep.tile([P, V], F32, name=f"lift{u}", tag=tag, align_bytes=64)
-            nc.scalar.activation(lift[:], gap[u][:], ACT.Relu)
+            for a, b, part in gap[u]:
+                nc.scalar.activation(lift[:, a:b], part[:], ACT.Relu)
             add_turned_all(lift, u)
 
-        def fetch_centre(u, tag):
-            add_turned_all(fetch(f"centre{u}", rows[TILES + u], cen_t[:], tag), u)
-
-        def head_pass(z):
-            grouped = stage(f"k0p{z}", K_PASS)
-            cast("scalar", grouped[:], raw["w2", 0, z][:])
-            return quantize(f"k0p{z}", grouped)
+        def head_cast(k, z):
+            grouped = stage(f"k{k}p{z}", K_PASS)
+            cast("scalar", grouped[:], raw["w2", k, z][:])
+            return grouped
 
         for h in range(HALVES):
             pick_words(0, h)
         x_scale = keep.tile([P, S], U8, name="x_scale", align_bytes=64)
         nc.vector.tensor_copy(x_scale[:], scale_table[:].indirect(offs_t[:]))
-        banks[0] = open_banks(0)
-        multiply(banks[0], head_pass(0), 0)
+        banks[0], banks[1] = open_banks(0), open_banks(1)
+        multiply(banks[0], quantize("k0p0", head_cast(0, 0)), 0)
         pick_words(1, 0)
-        wq = head_pass(1)
+        wq = quantize("k0p1", head_cast(0, 1))
         multiply(banks[0], wq, 1, (0,))
-        pick_words(1, 1, tag="w2_raw10")
+        multiply(banks[1], quantize("k1p0", head_cast(1, 0)), 0)
+        pick_words(1, 1, tag="w2_raw01")
         multiply(banks[0], wq, 1, (1,))
-        empty(0)
-        products(1, cast_group("w2", 1, ("vector", "vector")))
+        wq = quantize("k1p1", head_cast(1, 1))
+        empty(0, "w2_raw11")
+        multiply(banks[1], wq, 1)
 
-        def gather_first(u):
-            first[u] = fetch(f"first{u}", rows[u], pos1_t[:])
+        def gather_first(u, tag=None):
+            first[u] = fetch(f"first{u}", rows[u], pos1_t[:], tag)
 
-        def subtract(u, tag):
-            gap[u] = keep.tile([P, V], F32, name=f"gap{u}", tag=tag, align_bytes=64)
-            nc.gpsimd.tensor_tensor(gap[u][:], first[u][:], second[u][:], ALU.subtract)
+        def subtract(u, tag, a=0, b=V):
+            part = keep.tile([P, b - a], F32, name=f"gap{u}{a}", tag=tag, align_bytes=64)
+            nc.gpsimd.tensor_tensor(part[:], first[u][:, a:b], second[u][:, a:b], ALU.subtract)
+            gap.setdefault(u, []).append((a, b, part))
 
-        grouped = cast_group("w2", 2, ("gpsimd", "scalar"), "stage")
-        fetch_second(0, tag="w2_1_bf")
+        products(2, cast_group("w2", 2, ("gpsimd", "gpsimd"), ("stage0", "stage1")))
+        grouped = cast_group("w1", 0, ("gpsimd", "gpsimd"), ("stage0", "stage1"))
+        fetch_second(0, tag="w2_raw12")
         gather_first(0)
-        empty(1, "w2_raw12")
-        products(2, grouped)
-        subtract(0, "stage")
-        grouped = cast_group("w1", 0, ("gpsimd", "scalar"), "first0")
-        fetch_second(1, tag="w2_raw02")
-        gather_first(1)
-        empty(2, "w1_raw10")
-        products(4, grouped)
-        subtract(1, "first0")
-        grouped = cast_group("w1", 2, ("gpsimd", "scalar"), "first1")
-        empty(3, "w1_raw12")
-        fetch_second(2, tag="w1_raw00")
-        gather_first(2)
+        empty(1)
+        empty(2)
+        empty(3)
+        fetch_second(1)
+        products(4, grouped, "w2_raw11")
+        grouped = cast_group("w1", 2, ("gpsimd", "scalar"), ("stage0", "k2p1_code"))
+        gather_first(1, tag="w1_raw10")
+        subtract(0, "w1_raw02", 0, V // 2)
+        fetch_second(2, tag="stage1")
         empty(4)
         empty(5)
-        products(6, grouped)
-        subtract(2, "first1")
-        w3_bf = stage("w3", N * PACK, "first2")
-        cast("gpsimd", w3_bf[:], w3_raw[:])
-        fetch_second(3, tag="w1_raw02")
-        gather_first(3)
-        w3_code, w3_scale = quantize("w3", w3_bf)
+        products(6, grouped, "rows1")
+        subtract(0, "stage0", V // 2, V)
+        subtract(1, "w2_raw12")
+        add_lift(0, "k4p1_code")
+        gather_first(2, tag="w1_raw12")
+        subtract(2, "gap2")
+        fetch_second(3, tag="k2p1_code")
+        gather_first(3, tag="rows2")
         subtract(3, "gap3")
         empty(6)
         empty(7)
-        add_lift(0, "k2_code")
-        add_lift(1, "k4_code")
-        fetch_centre(0, "w3_raw")
-        add_lift(2, "k6_code")
-        fetch_centre(1, "w1_raw12")
-        add_lift(3, "lift3")
+        w3_bf = stage("w3", N * PACK, "rows2")
+        cast("gpsimd", w3_bf[:], w3_raw[:])
 
         out_view = out.rearrange("(u p) v -> p u v", p=P)
         z_bf = {}
 
-        def gather_block(b):
-            centres = cen_t[:, b * P // LIST_ROWS : (b + 1) * P // LIST_ROWS]
-            for u in (2, 3):
-                got = fetch(f"centre{u}{b}", rows[TILES + u], centres, tag=f"piece{(2 * b + u) % 3}")
-                add_turned(got[:], u, b, stop=(u == 3))
+        def fetch_centre(c, u, tag, stop=False):
+            first_block, count = GROUPS[c]
+            centres = cen_t[:, first_block * P // LIST_ROWS : (first_block + count) * P // LIST_ROWS]
+            got = fetch(f"centre{c}{u}", rows[TILES + u], centres, tag)
+            for b in range(count):
+                add_turned(got[:, b * P : (b + 1) * P], u, first_block + b, stop=stop)
 
-        def turn_back(b):
-            z_rows = keep.tile([P, H], BF16, name=f"z_rows{b}")
-            nc.scalar.activation(
-                z_rows[:].rearrange("v (g p e) -> v g p e", g=2, e=2),
-                edge[b][:].rearrange("v (p g e) -> v g p e", g=2, e=2),
-                ACT.Relu,
-            )
-            words = z_rows[:].bitcast(F32)
-            turned = psum.tile([P, 2, P], F32, name=f"turned{b}", tag=f"bank{b % 2}")
-            for g in range(2):
-                nc.tensor.transpose(turned[:, g, :], words[:, g * P : (g + 1) * P], identity[:])
-            z_bf[b] = keep.tile([P, P * PACK], BF16, name=f"z_bf{b}", align_bytes=64)
-            nc.vector.tensor_copy(
-                z_bf[b][:].bitcast(F32).rearrange("p (v g) -> p v g", g=2),
-                turned[:].rearrange("p g v -> p v g"),
-            )
+        def turn_back(c, engine):
+            first_block, count = GROUPS[c]
+            turned = psum.tile([P, count, 2, P], F32, name=f"turned{c}", tag=f"bank{(0, 4, 5)[c]}")
+            for b in range(count):
+                z_rows = keep.tile([P, H], BF16, name=f"z_rows{first_block + b}")
+                dst = z_rows[:].rearrange("v (g p e) -> v g p e", g=2, e=2)
+                parts = [(dst, edge[first_block + b][:])]
+                if first_block + b == BLOCKS - 1:
+                    cut = (TILES - 1) * P
+                    parts = [
+                        (dst[:, :, : cut // PACK, :], edge[BLOCKS - 1][:, :cut]),
+                        (dst[:, :, cut // PACK :, :], last["edge"][:]),
+                    ]
+                for part, sums in parts:
+                    nc.scalar.activation(part, sums.rearrange("v (p g e) -> v g p e", g=2, e=2), ACT.Relu)
+                words = z_rows[:].bitcast(F32)
+                for g in range(2):
+                    nc.tensor.transpose(turned[:, b, g, :], words[:, g * P : (g + 1) * P], identity[:])
+            z_bf[c] = keep.tile([P, count * P * PACK], BF16, name=f"z_bf{c}", align_bytes=64)
+            dst = z_bf[c][:].bitcast(F32).rearrange("p (b v g) -> p b v g", b=count, g=2)
+            src = turned[:].rearrange("p b g v -> p b v g")
+            if engine == "vector":
+                nc.vector.tensor_copy(dst, src)
+            else:
+                nc.scalar.copy(dst, src)
 
-        def project(b):
-            z_code, z_scale = quantize(f"z{b}", z_bf[b])
-            acc = psum.tile([P, N // P, P], F32, name=f"out_acc{b}", tag=f"bank{2 + b % 2}")
+        def project(c):
+            first_block, count = GROUPS[c]
+            z_code, z_scale = quantize(f"z{c}", z_bf[c])
+            acc = psum.tile([P, N // P, count * P], F32, name=f"out_acc{c}", tag=f"bank{(2, 3, 6)[c]}")
             for u in range(N // P):
                 cols = slice(u * P, (u + 1) * P)
                 nc.tensor.matmul_mx(
@@ -301,14 +317,26 @@ def tile_picked_edgecv_relu_p_kernel(
                     start=True,
                     stop=True,
                 )
-            result = keep.tile([P, N // P, P], F32, name=f"result{b}")
+            result = keep.tile([P, N // P, count * P], F32, name=f"result{c}")
             nc.scalar.activation(result[:], acc[:], ACT.Copy)
-            nc.sync.dma_start(out_view[:, :, b * P : (b + 1) * P], result[:])
+            nc.sync.dma_start(out_view[:, :, first_block * P : (first_block + count) * P], result[:])
 
-        for b in range(BLOCKS + 2):
-            if b < BLOCKS:
-                gather_block(b)
-            if 0 < b <= BLOCKS:
-                turn_back(b - 1)
-            if b > 1:
-                project(b - 2)
+        add_lift(1, "rows1")
+        fetch_centre(0, 0, "first0")
+        add_lift(2, "k6p1_code")
+        fetch_centre(0, 1, "rows3")
+        fetch_centre(0, 2, "piece0")
+        add_lift(3, "lift3")
+        fetch_centre(0, 3, "piece1", stop=True)
+        tags = ("rows1", "k6p1_code", "w2_raw12", "piece2")
+        for u in range(TILES):
+            fetch_centre(1, u, tags[u], stop=(u == TILES - 1))
+        turn_back(0, "scalar")
+        for u in range(TILES):
+            fetch_centre(2, u, tags[u], stop=(u >= TILES - 2))
+        w3_code, w3_scale = quantize("w3", w3_bf, "rows4")
+        turn_back(1, "vector")
+        project(0)
+        turn_back(2, "vector")
+        project(1)
+        project(2)

@@ -25,6 +25,7 @@ HALVES = S // BANK
 LIST_ROWS = 16
 TILES = H // P
 BLOCKS = V // P
+SLOT = 1024
 GROUPS = ((0, 2), (2, 1), (3, 1))
 
 
@@ -34,6 +35,7 @@ def tile_picked_edgecv_relu_p_kernel(
     nc = tc.nc
     with ExitStack() as ctx:
         keep = ctx.enter_context(tc.tile_pool(name="keep", bufs=1))
+        lane = ctx.enter_context(tc.tile_pool(name="lane", bufs=1))
         psum = ctx.enter_context(tc.psum_pool(name="psum", bufs=1))
 
         def load_list(name, src):
@@ -148,7 +150,10 @@ def tile_picked_edgecv_relu_p_kernel(
             return rows
 
         def fetch(name, rows, lst, tag=None):
-            got = keep.tile([P, lst.shape[1] * LIST_ROWS], F32, name=name, tag=tag or name, align_bytes=64)
+            if isinstance(tag, int):
+                got = place(name, lst.shape[1] * LIST_ROWS, F32, tag)
+            else:
+                got = keep.tile([P, lst.shape[1] * LIST_ROWS], F32, name=name, tag=tag or name, align_bytes=64)
             nc.vector.tensor_copy(got[:], rows[:].indirect(lst))
             return got
 
@@ -179,21 +184,23 @@ def tile_picked_edgecv_relu_p_kernel(
 
         first, second, gap, rows, banks = {}, {}, {}, {}, {}
 
-        def cast_group(name, start, engines, tags):
-            grouped = []
-            for z, engine in enumerate(engines):
-                src = raw[name, start, z]
-                grouped.append(stage(f"{name}_{start}{z}", src.shape[2] * PACK, tags[z]))
-                cast(engine, grouped[z][:], src[:])
+        def place(name, width, dtype, slot):
+            return lane.tile([P, width], dtype, name=name, offset=slot * SLOT, align_bytes=64)
+
+        def cast_group(name, start, slot):
+            width = 2 * K_PASS
+            grouped = place(f"{name}_{start}_bf", PASSES * width, BF16, slot)
+            for z, engine in enumerate(("gpsimd", "scalar")):
+                cast(engine, grouped[:, z * width : (z + 1) * width], raw[name, start, z][:])
             return grouped
 
-        def products(k, grouped, tag=None):
-            wq = [quantize(f"k{k}p0", grouped[0], tag), quantize(f"k{k}p1", grouped[1])]
+        def products(k, grouped):
+            wq = quantize(f"k{k}", grouped)
             for u in range(2):
                 banks[k + u] = open_banks(k + u)
                 for h in range(HALVES):
                     for z in range(PASSES):
-                        multiply(banks[k + u], wq[z], z, (h,), s=u)
+                        multiply(banks[k + u], wq, z, (h,), s=2 * z + u)
 
         def empty(k, tag=None):
             rows[k] = evacuate(f"rows{k}", banks[k], tag)
@@ -233,37 +240,40 @@ def tile_picked_edgecv_relu_p_kernel(
             first[u] = fetch(f"first{u}", rows[u], pos1_t[:], tag)
 
         def subtract(u, tag, a=0, b=V):
-            part = keep.tile([P, b - a], F32, name=f"gap{u}{a}", tag=tag, align_bytes=64)
+            if isinstance(tag, int):
+                part = place(f"gap{u}{a}", b - a, F32, tag)
+            else:
+                part = keep.tile([P, b - a], F32, name=f"gap{u}{a}", tag=tag, align_bytes=64)
             nc.gpsimd.tensor_tensor(part[:], first[u][:, a:b], second[u][:, a:b], ALU.subtract)
             gap.setdefault(u, []).append((a, b, part))
 
-        products(2, cast_group("w2", 2, ("gpsimd", "gpsimd"), ("stage0", "stage1")))
-        grouped = cast_group("w1", 0, ("gpsimd", "gpsimd"), ("stage0", "stage1"))
-        fetch_second(0, tag="w2_raw12")
-        gather_first(0)
-        empty(1)
+        grouped = cast_group("w2", 2, 0)
+        fetch_second(0)
+        products(2, grouped)
+        grouped = cast_group("w1", 0, 2)
+        gather_first(0, tag=0)
+        empty(1, "w2_raw12")
+        subtract(0, "w1_raw00")
+        fetch_second(1)
+        gather_first(1)
         empty(2)
         empty(3)
-        fetch_second(1)
-        products(4, grouped, "w2_raw11")
-        grouped = cast_group("w1", 2, ("gpsimd", "scalar"), ("stage0", "k2p1_code"))
-        gather_first(1, tag="w1_raw10")
-        subtract(0, "w1_raw02", 0, V // 2)
-        fetch_second(2, tag="stage1")
+        products(4, grouped)
+        grouped = cast_group("w1", 2, 5)
+        fetch_second(2, tag=2)
+        gather_first(2)
         empty(4)
         empty(5)
-        products(6, grouped, "rows1")
-        subtract(0, "stage0", V // 2, V)
-        subtract(1, "w2_raw12")
-        add_lift(0, "k4p1_code")
-        gather_first(2, tag="w1_raw12")
-        subtract(2, "gap2")
-        fetch_second(3, tag="k2p1_code")
-        gather_first(3, tag="rows2")
+        products(6, grouped)
+        subtract(1, 8)
+        subtract(2, "second1")
+        add_lift(0, "k4_code")
+        fetch_second(3, tag=4)
+        gather_first(3, tag=6)
         subtract(3, "gap3")
         empty(6)
         empty(7)
-        w3_bf = stage("w3", N * PACK, "rows2")
+        w3_bf = place("w3_bf", N * PACK, BF16, 6)
         cast("gpsimd", w3_bf[:], w3_raw[:])
 
         out_view = out.rearrange("(u p) v -> p u v", p=P)
@@ -321,14 +331,14 @@ def tile_picked_edgecv_relu_p_kernel(
             nc.scalar.activation(result[:], acc[:], ACT.Copy)
             nc.sync.dma_start(out_view[:, :, first_block * P : (first_block + count) * P], result[:])
 
-        add_lift(1, "rows1")
-        fetch_centre(0, 0, "first0")
-        add_lift(2, "k6p1_code")
+        add_lift(1, "k6_scale")
+        fetch_centre(0, 0, "first1")
+        add_lift(2, "k6_code")
         fetch_centre(0, 1, "rows3")
         fetch_centre(0, 2, "piece0")
         add_lift(3, "lift3")
         fetch_centre(0, 3, "piece1", stop=True)
-        tags = ("rows1", "k6p1_code", "w2_raw12", "piece2")
+        tags = ("k6_scale", "k6_code", 8, "piece2")
         for u in range(TILES):
             fetch_centre(1, u, tags[u], stop=(u == TILES - 1))
         turn_back(0, "scalar")

@@ -25,7 +25,8 @@ HALVES = S // BANK
 LIST_ROWS = 16
 TILES = H // P
 BLOCKS = V // P
-SLOT = 1024
+SLOT = 512
+HEAD_PIECES = ((0, 512, 0), (512, 768, 1), (768, 1024, 4))
 GROUPS = ((0, 2), (2, 1), (3, 1))
 
 
@@ -52,9 +53,12 @@ def tile_picked_edgecv_relu_p_kernel(
 
         raw = {}
 
-        def load_weight(name, w, z, first, count):
+        def load_weight(name, w, z, first, count, slot=None):
             tag = f"{name}_raw{z}{first}"
-            tile = keep.tile([P, PACK, count * P], F32, name=tag, tag=tag, align_bytes=64)
+            if slot is None:
+                tile = keep.tile([P, PACK, count * P], F32, name=tag, tag=tag, align_bytes=64)
+            else:
+                tile = lane.tile([P, PACK, count * P], F32, name=tag, offset=slot * SLOT, align_bytes=64)
             rows = w[z * K_PASS : (z + 1) * K_PASS, first * P : (first + count) * P]
             nc.sync.dma_start(tile[:], rows.rearrange("(p j) c -> p j c", j=PACK))
             raw[name, first, z] = tile
@@ -78,11 +82,9 @@ def tile_picked_edgecv_relu_p_kernel(
         pos2_t = load_list("pos2_t", pos2)
         for z in range(PASSES):
             load_weight("w2", w2, z, 1, 1)
-        for z in range(PASSES):
-            load_weight("w2", w2, z, 2, 2)
-        for first in (0, 2):
-            for z in range(PASSES):
-                load_weight("w1", w1, z, first, 2)
+        for name, w, first, slot in (("w2", w2, 2, 0), ("w1", w1, 0, 24), ("w1", w1, 2, 46)):
+            load_weight(name, w, 0, first, 2)
+            load_weight(name, w, 1, first, 2, slot)
         cen_t = load_list("cen_t", cen)
         w3_raw = keep.tile([P, PACK, N], F32, name="w3_raw", tag="w3_raw", align_bytes=64)
         nc.sync.dma_start(w3_raw[:], w3.rearrange("(p j) n -> p j n", j=PACK))
@@ -110,7 +112,7 @@ def tile_picked_edgecv_relu_p_kernel(
 
         def quantize(name, grouped, tag=None):
             width = grouped.shape[1] // PACK
-            codes = keep.tile([P, width], U32, name=f"{name}_code", tag=tag or f"{name}_code", align_bytes=64)
+            codes = buffer(f"{name}_code", width, tag, U32)
             scales = keep.tile([P, width], U8, name=f"{name}_scale", tag=f"{name}_scale", align_bytes=64)
             nc.vector.quantize_mx(out=codes[:].bitcast(FP8X4), scales=scales[:], in_=grouped[:])
             return codes, scales
@@ -144,20 +146,20 @@ def tile_picked_edgecv_relu_p_kernel(
                 )
 
         def evacuate(name, banks, tag):
-            rows = keep.tile([P, S], F32, name=name, tag=tag or name, align_bytes=64)
+            rows = buffer(name, S, tag)
             for h in range(HALVES):
                 nc.scalar.activation(rows[:, h * BANK : (h + 1) * BANK], banks[h][:], ACT.Copy)
             return rows
 
-        def fetch(name, rows, lst, tag=None):
+        def buffer(name, width, tag, dtype=F32):
             if isinstance(tag, int):
-                got = place(name, lst.shape[1] * LIST_ROWS, F32, tag)
-            else:
-                got = keep.tile([P, lst.shape[1] * LIST_ROWS], F32, name=name, tag=tag or name, align_bytes=64)
+                return place(name, width, dtype, tag)
+            return keep.tile([P, width], dtype, name=name, tag=tag or name, align_bytes=64)
+
+        def fetch(name, rows, lst, tag=None):
+            got = buffer(name, lst.shape[1] * LIST_ROWS, tag)
             nc.vector.tensor_copy(got[:], rows[:].indirect(lst))
             return got
-
-        edge = [psum.tile([P, H], F32, name=f"edge{b}", tag=f"bank{4 + b}") for b in range(BLOCKS)]
 
         last = {}
 
@@ -187,20 +189,20 @@ def tile_picked_edgecv_relu_p_kernel(
         def place(name, width, dtype, slot):
             return lane.tile([P, width], dtype, name=name, offset=slot * SLOT, align_bytes=64)
 
-        def cast_group(name, start, slot):
-            width = 2 * K_PASS
-            grouped = place(f"{name}_{start}_bf", PASSES * width, BF16, slot)
+        def cast_group(name, start, slots):
+            grouped = []
             for z, engine in enumerate(("gpsimd", "scalar")):
-                cast(engine, grouped[:, z * width : (z + 1) * width], raw[name, start, z][:])
+                grouped.append(place(f"{name}_{start}{z}_bf", 2 * K_PASS, BF16, slots[z]))
+                cast(engine, grouped[z][:], raw[name, start, z][:])
             return grouped
 
-        def products(k, grouped):
-            wq = quantize(f"k{k}", grouped)
+        def products(k, grouped, slots):
+            wq = [quantize(f"k{k}p{z}", grouped[z], slots[z]) for z in range(PASSES)]
             for u in range(2):
                 banks[k + u] = open_banks(k + u)
                 for h in range(HALVES):
                     for z in range(PASSES):
-                        multiply(banks[k + u], wq, z, (h,), s=2 * z + u)
+                        multiply(banks[k + u], wq[z], z, (h,), s=u)
 
         def empty(k, tag=None):
             rows[k] = evacuate(f"rows{k}", banks[k], tag)
@@ -209,71 +211,106 @@ def tile_picked_edgecv_relu_p_kernel(
             second[u] = fetch(f"second{u}", rows[u], pos2_t[:], tag)
             add_turned_all(second[u], u, start=(u == 0))
 
-        def add_lift(u, tag):
-            lift = keep.tile([P, V], F32, name=f"lift{u}", tag=tag, align_bytes=64)
-            for a, b, part in gap[u]:
-                nc.scalar.activation(lift[:, a:b], part[:], ACT.Relu)
-            add_turned_all(lift, u)
+        def add_lift(u, tag, a=0, b=V):
+            lift = buffer(f"lift{u}{a}", b - a, tag)
+            nc.scalar.activation(lift[:], gap[u, a][:], ACT.Relu)
+            for v in range(a, b, P):
+                add_turned(lift[:, v - a : v - a + P], u, v // P)
 
-        def head_cast(k, z):
-            grouped = stage(f"k{k}p{z}", K_PASS)
-            cast("scalar", grouped[:], raw["w2", k, z][:])
-            return grouped
+        def head_weights(k):
+            grouped = stage(f"k{k}", PASSES * K_PASS)
+            for z in range(PASSES):
+                cast("scalar", grouped[:, z * K_PASS : (z + 1) * K_PASS], raw["w2", k, z][:])
+            return quantize(f"k{k}", grouped)
+
+        def head_pass(z):
+            grouped = stage(f"k0p{z}", K_PASS)
+            cast("scalar", grouped[:], raw["w2", 0, z][:])
+            return quantize(f"k0p{z}", grouped)
+
+        def head_product(wq, z, piece):
+            a, b, bank = HEAD_PIECES[piece]
+            h = a // BANK
+            nc.tensor.matmul_mx(
+                out=head_banks[piece][:],
+                lhsT=wq[0][:].bitcast(FP8X4),
+                lhsT_scale=wq[1][:],
+                rhs=x_code[z, h][:, a - h * BANK : b - h * BANK].bitcast(FP8X4),
+                rhs_scale=x_scale[4 * z : P, a:b],
+                start=(z == 0),
+                stop=(z == PASSES - 1),
+            )
 
         for h in range(HALVES):
             pick_words(0, h)
         x_scale = keep.tile([P, S], U8, name="x_scale", align_bytes=64)
         nc.vector.tensor_copy(x_scale[:], scale_table[:].indirect(offs_t[:]))
-        banks[0], banks[1] = open_banks(0), open_banks(1)
-        multiply(banks[0], quantize("k0p0", head_cast(0, 0)), 0)
+        head_banks = [
+            psum.tile([P, b - a], F32, name=f"head{a}", tag=f"bank{bank}") for a, b, bank in HEAD_PIECES
+        ]
+        wq = head_pass(0)
+        for piece in range(len(HEAD_PIECES)):
+            head_product(wq, 0, piece)
         pick_words(1, 0)
-        wq = quantize("k0p1", head_cast(0, 1))
-        multiply(banks[0], wq, 1, (0,))
-        multiply(banks[1], quantize("k1p0", head_cast(1, 0)), 0)
-        pick_words(1, 1, tag="w2_raw01")
-        multiply(banks[0], wq, 1, (1,))
-        wq = quantize("k1p1", head_cast(1, 1))
-        empty(0, "w2_raw11")
-        multiply(banks[1], wq, 1)
+        wq = head_pass(1)
+        head_product(wq, 1, 0)
+        x_code[1, 1] = keep.tile([P, BANK], U32, name="x_code11", tag="w2_raw10", align_bytes=64)
+        for piece in range(1, len(HEAD_PIECES)):
+            a, b, bank = HEAD_PIECES[piece]
+            nc.vector.tensor_copy(
+                x_code[1, 1][:, a - BANK : b - BANK],
+                x_table[1][:].indirect(offs_t[:, a // LIST_ROWS : b // LIST_ROWS]),
+            )
+            head_product(wq, 1, piece)
+        wq = head_weights(1)
+        rows[0] = keep.tile([P, S], F32, name="rows0", tag="w2_raw11", align_bytes=64)
+        for piece, (a, b, bank) in enumerate(HEAD_PIECES):
+            nc.scalar.activation(rows[0][:, a:b], head_banks[piece][:], ACT.Copy)
+        banks[1] = open_banks(1)
+        for h in range(HALVES):
+            for z in range(PASSES):
+                multiply(banks[1], wq, z, (h,), s=z)
+        edge = [psum.tile([P, H], F32, name=f"edge{b}", tag=f"bank{4 + b}") for b in range(BLOCKS)]
 
         def gather_first(u, tag=None):
             first[u] = fetch(f"first{u}", rows[u], pos1_t[:], tag)
 
         def subtract(u, tag, a=0, b=V):
-            if isinstance(tag, int):
-                part = place(f"gap{u}{a}", b - a, F32, tag)
-            else:
-                part = keep.tile([P, b - a], F32, name=f"gap{u}{a}", tag=tag, align_bytes=64)
+            part = buffer(f"gap{u}{a}", b - a, tag)
             nc.gpsimd.tensor_tensor(part[:], first[u][:, a:b], second[u][:, a:b], ALU.subtract)
-            gap.setdefault(u, []).append((a, b, part))
+            gap[u, a] = part
 
-        grouped = cast_group("w2", 2, 0)
+        half = V // 2
+        grouped = cast_group("w2", 2, (16, 20))
         fetch_second(0)
-        products(2, grouped)
-        grouped = cast_group("w1", 0, 2)
-        gather_first(0, tag=0)
-        empty(1, "w2_raw12")
+        products(2, grouped, (0, 40))
+        empty(1, 7)
+        grouped = cast_group("w1", 0, (20, 32))
+        gather_first(0, tag=16)
         subtract(0, "w1_raw00")
         fetch_second(1)
         gather_first(1)
         empty(2)
         empty(3)
-        products(4, grouped)
-        grouped = cast_group("w1", 2, 5)
-        fetch_second(2, tag=2)
+        products(4, grouped, (24, None))
+        grouped = cast_group("w1", 2, (32, 40))
+        fetch_second(2, tag=20)
         gather_first(2)
         empty(4)
         empty(5)
-        products(6, grouped)
-        subtract(1, 8)
-        subtract(2, "second1")
-        add_lift(0, "k4_code")
-        fetch_second(3, tag=4)
-        gather_first(3, tag=6)
-        subtract(3, "gap3")
+        products(6, grouped, (46, None))
+        subtract(1, 39, 0, half)
+        subtract(2, 41, 0, half)
+        add_lift(0, "k4p1_code")
+        fetch_second(3, tag=29)
+        gather_first(3, tag=35)
+        subtract(3, None, 0, half)
+        subtract(1, 43, half, V)
+        subtract(2, "second1", half, V)
+        subtract(3, None, half, V)
         empty(6)
         empty(7)
-        w3_bf = place("w3_bf", N * PACK, BF16, 6)
+        w3_bf = place("w3_bf", N * PACK, BF16, 35)
         cast("gpsimd", w3_bf[:], w3_raw[:])
 
         out_view = out.rearrange("(u p) v -> p u v", p=P)
@@ -286,9 +323,11 @@ def tile_picked_edgecv_relu_p_kernel(
             for b in range(count):
                 add_turned(got[:, b * P : (b + 1) * P], u, first_block + b, stop=stop)
 
-        def turn_back(c, engine):
+        turned = {}
+
+        def turn_back(c):
             first_block, count = GROUPS[c]
-            turned = psum.tile([P, count, 2, P], F32, name=f"turned{c}", tag=f"bank{(0, 4, 5)[c]}")
+            turned[c] = psum.tile([P, count, 2, P], F32, name=f"turned{c}", tag=f"bank{(0, 4, 5)[c]}")
             for b in range(count):
                 z_rows = keep.tile([P, H], BF16, name=f"z_rows{first_block + b}")
                 dst = z_rows[:].rearrange("v (g p e) -> v g p e", g=2, e=2)
@@ -299,22 +338,32 @@ def tile_picked_edgecv_relu_p_kernel(
                         (dst[:, :, : cut // PACK, :], edge[BLOCKS - 1][:, :cut]),
                         (dst[:, :, cut // PACK :, :], last["edge"][:]),
                     ]
-                for part, sums in parts:
-                    nc.scalar.activation(part, sums.rearrange("v (p g e) -> v g p e", g=2, e=2), ACT.Relu)
+                for n, (part, sums) in enumerate(parts):
+                    view = sums.rearrange("v (p g e) -> v g p e", g=2, e=2)
+                    if n == 0:
+                        nc.scalar.activation(part, view, ACT.Relu)
+                    else:
+                        nc.vector.tensor_scalar_max(part, view, 0.0)
                 words = z_rows[:].bitcast(F32)
                 for g in range(2):
-                    nc.tensor.transpose(turned[:, b, g, :], words[:, g * P : (g + 1) * P], identity[:])
+                    nc.tensor.transpose(turned[c][:, b, g, :], words[:, g * P : (g + 1) * P], identity[:])
+
+        def weave(c, engine):
+            count = GROUPS[c][1]
             z_bf[c] = keep.tile([P, count * P * PACK], BF16, name=f"z_bf{c}", align_bytes=64)
             dst = z_bf[c][:].bitcast(F32).rearrange("p (b v g) -> p b v g", b=count, g=2)
-            src = turned[:].rearrange("p b g v -> p b v g")
+            src = turned[c][:].rearrange("p b g v -> p b v g")
             if engine == "vector":
                 nc.vector.tensor_copy(dst, src)
             else:
                 nc.scalar.copy(dst, src)
 
-        def project(c):
+        def pack(c):
+            return quantize(f"z{c}", z_bf[c])
+
+        def project(c, zq):
             first_block, count = GROUPS[c]
-            z_code, z_scale = quantize(f"z{c}", z_bf[c])
+            z_code, z_scale = zq
             acc = psum.tile([P, N // P, count * P], F32, name=f"out_acc{c}", tag=f"bank{(2, 3, 6)[c]}")
             for u in range(N // P):
                 cols = slice(u * P, (u + 1) * P)
@@ -328,25 +377,36 @@ def tile_picked_edgecv_relu_p_kernel(
                     stop=True,
                 )
             result = keep.tile([P, N // P, count * P], F32, name=f"result{c}")
-            nc.scalar.activation(result[:], acc[:], ACT.Copy)
+            if c == 1:
+                nc.vector.tensor_copy(result[:], acc[:])
+            else:
+                nc.scalar.activation(result[:], acc[:], ACT.Copy)
             nc.sync.dma_start(out_view[:, :, first_block * P : (first_block + count) * P], result[:])
 
-        add_lift(1, "k6_scale")
         fetch_centre(0, 0, "first1")
-        add_lift(2, "k6_code")
+        add_lift(1, "k6p1_scale", 0, half)
         fetch_centre(0, 1, "rows3")
+        add_lift(2, "k6p1_code", 0, half)
         fetch_centre(0, 2, "piece0")
-        add_lift(3, "lift3")
+        add_lift(3, None, 0, half)
         fetch_centre(0, 3, "piece1", stop=True)
-        tags = ("k6_scale", "k6_code", 8, "piece2")
+        add_lift(1, 39, half, V)
+        add_lift(2, 41, half, V)
+        tags = ("k6p1_scale", "k6p1_code", 43, "piece2")
         for u in range(TILES):
+            if u == TILES - 1:
+                add_lift(3, None, half, V)
             fetch_centre(1, u, tags[u], stop=(u == TILES - 1))
-        turn_back(0, "scalar")
+        turn_back(0)
         for u in range(TILES):
-            fetch_centre(2, u, tags[u], stop=(u >= TILES - 2))
-        w3_code, w3_scale = quantize("w3", w3_bf, "rows4")
-        turn_back(1, "vector")
-        project(0)
-        turn_back(2, "vector")
-        project(1)
-        project(2)
+            fetch_centre(2, u, (39, 41, "second1", f"lift3{half}")[u], stop=(u >= TILES - 2))
+        turn_back(1)
+        weave(0, "scalar")
+        turn_back(2)
+        w3_code, w3_scale = quantize("w3", w3_bf, "rows6")
+        weave(1, "scalar")
+        project(0, pack(0))
+        weave(2, "vector")
+        quantized = [pack(1), pack(2)]
+        project(1, quantized[0])
+        project(2, quantized[1])

@@ -81,7 +81,7 @@ def tile_picked_edgecv_relu_p_kernel(
         pos1_t = load_list("pos1_t", pos1)
         pos2_t = load_list("pos2_t", pos2)
         for z in range(PASSES):
-            load_weight("w2", w2, z, 1, 1)
+            load_weight("w2", w2, z, 1, 1, (None, 62)[z])
         for name, w, first, slot in (("w2", w2, 2, 0), ("w1", w1, 0, 24), ("w1", w1, 2, 46)):
             load_weight(name, w, 0, first, 2)
             load_weight(name, w, 1, first, 2, slot)
@@ -218,7 +218,7 @@ def tile_picked_edgecv_relu_p_kernel(
                 add_turned(lift[:, v - a : v - a + P], u, v // P)
 
         def head_weights(k):
-            grouped = stage(f"k{k}", PASSES * K_PASS)
+            grouped = place(f"k{k}_bf", PASSES * K_PASS, BF16, 16)
             for z in range(PASSES):
                 cast("scalar", grouped[:, z * K_PASS : (z + 1) * K_PASS], raw["w2", k, z][:])
             return quantize(f"k{k}", grouped)
@@ -263,7 +263,7 @@ def tile_picked_edgecv_relu_p_kernel(
             )
             head_product(wq, 1, piece)
         wq = head_weights(1)
-        rows[0] = keep.tile([P, S], F32, name="rows0", tag="w2_raw11", align_bytes=64)
+        rows[0] = place("rows0", S, F32, 62)
         for piece, (a, b, bank) in enumerate(HEAD_PIECES):
             nc.scalar.activation(rows[0][:, a:b], head_banks[piece][:], ACT.Copy)
         banks[1] = open_banks(1)
@@ -285,16 +285,16 @@ def tile_picked_edgecv_relu_p_kernel(
         fetch_second(0)
         products(2, grouped, (0, 40))
         empty(1, 7)
-        grouped = cast_group("w1", 0, (20, 32))
-        gather_first(0, tag=16)
-        subtract(0, "w1_raw00")
+        gap[0, 0] = buffer("gap00", V, 16)
+        nc.vector.tensor_tensor(gap[0, 0][:], rows[0][:].indirect(pos1_t[:]), second[0][:], ALU.subtract)
+        grouped = cast_group("w1", 0, (62, 32))
         fetch_second(1)
         gather_first(1)
         empty(2)
         empty(3)
         products(4, grouped, (24, None))
         grouped = cast_group("w1", 2, (32, 40))
-        fetch_second(2, tag=20)
+        fetch_second(2, tag=62)
         gather_first(2)
         empty(4)
         empty(5)

@@ -275,42 +275,42 @@ def tile_picked_edgecv_relu_p_kernel(
         def gather_first(u, tag=None):
             first[u] = fetch(f"first{u}", rows[u], pos1_t[:], tag)
 
+        def fetch_gap(u, tag):
+            gap[u, 0] = buffer(f"gap{u}0", V, tag)
+            nc.vector.tensor_tensor(gap[u, 0][:], rows[u][:].indirect(pos1_t[:]), second[u][:], ALU.subtract)
+
         def subtract(u, tag, a=0, b=V):
             part = buffer(f"gap{u}{a}", b - a, tag)
             nc.gpsimd.tensor_tensor(part[:], first[u][:, a:b], second[u][:, a:b], ALU.subtract)
             gap[u, a] = part
 
-        half = V // 2
         grouped = cast_group("w2", 2, (16, 20))
         fetch_second(0)
         products(2, grouped, (0, 40))
         empty(1, 7)
-        gap[0, 0] = buffer("gap00", V, 16)
-        nc.vector.tensor_tensor(gap[0, 0][:], rows[0][:].indirect(pos1_t[:]), second[0][:], ALU.subtract)
+        fetch_gap(0, 16)
         grouped = cast_group("w1", 0, (62, 32))
         fetch_second(1)
         gather_first(1)
         empty(2)
-        empty(3)
+        empty(3, 54)
         products(4, grouped, (24, None))
         grouped = cast_group("w1", 2, (32, 40))
+        subtract(1, "w1_raw02")
         fetch_second(2, tag=62)
         gather_first(2)
+        second[3] = fetch("second3", rows[3], pos2_t[:])
         empty(4)
         empty(5)
         products(6, grouped, (46, None))
-        subtract(1, 39, 0, half)
-        subtract(2, 41, 0, half)
         add_lift(0, "k4p1_code")
-        fetch_second(3, tag=29)
-        gather_first(3, tag=35)
-        subtract(3, None, 0, half)
-        subtract(1, 43, half, V)
-        subtract(2, "second1", half, V)
-        subtract(3, None, half, V)
+        add_lift(1, "k4p1_scale")
+        fetch_gap(3, 35)
+        add_turned_all(second[3], 3)
+        subtract(2, 54)
         empty(6)
         empty(7)
-        w3_bf = place("w3_bf", N * PACK, BF16, 35)
+        w3_bf = place("w3_bf", N * PACK, BF16, 62)
         cast("gpsimd", w3_bf[:], w3_raw[:])
 
         out_view = out.rearrange("(u p) v -> p u v", p=P)
@@ -348,9 +348,9 @@ def tile_picked_edgecv_relu_p_kernel(
                 for g in range(2):
                     nc.tensor.transpose(turned[c][:, b, g, :], words[:, g * P : (g + 1) * P], identity[:])
 
-        def weave(c, engine):
+        def weave(c, engine, tag=None):
             count = GROUPS[c][1]
-            z_bf[c] = keep.tile([P, count * P * PACK], BF16, name=f"z_bf{c}", align_bytes=64)
+            z_bf[c] = buffer(f"z_bf{c}", count * P * PACK, tag, BF16)
             dst = z_bf[c][:].bitcast(F32).rearrange("p (b v g) -> p b v g", b=count, g=2)
             src = turned[c][:].rearrange("p b g v -> p b v g")
             if engine == "vector":
@@ -364,11 +364,15 @@ def tile_picked_edgecv_relu_p_kernel(
         def project(c, zq):
             first_block, count = GROUPS[c]
             z_code, z_scale = zq
-            acc = psum.tile([P, N // P, count * P], F32, name=f"out_acc{c}", tag=f"bank{(2, 3, 6)[c]}")
+            if c == len(GROUPS) - 1:
+                acc = [psum.tile([P, P], F32, name=f"out_acc{c}{u}", tag=f"bank{6 + u}")[:] for u in range(N // P)]
+            else:
+                both = psum.tile([P, N // P, count * P], F32, name=f"out_acc{c}", tag=f"bank{2 + c}")
+                acc = [both[:, u, :] for u in range(N // P)]
             for u in range(N // P):
                 cols = slice(u * P, (u + 1) * P)
                 nc.tensor.matmul_mx(
-                    out=acc[:, u, :],
+                    out=acc[u],
                     lhsT=w3_code[:, cols].bitcast(FP8X4),
                     lhsT_scale=w3_scale[:, cols],
                     rhs=z_code[:].bitcast(FP8X4),
@@ -377,33 +381,28 @@ def tile_picked_edgecv_relu_p_kernel(
                     stop=True,
                 )
             result = keep.tile([P, N // P, count * P], F32, name=f"result{c}")
-            if c == 1:
-                nc.vector.tensor_copy(result[:], acc[:])
+            if c < len(GROUPS) - 1:
+                nc.scalar.activation(result[:], both[:], ACT.Copy)
             else:
-                nc.scalar.activation(result[:], acc[:], ACT.Copy)
+                nc.scalar.activation(result[:, 0, :], acc[0], ACT.Copy)
+                nc.vector.tensor_copy(result[:, 1, :], acc[1])
             nc.sync.dma_start(out_view[:, :, first_block * P : (first_block + count) * P], result[:])
 
-        fetch_centre(0, 0, "first1")
-        add_lift(1, "k6p1_scale", 0, half)
-        fetch_centre(0, 1, "rows3")
-        add_lift(2, "k6p1_code", 0, half)
+        fetch_centre(0, 0, 43)
+        fetch_centre(0, 1, 58)
+        add_lift(3, "k6p1_code")
         fetch_centre(0, 2, "piece0")
-        add_lift(3, None, 0, half)
+        add_lift(2, 46)
         fetch_centre(0, 3, "piece1", stop=True)
-        add_lift(1, 39, half, V)
-        add_lift(2, 41, half, V)
-        tags = ("k6p1_scale", "k6p1_code", 43, "piece2")
         for u in range(TILES):
-            if u == TILES - 1:
-                add_lift(3, None, half, V)
-            fetch_centre(1, u, tags[u], stop=(u == TILES - 1))
+            fetch_centre(1, u, ("k6p1_code", 46, 35, "piece2")[u], stop=(u == TILES - 1))
         turn_back(0)
         for u in range(TILES):
-            fetch_centre(2, u, (39, 41, "second1", f"lift3{half}")[u], stop=(u >= TILES - 2))
+            fetch_centre(2, u, (54, 47, 48, 49)[u], stop=(u >= TILES - 2))
         turn_back(1)
-        weave(0, "scalar")
+        weave(0, "vector", "rows6")
         turn_back(2)
-        w3_code, w3_scale = quantize("w3", w3_bf, "rows6")
+        w3_code, w3_scale = quantize("w3", w3_bf, "rows7")
         weave(1, "scalar")
         project(0, pack(0))
         weave(2, "vector")

@@ -27,6 +27,7 @@ TILES = H // P
 BLOCKS = V // P
 SLOT = 512
 HEAD_PIECES = ((0, 512, 0), (512, 768, 1), (768, 1024, 4))
+TILE_BANKS = (0, 2, 0, 0, 2, 2, 0, 2)
 GROUPS = ((0, 2), (2, 1), (3, 1))
 
 
@@ -110,16 +111,16 @@ def tile_picked_edgecv_relu_p_kernel(
                 else:
                     nc.scalar.activation(dst, view, ACT.Copy)
 
-        def quantize(name, grouped, tag=None):
+        def quantize(name, grouped, tag=None, scale_tag=None):
             width = grouped.shape[1] // PACK
             codes = buffer(f"{name}_code", width, tag, U32)
-            scales = keep.tile([P, width], U8, name=f"{name}_scale", tag=f"{name}_scale", align_bytes=64)
+            scales = keep.tile([P, width], U8, name=f"{name}_scale", tag=scale_tag or f"{name}_scale", align_bytes=64)
             nc.vector.quantize_mx(out=codes[:].bitcast(FP8X4), scales=scales[:], in_=grouped[:])
             return codes, scales
 
         def open_banks(k):
             return [
-                psum.tile([P, BANK], F32, name=f"acc{k}{h}", tag=f"bank{HALVES * (k % 2) + h}")
+                psum.tile([P, BANK], F32, name=f"acc{k}{h}", tag=f"bank{TILE_BANKS[k] + h}")
                 for h in range(HALVES)
             ]
 
@@ -184,7 +185,7 @@ def tile_picked_edgecv_relu_p_kernel(
             for b in range(BLOCKS):
                 add_turned(values[:, b * P : (b + 1) * P], u, b, start=start)
 
-        first, second, gap, rows, banks = {}, {}, {}, {}, {}
+        first, second, gap, rows, banks, pair_codes = {}, {}, {}, {}, {}, {}
 
         def place(name, width, dtype, slot):
             return lane.tile([P, width], dtype, name=name, offset=slot * SLOT, align_bytes=64)
@@ -196,13 +197,15 @@ def tile_picked_edgecv_relu_p_kernel(
                 cast(engine, grouped[z][:], raw[name, start, z][:])
             return grouped
 
-        def products(k, grouped, slots):
-            wq = [quantize(f"k{k}p{z}", grouped[z], slots[z]) for z in range(PASSES)]
-            for u in range(2):
-                banks[k + u] = open_banks(k + u)
-                for h in range(HALVES):
-                    for z in range(PASSES):
-                        multiply(banks[k + u], wq[z], z, (h,), s=u)
+        def products(k, grouped, slots, scale_tags=(None, None)):
+            pair_codes[k] = [quantize(f"k{k}p{z}", grouped[z], slots[z], scale_tags[z]) for z in range(PASSES)]
+            product(k)
+
+        def product(k):
+            banks[k] = open_banks(k)
+            for h in range(HALVES):
+                for z in range(PASSES):
+                    multiply(banks[k], pair_codes[k - k % 2][z], z, (h,), s=k % 2)
 
         def empty(k, tag=None):
             rows[k] = evacuate(f"rows{k}", banks[k], tag)
@@ -290,21 +293,26 @@ def tile_picked_edgecv_relu_p_kernel(
         empty(1, 7)
         fetch_gap(0, 16)
         grouped = cast_group("w1", 0, (62, 32))
-        fetch_second(1)
+        second[1] = fetch("second1", rows[1], pos2_t[:])
         gather_first(1)
         empty(2)
+        product(3)
         empty(3, 54)
         products(4, grouped, (24, None))
         grouped = cast_group("w1", 2, (32, 40))
         subtract(1, "w1_raw02")
-        fetch_second(2, tag=62)
+        second[2] = fetch("second2", rows[2], pos2_t[:], 62)
         gather_first(2)
         second[3] = fetch("second3", rows[3], pos2_t[:])
         empty(4)
+        product(5)
         empty(5)
-        products(6, grouped, (46, None))
-        add_lift(0, "k4p1_code")
-        add_lift(1, "k4p1_scale")
+        products(6, grouped, (46, "k4p1_code"), ("k4p1_scale", None))
+        product(7)
+        add_lift(0, 21)
+        add_turned_all(second[1], 1)
+        add_turned_all(second[2], 2)
+        add_lift(1, 25)
         fetch_gap(3, 35)
         add_turned_all(second[3], 3)
         subtract(2, 54)
@@ -390,12 +398,12 @@ def tile_picked_edgecv_relu_p_kernel(
 
         fetch_centre(0, 0, 43)
         fetch_centre(0, 1, 58)
-        add_lift(3, "k6p1_code")
+        add_lift(3, "k4p1_code")
         fetch_centre(0, 2, "piece0")
         add_lift(2, 46)
         fetch_centre(0, 3, "piece1", stop=True)
         for u in range(TILES):
-            fetch_centre(1, u, ("k6p1_code", 46, 35, "piece2")[u], stop=(u == TILES - 1))
+            fetch_centre(1, u, ("k4p1_code", 46, 35, "piece2")[u], stop=(u == TILES - 1))
         turn_back(0)
         for u in range(TILES):
             fetch_centre(2, u, (54, 47, 48, 49)[u], stop=(u >= TILES - 2))

@@ -27,7 +27,7 @@ TILES = H // P
 BLOCKS = V // P
 SLOT = 512
 HEAD_PIECES = ((0, 512, 0), (512, 768, 1), (768, 1024, 4))
-TILE_BANKS = (0, 2, 0, 0, 2, 2, 0, 2)
+TILE_BANKS = (0, 2, 0, 0, 2, 0, 2, 0)
 GROUPS = ((0, 2), (2, 1), (3, 1))
 
 
@@ -168,7 +168,7 @@ def tile_picked_edgecv_relu_p_kernel(
             if (u, b) == (TILES - 1, BLOCKS - 1):
                 start = not last
                 if start:
-                    last["edge"] = psum.tile([P, P], F32, name="edge_last", tag="bank1")
+                    last["edge"] = psum.tile([P, P], F32, name="edge_last", tag="bank3")
                 dst = last["edge"][:]
             else:
                 dst = edge[b][:, u * P : (u + 1) * P]
@@ -216,7 +216,8 @@ def tile_picked_edgecv_relu_p_kernel(
 
         def add_lift(u, tag, a=0, b=V):
             lift = buffer(f"lift{u}{a}", b - a, tag)
-            nc.scalar.activation(lift[:], gap[u, a][:], ACT.Relu)
+            src = gap[u, a][:] if (u, a) in gap and gap[u, a].shape[1] == b - a else gap[u, 0][:, a:b]
+            nc.scalar.activation(lift[:], src, ACT.Relu)
             for v in range(a, b, P):
                 add_turned(lift[:, v - a : v - a + P], u, v // P)
 
@@ -299,27 +300,24 @@ def tile_picked_edgecv_relu_p_kernel(
         product(3)
         empty(3, 54)
         products(4, grouped, (24, None))
+        product(5)
         grouped = cast_group("w1", 2, (32, 40))
-        subtract(1, "w1_raw02")
         second[2] = fetch("second2", rows[2], pos2_t[:], 62)
         gather_first(2)
-        second[3] = fetch("second3", rows[3], pos2_t[:])
         empty(4)
-        product(5)
         empty(5)
-        products(6, grouped, (46, "k4p1_code"), ("k4p1_scale", None))
+        products(6, grouped, (46, None))
         product(7)
-        add_lift(0, 21)
+        half = V // 2
+        subtract(1, 38)
+        subtract(2, 42, 0, half)
+        add_lift(0, 24)
         add_turned_all(second[1], 1)
         add_turned_all(second[2], 2)
-        add_lift(1, 25)
-        fetch_gap(3, 35)
-        add_turned_all(second[3], 3)
-        subtract(2, 54)
         empty(6)
         empty(7)
+        fetch_second(3, 29)
         w3_bf = place("w3_bf", N * PACK, BF16, 62)
-        cast("gpsimd", w3_bf[:], w3_raw[:])
 
         out_view = out.rearrange("(u p) v -> p u v", p=P)
         z_bf = {}
@@ -375,7 +373,7 @@ def tile_picked_edgecv_relu_p_kernel(
             if c == len(GROUPS) - 1:
                 acc = [psum.tile([P, P], F32, name=f"out_acc{c}{u}", tag=f"bank{6 + u}")[:] for u in range(N // P)]
             else:
-                both = psum.tile([P, N // P, count * P], F32, name=f"out_acc{c}", tag=f"bank{2 + c}")
+                both = psum.tile([P, N // P, count * P], F32, name=f"out_acc{c}", tag=f"bank{(2, 1)[c]}")
                 acc = [both[:, u, :] for u in range(N // P)]
             for u in range(N // P):
                 cols = slice(u * P, (u + 1) * P)
@@ -396,21 +394,27 @@ def tile_picked_edgecv_relu_p_kernel(
                 nc.vector.tensor_copy(result[:, 1, :], acc[1])
             nc.sync.dma_start(out_view[:, :, first_block * P : (first_block + count) * P], result[:])
 
-        fetch_centre(0, 0, 43)
-        fetch_centre(0, 1, 58)
-        add_lift(3, "k4p1_code")
+        fetch_centre(0, 0, 33)
+        fetch_centre(0, 1, 35)
+        fetch_gap(3, 16)
+        subtract(2, 54, half, V)
+        cast("gpsimd", w3_bf[:], w3_raw[:])
+        add_lift(1, "k6p1_code")
+        add_lift(2, 46, 0, half)
+        add_lift(3, None, 0, half)
         fetch_centre(0, 2, "piece0")
-        add_lift(2, 46)
         fetch_centre(0, 3, "piece1", stop=True)
+        add_lift(3, 38, half, V)
+        add_lift(2, 42, half, V)
         for u in range(TILES):
-            fetch_centre(1, u, ("k4p1_code", 46, 35, "piece2")[u], stop=(u == TILES - 1))
+            fetch_centre(1, u, (46, 47, "lift30", "piece2")[u], stop=(u == TILES - 1))
         turn_back(0)
         for u in range(TILES):
-            fetch_centre(2, u, (54, 47, 48, 49)[u], stop=(u >= TILES - 2))
+            fetch_centre(2, u, (38, 39, 42, 43)[u], stop=(u >= TILES - 2))
         turn_back(1)
-        weave(0, "vector", "rows6")
+        weave(0, "scalar")
         turn_back(2)
-        w3_code, w3_scale = quantize("w3", w3_bf, "rows7")
+        w3_code, w3_scale = quantize("w3", w3_bf, "rows6")
         weave(1, "scalar")
         project(0, pack(0))
         weave(2, "vector")

@@ -1,7 +1,6 @@
 from contextlib import ExitStack
 
 import concourse.mybir as mybir
-from concourse.masks import make_identity
 
 K, T, S, V, H, N = 1024, 2048, 1024, 512, 512, 256
 FLOPS = 2 * (2 * K * H * S + H * N * V)
@@ -24,11 +23,15 @@ BANK = 512
 HALVES = S // BANK
 LIST_ROWS = 16
 TILES = H // P
-BLOCKS = V // P
-SLOT = 512
-HEAD_PIECES = ((0, 512, 0), (512, 768, 1), (768, 1024, 4))
-TILE_BANKS = (0, 2, 0, 0, 2, 0, 2, 0)
-GROUPS = ((0, 2), (2, 1), (3, 1))
+RUN = 4
+CHUNKS = ((0, 256), (256, 384), (384, 512))
+
+FIRST_BANK = {"w2": (0, 2, 4, 2), "w1": (6, 0, 4, 2)}
+OUT_BANK = (6, 7, 0)
+
+BEST_FIRST, BEST_REST = 2048, 6144
+LAST_RAW = 2048
+PAIR_STAGE, FAR_REST = 10816, 13888
 
 
 def tile_picked_edgecv_relu_p_kernel(
@@ -39,6 +42,11 @@ def tile_picked_edgecv_relu_p_kernel(
         keep = ctx.enter_context(tc.tile_pool(name="keep", bufs=1))
         lane = ctx.enter_context(tc.tile_pool(name="lane", bufs=1))
         psum = ctx.enter_context(tc.psum_pool(name="psum", bufs=1))
+
+        def buffer(name, shape, dtype, at=None, tag=None):
+            if at is None:
+                return keep.tile(shape, dtype, name=name, tag=tag or name, align_bytes=64)
+            return lane.tile(shape, dtype, name=name, offset=at, align_bytes=64)
 
         def load_list(name, src):
             lst = keep.tile(list(src.shape), U16, name=name)
@@ -54,20 +62,13 @@ def tile_picked_edgecv_relu_p_kernel(
 
         raw = {}
 
-        def load_weight(name, w, z, first, count, slot=None):
-            tag = f"{name}_raw{z}{first}"
-            if slot is None:
-                tile = keep.tile([P, PACK, count * P], F32, name=tag, tag=tag, align_bytes=64)
-            else:
-                tile = lane.tile([P, PACK, count * P], F32, name=tag, offset=slot * SLOT, align_bytes=64)
-            rows = w[z * K_PASS : (z + 1) * K_PASS, first * P : (first + count) * P]
-            nc.sync.dma_start(tile[:], rows.rearrange("(p j) c -> p j c", j=PACK))
-            raw[name, first, z] = tile
+        def load_weight(name, w, z, at=None):
+            raw[name, z] = buffer(f"{name}_raw{z}", [P, PACK, H], F32, at)
+            rows = w[z * K_PASS : (z + 1) * K_PASS, :]
+            nc.sync.dma_start(raw[name, z][:], rows.rearrange("(p j) c -> p j c", j=PACK))
 
         scale_table = keep.tile([P, T], U8, name="scale_table")
         nc.vector.memset(scale_table[:].bitcast(I32), 0)
-        identity = keep.tile([P, P], F32, name="identity")
-        make_identity(nc, identity[:])
 
         offs_t = load_list("offs_t", offs)
         x_table = [load_words(0)]
@@ -76,304 +77,209 @@ def tile_picked_edgecv_relu_p_kernel(
                 scale_table[32 * q : 32 * q + 4 * PASSES, :].bitcast(I32),
                 x_scales[:, 4 * q : 4 * q + 4, :].bitcast(I32),
             )
-        load_weight("w2", w2, 0, 0, 1)
+        load_weight("w2", w2, 0)
         x_table.append(load_words(1))
-        load_weight("w2", w2, 1, 0, 1)
+        load_weight("w2", w2, 1)
         pos1_t = load_list("pos1_t", pos1)
         pos2_t = load_list("pos2_t", pos2)
-        for z in range(PASSES):
-            load_weight("w2", w2, z, 1, 1, (None, 62)[z])
-        for name, w, first, slot in (("w2", w2, 2, 0), ("w1", w1, 0, 24), ("w1", w1, 2, 46)):
-            load_weight(name, w, 0, first, 2)
-            load_weight(name, w, 1, first, 2, slot)
+        load_weight("w1", w1, 0)
+        load_weight("w1", w1, 1, LAST_RAW)
         cen_t = load_list("cen_t", cen)
-        w3_raw = keep.tile([P, PACK, N], F32, name="w3_raw", tag="w3_raw", align_bytes=64)
-        nc.sync.dma_start(w3_raw[:], w3.rearrange("(p j) n -> p j n", j=PACK))
+        w3_raw = buffer("w3_raw", [P, PACK, N], F32)
+        w3_rows = w3.rearrange("(a t b) n -> t a b n", t=TILES, b=RUN)
+        for t in range(TILES):
+            nc.sync.dma_start(w3_raw[:, t, :], w3_rows[t])
 
-        def stage(name, width, tag=None):
-            return keep.tile([P, width], BF16, name=f"{name}_bf", tag=tag or f"{name}_bf", align_bytes=64)
-
-        def cast(engine, grouped, src):
+        def cast(engine, stage, slot, name, z, t):
+            dst = stage[:, slot * K_PASS : (slot + 1) * K_PASS]
+            src = raw[name, z][:].rearrange("p j (a t i) -> p t a j i", t=TILES, i=RUN)[:, t]
             if engine == "gpsimd":
                 nc.gpsimd.tensor_scalar(
-                    grouped.rearrange("p (c j) -> p c j", j=PACK),
-                    src.rearrange("p j c -> p c j"),
+                    dst.rearrange("p (a i j) -> p a i j", i=RUN, j=PACK),
+                    src.rearrange("p a j i -> p a i j"),
                     1.0,
                     0.0,
                     ALU.mult,
                     ALU.add,
                 )
             else:
-                dst = grouped.rearrange("p (a i j) -> p a j i", i=4, j=PACK)
-                view = src.rearrange("p j (a i) -> p a j i", i=4)
-                if engine == "vector":
-                    nc.vector.tensor_copy(dst, view)
-                else:
-                    nc.scalar.activation(dst, view, ACT.Copy)
+                nc.scalar.activation(dst.rearrange("p (a i j) -> p a j i", i=RUN, j=PACK), src, ACT.Copy)
 
-        def quantize(name, grouped, tag=None, scale_tag=None):
-            width = grouped.shape[1] // PACK
-            codes = buffer(f"{name}_code", width, tag, U32)
-            scales = keep.tile([P, width], U8, name=f"{name}_scale", tag=scale_tag or f"{name}_scale", align_bytes=64)
-            nc.vector.quantize_mx(out=codes[:].bitcast(FP8X4), scales=scales[:], in_=grouped[:])
+        def quantize(name, stage, at=None, tag=None, scale_tag=None):
+            width = stage.shape[1] // PACK
+            codes = buffer(f"{name}_code", [P, width], U32, at, tag)
+            scales = buffer(f"{name}_scale", [P, width], U8, tag=scale_tag)
+            nc.vector.quantize_mx(out=codes[:].bitcast(FP8X4), scales=scales[:], in_=stage[:])
             return codes, scales
 
-        def open_banks(k):
-            return [
-                psum.tile([P, BANK], F32, name=f"acc{k}{h}", tag=f"bank{TILE_BANKS[k] + h}")
-                for h in range(HALVES)
-            ]
+        quantized = {}
+
+        def quantize_units(label, stage, name, units, tag=None, scale_tag=None):
+            codes, scales = quantize(label, stage, None, tag, scale_tag)
+            for slot, (z, t) in enumerate(units):
+                cols = slice(slot * P, (slot + 1) * P)
+                quantized[name, z, t] = (codes[:, cols], scales[:, cols])
 
         x_code = {}
 
-        def pick_words(z, h, tag=None):
-            picked = keep.tile([P, BANK], U32, name=f"x_code{z}{h}", tag=tag or f"x_code{z}{h}", align_bytes=64)
-            cols = slice(h * BANK // LIST_ROWS, (h + 1) * BANK // LIST_ROWS)
-            nc.vector.tensor_copy(picked[:], x_table[z][:].indirect(offs_t[:, cols]))
-            x_code[z, h] = picked
+        def pick_words(z, tag=None):
+            x_code[z] = buffer(f"x_code{z}", [P, S], U32, tag=tag)
+            nc.vector.tensor_copy(x_code[z][:], x_table[z][:].indirect(offs_t[:]))
 
-        def multiply(banks, wq, z, halves=range(HALVES), s=0):
-            codes, scales = wq
-            stat = slice(s * P, (s + 1) * P)
-            for h in halves:
+        banks = {}
+
+        def multiply(name, z, t):
+            codes, scales = quantized[name, z, t]
+            if z == 0:
+                banks[name, t] = [
+                    psum.tile([P, BANK], F32, name=f"{name}_acc{t}{h}", tag=f"bank{FIRST_BANK[name][t] + h}")
+                    for h in range(HALVES)
+                ]
+            for h in range(HALVES):
+                cols = slice(h * BANK, (h + 1) * BANK)
                 nc.tensor.matmul_mx(
-                    out=banks[h][:],
-                    lhsT=codes[:, stat].bitcast(FP8X4),
-                    lhsT_scale=scales[:, stat],
-                    rhs=x_code[z, h][:].bitcast(FP8X4),
-                    rhs_scale=x_scale[4 * z : P, h * BANK : (h + 1) * BANK],
+                    out=banks[name, t][h][:],
+                    lhsT=codes.bitcast(FP8X4),
+                    lhsT_scale=scales,
+                    rhs=x_code[z][:, cols].bitcast(FP8X4),
+                    rhs_scale=x_scale[4 * z : P, cols],
                     start=(z == 0),
                     stop=(z == PASSES - 1),
                 )
 
-        def evacuate(name, banks, tag):
-            rows = buffer(name, S, tag)
+        rows = {}
+
+        def empty(name, t, first="scalar"):
+            rows[name, t] = buffer(f"{name}_rows{t}", [P, S], F32)
             for h in range(HALVES):
-                nc.scalar.activation(rows[:, h * BANK : (h + 1) * BANK], banks[h][:], ACT.Copy)
-            return rows
+                dst = rows[name, t][:, h * BANK : (h + 1) * BANK]
+                if h == 0 and first == "vector":
+                    nc.vector.tensor_copy(dst, banks[name, t][h][:])
+                else:
+                    nc.scalar.activation(dst, banks[name, t][h][:], ACT.Copy)
 
-        def buffer(name, width, tag, dtype=F32):
-            if isinstance(tag, int):
-                return place(name, width, dtype, tag)
-            return keep.tile([P, width], dtype, name=name, tag=tag or name, align_bytes=64)
-
-        def fetch(name, rows, lst, tag=None):
-            got = buffer(name, lst.shape[1] * LIST_ROWS, tag)
-            nc.vector.tensor_copy(got[:], rows[:].indirect(lst))
-            return got
-
-        last = {}
-
-        def add_turned(values, u, b, start=False, stop=False):
-            if (u, b) == (TILES - 1, BLOCKS - 1):
-                start = not last
-                if start:
-                    last["edge"] = psum.tile([P, P], F32, name="edge_last", tag="bank3")
-                dst = last["edge"][:]
+        def fetch(engine, dst, t, lst):
+            window = rows["w2", t][:].indirect(lst[:])
+            if engine == "vector":
+                nc.vector.tensor_copy(dst, window)
             else:
-                dst = edge[b][:, u * P : (u + 1) * P]
-            nc.tensor.matmul(
-                dst,
-                lhsT=values,
-                rhs=identity[:],
-                start=start,
-                stop=stop,
-                is_transpose=True,
-            )
+                nc.scalar.activation(dst, window, ACT.Copy)
 
-        def add_turned_all(values, u, start=False):
-            for b in range(BLOCKS):
-                add_turned(values[:, b * P : (b + 1) * P], u, b, start=start)
-
-        first, second, gap, rows, banks, pair_codes = {}, {}, {}, {}, {}, {}
-
-        def place(name, width, dtype, slot):
-            return lane.tile([P, width], dtype, name=name, offset=slot * SLOT, align_bytes=64)
-
-        def cast_group(name, start, slots):
-            grouped = []
-            for z, engine in enumerate(("gpsimd", "scalar")):
-                grouped.append(place(f"{name}_{start}{z}_bf", 2 * K_PASS, BF16, slots[z]))
-                cast(engine, grouped[z][:], raw[name, start, z][:])
-            return grouped
-
-        def products(k, grouped, slots, scale_tags=(None, None)):
-            pair_codes[k] = [quantize(f"k{k}p{z}", grouped[z], slots[z], scale_tags[z]) for z in range(PASSES)]
-            product(k)
-
-        def product(k):
-            banks[k] = open_banks(k)
-            for h in range(HALVES):
-                for z in range(PASSES):
-                    multiply(banks[k], pair_codes[k - k % 2][z], z, (h,), s=k % 2)
-
-        def empty(k, tag=None):
-            rows[k] = evacuate(f"rows{k}", banks[k], tag)
-
-        def fetch_second(u, tag=None):
-            second[u] = fetch(f"second{u}", rows[u], pos2_t[:], tag)
-            add_turned_all(second[u], u, start=(u == 0))
-
-        def add_lift(u, tag, a=0, b=V):
-            lift = buffer(f"lift{u}{a}", b - a, tag)
-            src = gap[u, a][:] if (u, a) in gap and gap[u, a].shape[1] == b - a else gap[u, 0][:, a:b]
-            nc.scalar.activation(lift[:], src, ACT.Relu)
-            for v in range(a, b, P):
-                add_turned(lift[:, v - a : v - a + P], u, v // P)
-
-        def head_weights(k):
-            grouped = place(f"k{k}_bf", PASSES * K_PASS, BF16, 16)
-            for z in range(PASSES):
-                cast("scalar", grouped[:, z * K_PASS : (z + 1) * K_PASS], raw["w2", k, z][:])
-            return quantize(f"k{k}", grouped)
-
-        def head_pass(z):
-            grouped = stage(f"k0p{z}", K_PASS)
-            cast("scalar", grouped[:], raw["w2", 0, z][:])
-            return quantize(f"k0p{z}", grouped)
-
-        def head_product(wq, z, piece):
-            a, b, bank = HEAD_PIECES[piece]
-            h = a // BANK
-            nc.tensor.matmul_mx(
-                out=head_banks[piece][:],
-                lhsT=wq[0][:].bitcast(FP8X4),
-                lhsT_scale=wq[1][:],
-                rhs=x_code[z, h][:, a - h * BANK : b - h * BANK].bitcast(FP8X4),
-                rhs_scale=x_scale[4 * z : P, a:b],
-                start=(z == 0),
-                stop=(z == PASSES - 1),
-            )
-
-        for h in range(HALVES):
-            pick_words(0, h)
-        x_scale = keep.tile([P, S], U8, name="x_scale", align_bytes=64)
+        pick_words(0)
+        x_scale = buffer("x_scale", [P, S], U8)
         nc.vector.tensor_copy(x_scale[:], scale_table[:].indirect(offs_t[:]))
-        head_banks = [
-            psum.tile([P, b - a], F32, name=f"head{a}", tag=f"bank{bank}") for a, b, bank in HEAD_PIECES
-        ]
-        wq = head_pass(0)
-        for piece in range(len(HEAD_PIECES)):
-            head_product(wq, 0, piece)
-        pick_words(1, 0)
-        wq = head_pass(1)
-        head_product(wq, 1, 0)
-        x_code[1, 1] = keep.tile([P, BANK], U32, name="x_code11", tag="w2_raw10", align_bytes=64)
-        for piece in range(1, len(HEAD_PIECES)):
-            a, b, bank = HEAD_PIECES[piece]
-            nc.vector.tensor_copy(
-                x_code[1, 1][:, a - BANK : b - BANK],
-                x_table[1][:].indirect(offs_t[:, a // LIST_ROWS : b // LIST_ROWS]),
-            )
-            head_product(wq, 1, piece)
-        wq = head_weights(1)
-        rows[0] = place("rows0", S, F32, 62)
-        for piece, (a, b, bank) in enumerate(HEAD_PIECES):
-            nc.scalar.activation(rows[0][:, a:b], head_banks[piece][:], ACT.Copy)
-        banks[1] = open_banks(1)
-        for h in range(HALVES):
+        early = buffer("early_bf", [P, 3 * K_PASS], BF16)
+        for t in range(3):
+            cast("scalar", early, t, "w2", 0, t)
+        quantize_units("early", early, "w2", [(0, t) for t in range(3)])
+        for t in range(3):
+            multiply("w2", 0, t)
+        mixed = buffer("mixed_bf", [P, 3 * K_PASS], BF16)
+        cast("scalar", mixed, 0, "w2", 0, 3)
+        pick_words(1, "w2_raw0")
+        lead = buffer("lead_bf", [P, K_PASS], BF16)
+        cast("scalar", lead, 0, "w2", 1, 0)
+        quantize_units("lead", lead, "w2", [(1, 0)])
+        multiply("w2", 1, 0)
+        cast("gpsimd", mixed, 1, "w2", 1, 3)
+        cast("scalar", mixed, 2, "w2", 1, 1)
+        quantize_units("mixed", mixed, "w2", [(0, 3), (1, 3), (1, 1)])
+        third = buffer("third_bf", [P, K_PASS], BF16)
+        cast("scalar", third, 0, "w2", 1, 2)
+        empty("w2", 0, "vector")
+        quantize_units("third", third, "w2", [(1, 2)])
+        multiply("w2", 1, 1)
+        multiply("w2", 1, 2)
+        multiply("w2", 0, 3)
+        multiply("w2", 1, 3)
+
+        near = buffer("near", [P, TILES, V], F32)
+        far_first = buffer("far_first", [P, V], F32)
+        fetch("vector", near[:, 0, :], 0, pos1_t)
+        fetch("vector", far_first[:], 0, pos2_t)
+        for t in range(1, TILES):
+            empty("w2", t)
+        fetch("vector", near[:, 1, :], 1, pos1_t)
+
+        pair_units = [(0, 0), (0, 1), (1, 0), (1, 1)]
+        pair = buffer("pair_bf", [P, 4 * K_PASS], BF16, PAIR_STAGE)
+        single = buffer("single_bf", [P, K_PASS], BF16)
+        cast("gpsimd", pair, 0, "w1", 0, 0)
+        cast("gpsimd", pair, 1, "w1", 0, 1)
+        cast("gpsimd", single, 0, "w1", 0, 2)
+        cast("gpsimd", pair, 2, "w1", 1, 0)
+        cast("gpsimd", pair, 3, "w1", 1, 1)
+        quantize_units("pair", pair, "w1", pair_units, tag="mixed_code")
+        quantize_units("single", single, "w1", [(0, 2)], scale_tag="mixed_scale")
+        for t in range(2):
             for z in range(PASSES):
-                multiply(banks[1], wq, z, (h,), s=z)
-        edge = [psum.tile([P, H], F32, name=f"edge{b}", tag=f"bank{4 + b}") for b in range(BLOCKS)]
+                multiply("w1", z, t)
+        rest_units = [(0, 3), (1, 2), (1, 3)]
+        rest = buffer("rest_bf", [P, 3 * K_PASS], BF16, PAIR_STAGE)
+        for slot, (z, t) in enumerate(rest_units):
+            cast("gpsimd", rest, slot, "w1", z, t)
+        far_rest = buffer("far_rest", [P, TILES - 1, V], F32, FAR_REST)
+        fetch("vector", far_rest[:, 0, :], 1, pos2_t)
+        fetch("vector", far_rest[:, 1, :], 2, pos2_t)
+        fetch("scalar", near[:, 2, :], 2, pos1_t)
+        fetch("scalar", near[:, 3, :], 3, pos1_t)
+        fetch("scalar", far_rest[:, 2, :], 3, pos2_t)
+        quantize_units("rest", rest, "w1", rest_units)
+        for t in range(2, TILES):
+            for z in range(PASSES):
+                multiply("w1", z, t)
+        for t in range(TILES):
+            empty("w1", t)
 
-        def gather_first(u, tag=None):
-            first[u] = fetch(f"first{u}", rows[u], pos1_t[:], tag)
-
-        def fetch_gap(u, tag):
-            gap[u, 0] = buffer(f"gap{u}0", V, tag)
-            nc.vector.tensor_tensor(gap[u, 0][:], rows[u][:].indirect(pos1_t[:]), second[u][:], ALU.subtract)
-
-        def subtract(u, tag, a=0, b=V):
-            part = buffer(f"gap{u}{a}", b - a, tag)
-            nc.gpsimd.tensor_tensor(part[:], first[u][:, a:b], second[u][:, a:b], ALU.subtract)
-            gap[u, a] = part
-
-        grouped = cast_group("w2", 2, (16, 20))
-        fetch_second(0)
-        products(2, grouped, (0, 40))
-        empty(1, 7)
-        fetch_gap(0, 16)
-        grouped = cast_group("w1", 0, (62, 32))
-        second[1] = fetch("second1", rows[1], pos2_t[:])
-        gather_first(1)
-        empty(2)
-        product(3)
-        empty(3, 54)
-        products(4, grouped, (24, None))
-        product(5)
-        grouped = cast_group("w1", 2, (32, 40))
-        second[2] = fetch("second2", rows[2], pos2_t[:], 62)
-        gather_first(2)
-        empty(4)
-        empty(5)
-        products(6, grouped, (46, None))
-        product(7)
         half = V // 2
-        subtract(1, 38)
-        subtract(2, 42, 0, half)
-        add_lift(0, 24)
-        add_turned_all(second[1], 1)
-        add_turned_all(second[2], 2)
-        empty(6)
-        empty(7)
-        fetch_second(3, 29)
-        w3_bf = place("w3_bf", N * PACK, BF16, 62)
+        best = []
+        for part, at in enumerate((BEST_FIRST, BEST_REST)):
+            cols = slice(part * half, (part + 1) * half)
+            best.append(buffer(f"best{part}", [P, TILES, half], F32, at))
+            nc.vector.tensor_tensor(best[part][:, 0, :], near[:, 0, cols], far_first[:, cols], ALU.max)
+            nc.vector.tensor_tensor(best[part][:, 1:, :], near[:, 1:, cols], far_rest[:, :, cols], ALU.max)
+        w3_bf = buffer("w3_bf", [P, N * PACK], BF16, tag="near")
+        nc.scalar.activation(
+            w3_bf[:].rearrange("p (a i j) -> p a j i", i=RUN, j=PACK),
+            w3_raw[:].rearrange("p j (a i) -> p a j i", i=RUN),
+            ACT.Copy,
+        )
 
         out_view = out.rearrange("(u p) v -> p u v", p=P)
-        z_bf = {}
+        sums, z_bf = {}, {}
 
-        def fetch_centre(c, u, tag, stop=False):
-            first_block, count = GROUPS[c]
-            centres = cen_t[:, first_block * P // LIST_ROWS : (first_block + count) * P // LIST_ROWS]
-            got = fetch(f"centre{c}{u}", rows[TILES + u], centres, tag)
-            for b in range(count):
-                add_turned(got[:, b * P : (b + 1) * P], u, first_block + b, stop=stop)
-
-        turned = {}
-
-        def turn_back(c):
-            first_block, count = GROUPS[c]
-            turned[c] = psum.tile([P, count, 2, P], F32, name=f"turned{c}", tag=f"bank{(0, 4, 5)[c]}")
-            for b in range(count):
-                z_rows = keep.tile([P, H], BF16, name=f"z_rows{first_block + b}")
-                dst = z_rows[:].rearrange("v (g p e) -> v g p e", g=2, e=2)
-                parts = [(dst, edge[first_block + b][:])]
-                if first_block + b == BLOCKS - 1:
-                    cut = (TILES - 1) * P
-                    parts = [
-                        (dst[:, :, : cut // PACK, :], edge[BLOCKS - 1][:, :cut]),
-                        (dst[:, :, cut // PACK :, :], last["edge"][:]),
-                    ]
-                for n, (part, sums) in enumerate(parts):
-                    view = sums.rearrange("v (p g e) -> v g p e", g=2, e=2)
-                    if n == 0:
-                        nc.scalar.activation(part, view, ACT.Relu)
-                    else:
-                        nc.vector.tensor_scalar_max(part, view, 0.0)
-                words = z_rows[:].bitcast(F32)
-                for g in range(2):
-                    nc.tensor.transpose(turned[c][:, b, g, :], words[:, g * P : (g + 1) * P], identity[:])
-
-        def weave(c, engine, tag=None):
-            count = GROUPS[c][1]
-            z_bf[c] = buffer(f"z_bf{c}", count * P * PACK, tag, BF16)
-            dst = z_bf[c][:].bitcast(F32).rearrange("p (b v g) -> p b v g", b=count, g=2)
-            src = turned[c][:].rearrange("p b g v -> p b v g")
-            if engine == "vector":
-                nc.vector.tensor_copy(dst, src)
+        def add_centres(c):
+            a, b = CHUNKS[c]
+            if c == 1:
+                sums[c] = buffer("sums1", [P, TILES, b - a], F32, BEST_FIRST)
             else:
-                nc.scalar.copy(dst, src)
+                sums[c] = buffer(f"sums{c}", [P, TILES, b - a], F32, tag="sums")
+            centres = cen_t[:, a // LIST_ROWS : b // LIST_ROWS]
+            for t in range(TILES):
+                nc.vector.tensor_tensor(
+                    sums[c][:, t, :],
+                    rows["w1", t][:].indirect(centres),
+                    best[a // half][:, t, a % half : a % half + b - a],
+                    ALU.add,
+                )
 
-        def pack(c):
-            return quantize(f"z{c}", z_bf[c])
+        def weave(c):
+            a, b = CHUNKS[c]
+            z_bf[c] = buffer(f"z_bf{c}", [P, (b - a) * PACK], BF16)
+            nc.scalar.activation(
+                z_bf[c][:].rearrange("p (a i t) -> p a t i", i=RUN, t=TILES),
+                sums[c][:].rearrange("p t (a i) -> p a t i", i=RUN),
+                ACT.Relu,
+            )
 
-        def project(c, zq):
-            first_block, count = GROUPS[c]
-            z_code, z_scale = zq
-            if c == len(GROUPS) - 1:
-                acc = [psum.tile([P, P], F32, name=f"out_acc{c}{u}", tag=f"bank{6 + u}")[:] for u in range(N // P)]
+        def project(c):
+            a, b = CHUNKS[c]
+            z_code, z_scale = quantize(f"z{c}", z_bf[c])
+            last = c == len(CHUNKS) - 1
+            if last:
+                acc = [psum.tile([P, b - a], F32, name=f"out_acc{c}{u}", tag=f"bank{OUT_BANK[c] + u}")[:] for u in range(N // P)]
             else:
-                both = psum.tile([P, N // P, count * P], F32, name=f"out_acc{c}", tag=f"bank{(2, 1)[c]}")
+                both = psum.tile([P, N // P, b - a], F32, name=f"out_acc{c}", tag=f"bank{OUT_BANK[c]}")
                 acc = [both[:, u, :] for u in range(N // P)]
             for u in range(N // P):
                 cols = slice(u * P, (u + 1) * P)
@@ -386,38 +292,21 @@ def tile_picked_edgecv_relu_p_kernel(
                     start=True,
                     stop=True,
                 )
-            result = keep.tile([P, N // P, count * P], F32, name=f"result{c}")
-            if c < len(GROUPS) - 1:
-                nc.scalar.activation(result[:], both[:], ACT.Copy)
-            else:
+            result = buffer(f"result{c}", [P, N // P, b - a], F32)
+            if last:
                 nc.scalar.activation(result[:, 0, :], acc[0], ACT.Copy)
                 nc.vector.tensor_copy(result[:, 1, :], acc[1])
-            nc.sync.dma_start(out_view[:, :, first_block * P : (first_block + count) * P], result[:])
+            else:
+                nc.scalar.activation(result[:], both[:], ACT.Copy)
+            nc.sync.dma_start(out_view[:, :, a:b], result[:])
 
-        fetch_centre(0, 0, 33)
-        fetch_centre(0, 1, 35)
-        fetch_gap(3, 16)
-        subtract(2, 54, half, V)
-        cast("gpsimd", w3_bf[:], w3_raw[:])
-        add_lift(1, "k6p1_code")
-        add_lift(2, 46, 0, half)
-        add_lift(3, None, 0, half)
-        fetch_centre(0, 2, "piece0")
-        fetch_centre(0, 3, "piece1", stop=True)
-        add_lift(3, 38, half, V)
-        add_lift(2, 42, half, V)
-        for u in range(TILES):
-            fetch_centre(1, u, (46, 47, "lift30", "piece2")[u], stop=(u == TILES - 1))
-        turn_back(0)
-        for u in range(TILES):
-            fetch_centre(2, u, (38, 39, 42, 43)[u], stop=(u >= TILES - 2))
-        turn_back(1)
-        weave(0, "scalar")
-        turn_back(2)
-        w3_code, w3_scale = quantize("w3", w3_bf, "rows6")
-        weave(1, "scalar")
-        project(0, pack(0))
-        weave(2, "vector")
-        quantized = [pack(1), pack(2)]
-        project(1, quantized[0])
-        project(2, quantized[1])
+        add_centres(0)
+        weave(0)
+        add_centres(1)
+        w3_code, w3_scale = quantize("w3", w3_bf)
+        weave(1)
+        project(0)
+        add_centres(2)
+        weave(2)
+        project(1)
+        project(2)

@@ -24,14 +24,13 @@ HALVES = S // BANK
 LIST_ROWS = 16
 TILES = H // P
 RUN = 4
-CHUNKS = ((0, 256), (256, 384), (384, 512))
+CHUNK = 128
 
 FIRST_BANK = {"w2": (0, 2, 4, 2), "w1": (6, 0, 4, 2)}
-OUT_BANK = (6, 7, 0)
+OUT_BANK = (6, 7, 0, 1, 4)
 
-BEST_FIRST, BEST_REST = 2048, 6144
-LAST_RAW = 2048
-PAIR_STAGE, FAR_REST = 10816, 13888
+W3_STAGE, PAIR_STAGE, BEST = 0, 1984, 6016
+REST_STAGE, MIXED_CODES, PAIR_CODES = 14208, 17216, 17280
 
 
 def tile_picked_edgecv_relu_p_kernel(
@@ -70,8 +69,8 @@ def tile_picked_edgecv_relu_p_kernel(
         scale_table = keep.tile([P, T], U8, name="scale_table")
         nc.vector.memset(scale_table[:].bitcast(I32), 0)
 
-        offs_t = load_list("offs_t", offs)
         x_table = [load_words(0)]
+        offs_t = load_list("offs_t", offs)
         for q in range(4):
             nc.sync.dma_start(
                 scale_table[32 * q : 32 * q + 4 * PASSES, :].bitcast(I32),
@@ -83,7 +82,7 @@ def tile_picked_edgecv_relu_p_kernel(
         pos1_t = load_list("pos1_t", pos1)
         pos2_t = load_list("pos2_t", pos2)
         load_weight("w1", w1, 0)
-        load_weight("w1", w1, 1, LAST_RAW)
+        load_weight("w1", w1, 1)
         cen_t = load_list("cen_t", cen)
         w3_raw = buffer("w3_raw", [P, PACK, N], F32)
         w3_rows = w3.rearrange("(a t b) n -> t a b n", t=TILES, b=RUN)
@@ -102,6 +101,8 @@ def tile_picked_edgecv_relu_p_kernel(
                     ALU.mult,
                     ALU.add,
                 )
+            elif engine == "vector":
+                nc.vector.tensor_copy(dst.rearrange("p (a i j) -> p a j i", i=RUN, j=PACK), src)
             else:
                 nc.scalar.activation(dst.rearrange("p (a i j) -> p a j i", i=RUN, j=PACK), src, ACT.Copy)
 
@@ -114,8 +115,8 @@ def tile_picked_edgecv_relu_p_kernel(
 
         quantized = {}
 
-        def quantize_units(label, stage, name, units, tag=None, scale_tag=None):
-            codes, scales = quantize(label, stage, None, tag, scale_tag)
+        def quantize_units(label, stage, name, units, at=None, scale_tag=None):
+            codes, scales = quantize(label, stage, at, None, scale_tag)
             for slot, (z, t) in enumerate(units):
                 cols = slice(slot * P, (slot + 1) * P)
                 quantized[name, z, t] = (codes[:, cols], scales[:, cols])
@@ -179,11 +180,11 @@ def tile_picked_edgecv_relu_p_kernel(
         pick_words(1, "w2_raw0")
         lead = buffer("lead_bf", [P, K_PASS], BF16)
         cast("scalar", lead, 0, "w2", 1, 0)
+        cast("vector", mixed, 1, "w2", 1, 3)
         quantize_units("lead", lead, "w2", [(1, 0)])
         multiply("w2", 1, 0)
-        cast("gpsimd", mixed, 1, "w2", 1, 3)
         cast("scalar", mixed, 2, "w2", 1, 1)
-        quantize_units("mixed", mixed, "w2", [(0, 3), (1, 3), (1, 1)])
+        quantize_units("mixed", mixed, "w2", [(0, 3), (1, 3), (1, 1)], at=MIXED_CODES)
         third = buffer("third_bf", [P, K_PASS], BF16)
         cast("scalar", third, 0, "w2", 1, 2)
         empty("w2", 0, "vector")
@@ -194,14 +195,14 @@ def tile_picked_edgecv_relu_p_kernel(
         multiply("w2", 1, 3)
 
         near = buffer("near", [P, TILES, V], F32)
-        far_first = buffer("far_first", [P, V], F32)
-        fetch("vector", near[:, 0, :], 0, pos1_t)
-        fetch("vector", far_first[:], 0, pos2_t)
+        far = buffer("far", [P, TILES, V], F32)
         for t in range(1, TILES):
             empty("w2", t)
-        fetch("vector", near[:, 1, :], 1, pos1_t)
+        for t in range(TILES):
+            engine = "vector" if t < 2 else "scalar"
+            fetch(engine, near[:, t, :], t, pos1_t)
+            fetch(engine, far[:, t, :], t, pos2_t)
 
-        pair_units = [(0, 0), (0, 1), (1, 0), (1, 1)]
         pair = buffer("pair_bf", [P, 4 * K_PASS], BF16, PAIR_STAGE)
         single = buffer("single_bf", [P, K_PASS], BF16)
         cast("gpsimd", pair, 0, "w1", 0, 0)
@@ -209,77 +210,54 @@ def tile_picked_edgecv_relu_p_kernel(
         cast("gpsimd", single, 0, "w1", 0, 2)
         cast("gpsimd", pair, 2, "w1", 1, 0)
         cast("gpsimd", pair, 3, "w1", 1, 1)
-        quantize_units("pair", pair, "w1", pair_units, tag="mixed_code")
+        rest = buffer("rest_bf", [P, 3 * K_PASS], BF16, REST_STAGE)
+        cast("vector", rest, 0, "w1", 0, 3)
+        nc.vector.tensor_copy(
+            rest[:, K_PASS:].rearrange("p (t a i j) -> p t a j i", t=2, i=RUN, j=PACK),
+            raw["w1", 1][:].rearrange("p j (a t i) -> p t a j i", t=TILES, i=RUN)[:, 2:],
+        )
+        quantize_units("pair", pair, "w1", [(0, 0), (0, 1), (1, 0), (1, 1)], at=PAIR_CODES)
         quantize_units("single", single, "w1", [(0, 2)], scale_tag="mixed_scale")
-        for t in range(2):
-            for z in range(PASSES):
-                multiply("w1", z, t)
-        rest_units = [(0, 3), (1, 2), (1, 3)]
-        rest = buffer("rest_bf", [P, 3 * K_PASS], BF16, PAIR_STAGE)
-        for slot, (z, t) in enumerate(rest_units):
-            cast("gpsimd", rest, slot, "w1", z, t)
-        far_rest = buffer("far_rest", [P, TILES - 1, V], F32, FAR_REST)
-        fetch("vector", far_rest[:, 0, :], 1, pos2_t)
-        fetch("vector", far_rest[:, 1, :], 2, pos2_t)
-        fetch("scalar", near[:, 2, :], 2, pos1_t)
-        fetch("scalar", near[:, 3, :], 3, pos1_t)
-        fetch("scalar", far_rest[:, 2, :], 3, pos2_t)
-        quantize_units("rest", rest, "w1", rest_units)
-        for t in range(2, TILES):
-            for z in range(PASSES):
-                multiply("w1", z, t)
+        quantize_units("rest", rest, "w1", [(0, 3), (1, 2), (1, 3)])
         for t in range(TILES):
+            for z in range(PASSES):
+                multiply("w1", z, t)
             empty("w1", t)
 
-        half = V // 2
-        best = []
-        for part, at in enumerate((BEST_FIRST, BEST_REST)):
-            cols = slice(part * half, (part + 1) * half)
-            best.append(buffer(f"best{part}", [P, TILES, half], F32, at))
-            nc.vector.tensor_tensor(best[part][:, 0, :], near[:, 0, cols], far_first[:, cols], ALU.max)
-            nc.vector.tensor_tensor(best[part][:, 1:, :], near[:, 1:, cols], far_rest[:, :, cols], ALU.max)
-        w3_bf = buffer("w3_bf", [P, N * PACK], BF16, tag="near")
-        nc.scalar.activation(
+        w3_bf = buffer("w3_bf", [P, N * PACK], BF16, W3_STAGE)
+        nc.vector.tensor_copy(
             w3_bf[:].rearrange("p (a i j) -> p a j i", i=RUN, j=PACK),
             w3_raw[:].rearrange("p j (a i) -> p a j i", i=RUN),
-            ACT.Copy,
         )
+        best = buffer("best", [P, TILES, V], F32, BEST)
+        nc.vector.tensor_tensor(best[:, :2, :], near[:, :2, :], far[:, :2, :], ALU.max)
+        w3_code, w3_scale = quantize("w3", w3_bf)
+        nc.vector.tensor_tensor(best[:, 2:, :], near[:, 2:, :], far[:, 2:, :], ALU.max)
+
+        sums = buffer("sums", [P, TILES, V], F32)
+
+        def add_centres(t, a, b):
+            centres = cen_t[:, a // LIST_ROWS : b // LIST_ROWS]
+            nc.vector.tensor_tensor(sums[:, t, a:b], rows["w1", t][:].indirect(centres), best[:, t, a:b], ALU.add)
 
         out_view = out.rearrange("(u p) v -> p u v", p=P)
-        sums, z_bf = {}, {}
+        z_bf = {}
 
-        def add_centres(c):
-            a, b = CHUNKS[c]
-            if c == 1:
-                sums[c] = buffer("sums1", [P, TILES, b - a], F32, BEST_FIRST)
+        def weave(c, engine):
+            z_bf[c] = buffer(f"z_bf{c}", [P, CHUNK * PACK], BF16)
+            dst = z_bf[c][:].rearrange("p (a i t) -> p a t i", i=RUN, t=TILES)
+            src = sums[:, :, c * CHUNK : (c + 1) * CHUNK].rearrange("p t (a i) -> p a t i", i=RUN)
+            if engine == "vector":
+                nc.vector.tensor_scalar_max(dst, src, 0.0)
             else:
-                sums[c] = buffer(f"sums{c}", [P, TILES, b - a], F32, tag="sums")
-            centres = cen_t[:, a // LIST_ROWS : b // LIST_ROWS]
-            for t in range(TILES):
-                nc.vector.tensor_tensor(
-                    sums[c][:, t, :],
-                    rows["w1", t][:].indirect(centres),
-                    best[a // half][:, t, a % half : a % half + b - a],
-                    ALU.add,
-                )
+                nc.scalar.activation(dst, src, ACT.Relu)
 
-        def weave(c):
-            a, b = CHUNKS[c]
-            z_bf[c] = buffer(f"z_bf{c}", [P, (b - a) * PACK], BF16)
-            nc.scalar.activation(
-                z_bf[c][:].rearrange("p (a i t) -> p a t i", i=RUN, t=TILES),
-                sums[c][:].rearrange("p t (a i) -> p a t i", i=RUN),
-                ACT.Relu,
-            )
-
-        def project(c):
-            a, b = CHUNKS[c]
+        def project(c, engines):
             z_code, z_scale = quantize(f"z{c}", z_bf[c])
-            last = c == len(CHUNKS) - 1
-            if last:
-                acc = [psum.tile([P, b - a], F32, name=f"out_acc{c}{u}", tag=f"bank{OUT_BANK[c] + u}")[:] for u in range(N // P)]
+            if len(engines) > 1:
+                acc = [psum.tile([P, CHUNK], F32, name=f"out_acc{c}{u}", tag=f"bank{OUT_BANK[c + u]}")[:] for u in range(N // P)]
             else:
-                both = psum.tile([P, N // P, b - a], F32, name=f"out_acc{c}", tag=f"bank{OUT_BANK[c]}")
+                both = psum.tile([P, N // P, CHUNK], F32, name=f"out_acc{c}", tag=f"bank{OUT_BANK[c]}")
                 acc = [both[:, u, :] for u in range(N // P)]
             for u in range(N // P):
                 cols = slice(u * P, (u + 1) * P)
@@ -292,21 +270,20 @@ def tile_picked_edgecv_relu_p_kernel(
                     start=True,
                     stop=True,
                 )
-            result = buffer(f"result{c}", [P, N // P, b - a], F32)
-            if last:
-                nc.scalar.activation(result[:, 0, :], acc[0], ACT.Copy)
-                nc.vector.tensor_copy(result[:, 1, :], acc[1])
-            else:
-                nc.scalar.activation(result[:], both[:], ACT.Copy)
-            nc.sync.dma_start(out_view[:, :, a:b], result[:])
+            result = buffer(f"result{c}", [P, N // P, CHUNK], F32)
+            parts = [(result[:, u, :], acc[u]) for u in range(N // P)] if len(engines) > 1 else [(result[:], both[:])]
+            for engine, (dst, src) in zip(engines, parts):
+                if engine == "vector":
+                    nc.vector.tensor_copy(dst, src)
+                else:
+                    nc.scalar.activation(dst, src, ACT.Copy)
+            nc.sync.dma_start(out_view[:, :, c * CHUNK : (c + 1) * CHUNK], result[:])
 
-        add_centres(0)
-        weave(0)
-        add_centres(1)
-        w3_code, w3_scale = quantize("w3", w3_bf)
-        weave(1)
-        project(0)
-        add_centres(2)
-        weave(2)
-        project(1)
-        project(2)
+        for t in range(TILES - 1):
+            add_centres(t, 0, V)
+        for c in range(V // CHUNK):
+            add_centres(TILES - 1, c * CHUNK, (c + 1) * CHUNK)
+        for c, engine in enumerate(("scalar", "scalar", "vector", "scalar")):
+            weave(c, engine)
+        for c, engines in enumerate((("scalar",), ("scalar",), ("vector",), ("scalar", "vector"))):
+            project(c, engines)

@@ -27,10 +27,11 @@ RUN = 4
 CHUNK = 128
 
 FIRST_BANK = {"w2": (0, 2, 4, 2), "w1": (6, 0, 4, 2)}
+LEAD_PIECES = ((0, 512, 0), (512, 768, 1), (768, 1024, 6))
 OUT_BANK = (6, 7, 0, 1, 4)
 
-W3_STAGE, PAIR_STAGE, BEST = 0, 1984, 6016
-REST_STAGE, MIXED_CODES, PAIR_CODES = 14208, 17216, 17280
+PAIR_STAGE, BEST = 0, 4032
+REST_STAGE, MIXED_CODES, PAIR_CODES = 15232, 17216, 17280
 
 
 def tile_picked_edgecv_relu_p_kernel(
@@ -129,17 +130,21 @@ def tile_picked_edgecv_relu_p_kernel(
 
         banks = {}
 
-        def multiply(name, z, t):
+        def pieces(name, t):
+            if (name, t) == ("w2", 0):
+                return LEAD_PIECES
+            return [(h * BANK, (h + 1) * BANK, FIRST_BANK[name][t] + h) for h in range(HALVES)]
+
+        def multiply(name, z, t, only=None):
             codes, scales = quantized[name, z, t]
-            if z == 0:
-                banks[name, t] = [
-                    psum.tile([P, BANK], F32, name=f"{name}_acc{t}{h}", tag=f"bank{FIRST_BANK[name][t] + h}")
-                    for h in range(HALVES)
-                ]
-            for h in range(HALVES):
-                cols = slice(h * BANK, (h + 1) * BANK)
+            for h, (a, b, bank) in enumerate(pieces(name, t)):
+                if only not in (None, h):
+                    continue
+                if z == 0:
+                    banks[name, t, h] = psum.tile([P, b - a], F32, name=f"{name}_acc{t}{h}", tag=f"bank{bank}")
+                cols = slice(a, b)
                 nc.tensor.matmul_mx(
-                    out=banks[name, t][h][:],
+                    out=banks[name, t, h][:],
                     lhsT=codes.bitcast(FP8X4),
                     lhsT_scale=scales,
                     rhs=x_code[z][:, cols].bitcast(FP8X4),
@@ -152,12 +157,12 @@ def tile_picked_edgecv_relu_p_kernel(
 
         def empty(name, t, first="scalar"):
             rows[name, t] = buffer(f"{name}_rows{t}", [P, S], F32)
-            for h in range(HALVES):
-                dst = rows[name, t][:, h * BANK : (h + 1) * BANK]
+            for h, (a, b, bank) in enumerate(pieces(name, t)):
+                dst = rows[name, t][:, a:b]
                 if h == 0 and first == "vector":
-                    nc.vector.tensor_copy(dst, banks[name, t][h][:])
+                    nc.vector.tensor_copy(dst, banks[name, t, h][:])
                 else:
-                    nc.scalar.activation(dst, banks[name, t][h][:], ACT.Copy)
+                    nc.scalar.activation(dst, banks[name, t, h][:], ACT.Copy)
 
         def fetch(engine, dst, t, lst):
             window = rows["w2", t][:].indirect(lst[:])
@@ -175,20 +180,20 @@ def tile_picked_edgecv_relu_p_kernel(
         quantize_units("early", early, "w2", [(0, t) for t in range(3)])
         for t in range(3):
             multiply("w2", 0, t)
-        mixed = buffer("mixed_bf", [P, 3 * K_PASS], BF16)
+        mixed = buffer("mixed_bf", [P, 2 * K_PASS], BF16)
         cast("scalar", mixed, 0, "w2", 0, 3)
         pick_words(1, "w2_raw0")
         lead = buffer("lead_bf", [P, K_PASS], BF16)
         cast("scalar", lead, 0, "w2", 1, 0)
-        cast("vector", mixed, 1, "w2", 1, 3)
         quantize_units("lead", lead, "w2", [(1, 0)])
         multiply("w2", 1, 0)
-        cast("scalar", mixed, 2, "w2", 1, 1)
-        quantize_units("mixed", mixed, "w2", [(0, 3), (1, 3), (1, 1)], at=MIXED_CODES)
-        third = buffer("third_bf", [P, K_PASS], BF16)
+        third = buffer("third_bf", [P, 2 * K_PASS], BF16, tag="lead_bf")
+        cast("vector", third, 1, "w2", 1, 3)
+        cast("scalar", mixed, 1, "w2", 1, 1)
+        quantize_units("mixed", mixed, "w2", [(0, 3), (1, 1)])
         cast("scalar", third, 0, "w2", 1, 2)
         empty("w2", 0, "vector")
-        quantize_units("third", third, "w2", [(1, 2)])
+        quantize_units("third", third, "w2", [(1, 2), (1, 3)], at=MIXED_CODES)
         multiply("w2", 1, 1)
         multiply("w2", 1, 2)
         multiply("w2", 0, 3)
@@ -204,53 +209,57 @@ def tile_picked_edgecv_relu_p_kernel(
             fetch(engine, far[:, t, :], t, pos2_t)
 
         pair = buffer("pair_bf", [P, 4 * K_PASS], BF16, PAIR_STAGE)
-        single = buffer("single_bf", [P, K_PASS], BF16)
+        single = buffer("single_bf", [P, 2 * K_PASS], BF16)
         cast("gpsimd", pair, 0, "w1", 0, 0)
         cast("gpsimd", pair, 1, "w1", 0, 1)
         cast("gpsimd", single, 0, "w1", 0, 2)
+        cast("gpsimd", single, 1, "w1", 0, 3)
         cast("gpsimd", pair, 2, "w1", 1, 0)
         cast("gpsimd", pair, 3, "w1", 1, 1)
-        rest = buffer("rest_bf", [P, 3 * K_PASS], BF16, REST_STAGE)
-        cast("vector", rest, 0, "w1", 0, 3)
+        rest = buffer("rest_bf", [P, 2 * K_PASS], BF16, REST_STAGE)
         nc.vector.tensor_copy(
-            rest[:, K_PASS:].rearrange("p (t a i j) -> p t a j i", t=2, i=RUN, j=PACK),
+            rest[:].rearrange("p (t a i j) -> p t a j i", t=2, i=RUN, j=PACK),
             raw["w1", 1][:].rearrange("p j (a t i) -> p t a j i", t=TILES, i=RUN)[:, 2:],
         )
         quantize_units("pair", pair, "w1", [(0, 0), (0, 1), (1, 0), (1, 1)], at=PAIR_CODES)
-        quantize_units("single", single, "w1", [(0, 2)], scale_tag="mixed_scale")
-        quantize_units("rest", rest, "w1", [(0, 3), (1, 2), (1, 3)])
+        quantize_units("single", single, "w1", [(0, 2), (0, 3)], scale_tag="third_scale")
+        quantize_units("rest", rest, "w1", [(1, 2), (1, 3)])
         for t in range(TILES):
-            for z in range(PASSES):
-                multiply("w1", z, t)
+            for h in range(HALVES):
+                for z in range(PASSES):
+                    multiply("w1", z, t, h)
             empty("w1", t)
 
-        w3_bf = buffer("w3_bf", [P, N * PACK], BF16, W3_STAGE)
-        nc.vector.tensor_copy(
-            w3_bf[:].rearrange("p (a i j) -> p a j i", i=RUN, j=PACK),
-            w3_raw[:].rearrange("p j (a i) -> p a j i", i=RUN),
-        )
         best = buffer("best", [P, TILES, V], F32, BEST)
         nc.vector.tensor_tensor(best[:, :2, :], near[:, :2, :], far[:, :2, :], ALU.max)
-        w3_code, w3_scale = quantize("w3", w3_bf)
         nc.vector.tensor_tensor(best[:, 2:, :], near[:, 2:, :], far[:, 2:, :], ALU.max)
 
-        sums = buffer("sums", [P, TILES, V], F32)
+        w3_bf = buffer("w3_bf", [P, N * PACK], BF16, tag="near")
+        nc.scalar.activation(
+            w3_bf[:].rearrange("p (a i j) -> p a j i", i=RUN, j=PACK),
+            w3_raw[:].rearrange("p j (a i) -> p a j i", i=RUN),
+            ACT.Copy,
+        )
+        sums = buffer("sums", [P, TILES * V], F32)
 
         def add_centres(t, a, b):
             centres = cen_t[:, a // LIST_ROWS : b // LIST_ROWS]
-            nc.vector.tensor_tensor(sums[:, t, a:b], rows["w1", t][:].indirect(centres), best[:, t, a:b], ALU.add)
+            nc.vector.tensor_tensor(sums[:, t * V + a : t * V + b], rows["w1", t][:].indirect(centres), best[:, t, a:b], ALU.add)
 
         out_view = out.rearrange("(u p) v -> p u v", p=P)
         z_bf = {}
 
-        def weave(c, engine):
+        def weave(c, engines):
             z_bf[c] = buffer(f"z_bf{c}", [P, CHUNK * PACK], BF16)
             dst = z_bf[c][:].rearrange("p (a i t) -> p a t i", i=RUN, t=TILES)
-            src = sums[:, :, c * CHUNK : (c + 1) * CHUNK].rearrange("p t (a i) -> p a t i", i=RUN)
-            if engine == "vector":
-                nc.vector.tensor_scalar_max(dst, src, 0.0)
-            else:
-                nc.scalar.activation(dst, src, ACT.Relu)
+            src = sums[:].rearrange("p (t c a i) -> p c a t i", t=TILES, c=V // CHUNK, i=RUN)[:, c]
+            share = CHUNK // RUN // len(engines)
+            for n, engine in enumerate(engines):
+                part = slice(n * share, (n + 1) * share)
+                if engine == "vector":
+                    nc.vector.tensor_scalar_max(dst[:, part], src[:, part], 0.0)
+                else:
+                    nc.scalar.activation(dst[:, part], src[:, part], ACT.Relu)
 
         def project(c, engines):
             z_code, z_scale = quantize(f"z{c}", z_bf[c])
@@ -283,7 +292,8 @@ def tile_picked_edgecv_relu_p_kernel(
             add_centres(t, 0, V)
         for c in range(V // CHUNK):
             add_centres(TILES - 1, c * CHUNK, (c + 1) * CHUNK)
-        for c, engine in enumerate(("scalar", "scalar", "vector", "scalar")):
-            weave(c, engine)
+        w3_code, w3_scale = quantize("w3", w3_bf)
+        for c, engines in enumerate((("scalar",), ("scalar",), ("scalar",), ("scalar", "vector"))):
+            weave(c, engines)
         for c, engines in enumerate((("scalar",), ("scalar",), ("vector",), ("scalar", "vector"))):
             project(c, engines)

@@ -31,7 +31,7 @@ LEAD_PIECES = ((0, 512, 0), (512, 768, 1), (768, 1024, 6))
 OUT_BANK = (6, 7, 0, 1, 4)
 
 PAIR_STAGE, BEST = 0, 4032
-REST_STAGE, MIXED_CODES, PAIR_CODES = 15232, 17216, 17280
+REST_STAGE, MIXED_CODES, PAIR_CODES = 14208, 17216, 17280
 
 
 def tile_picked_edgecv_relu_p_kernel(
@@ -209,21 +209,27 @@ def tile_picked_edgecv_relu_p_kernel(
             fetch(engine, far[:, t, :], t, pos2_t)
 
         pair = buffer("pair_bf", [P, 4 * K_PASS], BF16, PAIR_STAGE)
-        single = buffer("single_bf", [P, 2 * K_PASS], BF16)
-        cast("gpsimd", pair, 0, "w1", 0, 0)
-        cast("gpsimd", pair, 1, "w1", 0, 1)
-        cast("gpsimd", single, 0, "w1", 0, 2)
-        cast("gpsimd", single, 1, "w1", 0, 3)
-        cast("gpsimd", pair, 2, "w1", 1, 0)
-        cast("gpsimd", pair, 3, "w1", 1, 1)
-        rest = buffer("rest_bf", [P, 2 * K_PASS], BF16, REST_STAGE)
-        nc.vector.tensor_copy(
-            rest[:].rearrange("p (t a i j) -> p t a j i", t=2, i=RUN, j=PACK),
-            raw["w1", 1][:].rearrange("p j (a t i) -> p t a j i", t=TILES, i=RUN)[:, 2:],
+        single = buffer("single_bf", [P, K_PASS], BF16)
+        for t in range(TILES):
+            cast("gpsimd", pair, t, "w1", 0, t)
+        cast("gpsimd", single, 0, "w1", 1, 0)
+        w3_bf = [buffer("w3_bf0", [P, K_PASS], BF16)]
+        nc.gpsimd.tensor_scalar(
+            w3_bf[0][:].rearrange("p (c j) -> p c j", j=PACK),
+            w3_raw[:, :, :P].rearrange("p j c -> p c j"),
+            1.0,
+            0.0,
+            ALU.mult,
+            ALU.add,
         )
-        quantize_units("pair", pair, "w1", [(0, 0), (0, 1), (1, 0), (1, 1)], at=PAIR_CODES)
-        quantize_units("single", single, "w1", [(0, 2), (0, 3)], scale_tag="third_scale")
-        quantize_units("rest", rest, "w1", [(1, 2), (1, 3)])
+        rest = buffer("rest_bf", [P, 3 * K_PASS], BF16, REST_STAGE)
+        nc.vector.tensor_copy(
+            rest[:].rearrange("p (t a i j) -> p a t j i", t=3, i=RUN, j=PACK),
+            raw["w1", 1][:].rearrange("p j (a t i) -> p a t j i", t=TILES, i=RUN)[:, :, 1:],
+        )
+        quantize_units("pair", pair, "w1", [(0, t) for t in range(TILES)], at=PAIR_CODES)
+        quantize_units("single", single, "w1", [(1, 0)], scale_tag="third_scale")
+        quantize_units("rest", rest, "w1", [(1, 1), (1, 2), (1, 3)])
         for t in range(TILES):
             for h in range(HALVES):
                 for z in range(PASSES):
@@ -232,12 +238,13 @@ def tile_picked_edgecv_relu_p_kernel(
 
         best = buffer("best", [P, TILES, V], F32, BEST)
         nc.vector.tensor_tensor(best[:, :2, :], near[:, :2, :], far[:, :2, :], ALU.max)
+        w3_parts = [quantize("w3_0", w3_bf[0])]
         nc.vector.tensor_tensor(best[:, 2:, :], near[:, 2:, :], far[:, 2:, :], ALU.max)
 
-        w3_bf = buffer("w3_bf", [P, N * PACK], BF16, tag="near")
+        w3_bf.append(buffer("w3_bf1", [P, K_PASS], BF16, tag="near"))
         nc.scalar.activation(
-            w3_bf[:].rearrange("p (a i j) -> p a j i", i=RUN, j=PACK),
-            w3_raw[:].rearrange("p j (a i) -> p a j i", i=RUN),
+            w3_bf[1][:].rearrange("p (a i j) -> p a j i", i=RUN, j=PACK),
+            w3_raw[:, :, P:].rearrange("p j (a i) -> p a j i", i=RUN),
             ACT.Copy,
         )
         sums = buffer("sums", [P, TILES * V], F32)
@@ -269,11 +276,10 @@ def tile_picked_edgecv_relu_p_kernel(
                 both = psum.tile([P, N // P, CHUNK], F32, name=f"out_acc{c}", tag=f"bank{OUT_BANK[c]}")
                 acc = [both[:, u, :] for u in range(N // P)]
             for u in range(N // P):
-                cols = slice(u * P, (u + 1) * P)
                 nc.tensor.matmul_mx(
                     out=acc[u],
-                    lhsT=w3_code[:, cols].bitcast(FP8X4),
-                    lhsT_scale=w3_scale[:, cols],
+                    lhsT=w3_parts[u][0][:].bitcast(FP8X4),
+                    lhsT_scale=w3_parts[u][1][:],
                     rhs=z_code[:].bitcast(FP8X4),
                     rhs_scale=z_scale[:],
                     start=True,
@@ -292,7 +298,7 @@ def tile_picked_edgecv_relu_p_kernel(
             add_centres(t, 0, V)
         for c in range(V // CHUNK):
             add_centres(TILES - 1, c * CHUNK, (c + 1) * CHUNK)
-        w3_code, w3_scale = quantize("w3", w3_bf)
+        w3_parts.append(quantize("w3_1", w3_bf[1]))
         for c, engines in enumerate((("scalar",), ("scalar",), ("scalar",), ("scalar", "vector"))):
             weave(c, engines)
         for c, engines in enumerate((("scalar",), ("scalar",), ("vector",), ("scalar", "vector"))):

@@ -24,11 +24,14 @@ HALVES = S // BANK
 LIST_ROWS = 16
 TILES = H // P
 RUN = 4
+RUNS = P // RUN
+LEAD_SPLIT = 20
 CHUNK = 128
+WARM_UPS = 4
 
 FIRST_BANK = {"w2": (0, 2, 4, 2), "w1": (6, 0, 4, 2)}
 LEAD_PIECES = ((0, 512, 0), (512, 768, 1), (768, 1024, 6))
-OUT_BANK = (6, 7, 0, 1, 4)
+OUT_BANK = (6, 7, 0, 4)
 
 PAIR_STAGE, BEST = 0, 4032
 REST_STAGE, MIXED_CODES, PAIR_CODES = 14208, 17216, 17280
@@ -90,9 +93,10 @@ def tile_picked_edgecv_relu_p_kernel(
         for t in range(TILES):
             nc.sync.dma_start(w3_raw[:, t, :], w3_rows[t])
 
-        def cast(engine, stage, slot, name, z, t):
-            dst = stage[:, slot * K_PASS : (slot + 1) * K_PASS]
-            src = raw[name, z][:].rearrange("p j (a t i) -> p t a j i", t=TILES, i=RUN)[:, t]
+        def cast(engine, stage, slot, name, z, t, first=0, last=RUNS):
+            step = RUN * PACK
+            dst = stage[:, slot * K_PASS + first * step : slot * K_PASS + last * step]
+            src = raw[name, z][:].rearrange("p j (a t i) -> p t a j i", t=TILES, i=RUN)[:, t, first:last]
             if engine == "gpsimd":
                 nc.gpsimd.tensor_scalar(
                     dst.rearrange("p (a i j) -> p a i j", i=RUN, j=PACK),
@@ -118,6 +122,7 @@ def tile_picked_edgecv_relu_p_kernel(
 
         def quantize_units(label, stage, name, units, at=None, scale_tag=None):
             codes, scales = quantize(label, stage, at, None, scale_tag)
+            quantized[label] = (codes, scales)
             for slot, (z, t) in enumerate(units):
                 cols = slice(slot * P, (slot + 1) * P)
                 quantized[name, z, t] = (codes[:, cols], scales[:, cols])
@@ -184,7 +189,8 @@ def tile_picked_edgecv_relu_p_kernel(
         cast("scalar", mixed, 0, "w2", 0, 3)
         pick_words(1, "w2_raw0")
         lead = buffer("lead_bf", [P, K_PASS], BF16)
-        cast("scalar", lead, 0, "w2", 1, 0)
+        cast("scalar", lead, 0, "w2", 1, 0, last=LEAD_SPLIT)
+        cast("gpsimd", lead, 0, "w2", 1, 0, first=LEAD_SPLIT)
         quantize_units("lead", lead, "w2", [(1, 0)])
         multiply("w2", 1, 0)
         third = buffer("third_bf", [P, 2 * K_PASS], BF16, tag="lead_bf")
@@ -207,6 +213,19 @@ def tile_picked_edgecv_relu_p_kernel(
             engine = "vector" if t < 2 else "scalar"
             fetch(engine, near[:, t, :], t, pos1_t)
             fetch(engine, far[:, t, :], t, pos2_t)
+
+        codes, scales = quantized["early"]
+        idle = psum.tile([P, 2 * P], F32, name="warm_up", tag=f"bank{FIRST_BANK['w2'][TILES - 1] + 1}")
+        for n in range(WARM_UPS):
+            nc.tensor.matmul_mx(
+                out=idle[:],
+                lhsT=codes[:, :P].bitcast(FP8X4),
+                lhsT_scale=scales[:, :P],
+                rhs=codes[:, : 2 * P].bitcast(FP8X4),
+                rhs_scale=scales[:, : 2 * P],
+                start=True,
+                stop=True,
+            )
 
         pair = buffer("pair_bf", [P, 4 * K_PASS], BF16, PAIR_STAGE)
         single = buffer("single_bf", [P, K_PASS], BF16)
@@ -257,7 +276,7 @@ def tile_picked_edgecv_relu_p_kernel(
         z_bf = {}
 
         def weave(c, engines):
-            z_bf[c] = buffer(f"z_bf{c}", [P, CHUNK * PACK], BF16)
+            z_bf[c] = buffer(f"z_bf{c}", [P, CHUNK * PACK], BF16, tag=f"z_bf{(0, 1, 2, 0)[c]}")
             dst = z_bf[c][:].rearrange("p (a i t) -> p a t i", i=RUN, t=TILES)
             src = sums[:].rearrange("p (t c a i) -> p c a t i", t=TILES, c=V // CHUNK, i=RUN)[:, c]
             share = CHUNK // RUN // len(engines)
@@ -269,9 +288,9 @@ def tile_picked_edgecv_relu_p_kernel(
                     nc.scalar.activation(dst[:, part], src[:, part], ACT.Relu)
 
         def project(c, engines):
-            z_code, z_scale = quantize(f"z{c}", z_bf[c])
+            z_code, z_scale = codes[c]
             if len(engines) > 1:
-                acc = [psum.tile([P, CHUNK], F32, name=f"out_acc{c}{u}", tag=f"bank{OUT_BANK[c + u]}")[:] for u in range(N // P)]
+                acc = [psum.tile([P, CHUNK], F32, name=f"out_acc{c}{u}", tag=f"bank{OUT_BANK[c] + u}")[:] for u in range(N // P)]
             else:
                 both = psum.tile([P, N // P, CHUNK], F32, name=f"out_acc{c}", tag=f"bank{OUT_BANK[c]}")
                 acc = [both[:, u, :] for u in range(N // P)]
@@ -299,7 +318,10 @@ def tile_picked_edgecv_relu_p_kernel(
         for c in range(V // CHUNK):
             add_centres(TILES - 1, c * CHUNK, (c + 1) * CHUNK)
         w3_parts.append(quantize("w3_1", w3_bf[1]))
-        for c, engines in enumerate((("scalar",), ("scalar",), ("scalar",), ("scalar", "vector"))):
-            weave(c, engines)
-        for c, engines in enumerate((("scalar",), ("scalar",), ("vector",), ("scalar", "vector"))):
+        for c in range(3):
+            weave(c, ("scalar",))
+        codes = [quantize(f"z{c}", z_bf[c]) for c in range(1)]
+        weave(3, ("vector",))
+        codes.extend(quantize(f"z{c}", z_bf[c]) for c in range(1, 4))
+        for c, engines in enumerate((("scalar",), ("scalar",), ("scalar", "vector"), ("scalar", "vector"))):
             project(c, engines)

@@ -27,7 +27,7 @@ RUN = 4
 RUNS = P // RUN
 LEAD_SPLIT = 20
 CHUNK = 128
-WARM_UPS = 4
+WARM_UPS = 6
 
 FIRST_BANK = {"w2": (0, 2, 4, 2), "w1": (6, 0, 4, 2)}
 LEAD_PIECES = ((0, 512, 0), (512, 768, 1), (768, 1024, 6))
@@ -311,7 +311,12 @@ def tile_picked_edgecv_relu_p_kernel(
                     nc.vector.tensor_copy(dst, src)
                 else:
                     nc.scalar.activation(dst, src, ACT.Copy)
-            nc.sync.dma_start(out_view[:, :, c * CHUNK : (c + 1) * CHUNK], result[:])
+            cols = slice(c * CHUNK, (c + 1) * CHUNK)
+            if len(engines) > 1:
+                nc.scalar.dma_start(out_view[:, 0, cols], result[:, 0, :])
+                nc.sync.dma_start(out_view[:, 1, cols], result[:, 1, :])
+            else:
+                nc.sync.dma_start(out_view[:, :, cols], result[:])
 
         for t in range(TILES - 1):
             add_centres(t, 0, V)

@@ -27,7 +27,6 @@ RUN = 4
 RUNS = P // RUN
 LEAD_SPLIT = 20
 CHUNK = 128
-WARM_UPS = 6
 
 FIRST_BANK = {"w2": (0, 2, 4, 2), "w1": (6, 0, 4, 2)}
 LEAD_PIECES = ((0, 512, 0), (512, 768, 1), (768, 1024, 6))
@@ -122,7 +121,6 @@ def tile_picked_edgecv_relu_p_kernel(
 
         def quantize_units(label, stage, name, units, at=None, scale_tag=None):
             codes, scales = quantize(label, stage, at, None, scale_tag)
-            quantized[label] = (codes, scales)
             for slot, (z, t) in enumerate(units):
                 cols = slice(slot * P, (slot + 1) * P)
                 quantized[name, z, t] = (codes[:, cols], scales[:, cols])
@@ -213,19 +211,6 @@ def tile_picked_edgecv_relu_p_kernel(
             engine = "vector" if t < 2 else "scalar"
             fetch(engine, near[:, t, :], t, pos1_t)
             fetch(engine, far[:, t, :], t, pos2_t)
-
-        codes, scales = quantized["early"]
-        idle = psum.tile([P, 2 * P], F32, name="warm_up", tag=f"bank{FIRST_BANK['w2'][TILES - 1] + 1}")
-        for n in range(WARM_UPS):
-            nc.tensor.matmul_mx(
-                out=idle[:],
-                lhsT=codes[:, :P].bitcast(FP8X4),
-                lhsT_scale=scales[:, :P],
-                rhs=codes[:, : 2 * P].bitcast(FP8X4),
-                rhs_scale=scales[:, : 2 * P],
-                start=True,
-                stop=True,
-            )
 
         pair = buffer("pair_bf", [P, 4 * K_PASS], BF16, PAIR_STAGE)
         single = buffer("single_bf", [P, K_PASS], BF16)

@@ -22,6 +22,7 @@ PASSES = K // K_PASS
 BANK = 512
 HALVES = S // BANK
 LIST_ROWS = 16
+SCALE_ROWS = 32
 TILES = H // P
 RUN = 4
 RUNS = P // RUN
@@ -56,7 +57,7 @@ def tile_picked_edgecv_relu_p_kernel(
             return lst
 
         def load_words(z):
-            table = keep.tile([P, T], U32, name=f"x_table{z}")
+            table = buffer(f"x_table{z}", [P, T], U32)
             nc.sync.dma_start(
                 table[:].bitcast(I32), x_words[z].rearrange("p c r -> p (c r)").bitcast(I32)
             )
@@ -64,29 +65,44 @@ def tile_picked_edgecv_relu_p_kernel(
 
         raw = {}
 
-        def load_weight(name, w, z, at=None):
-            raw[name, z] = buffer(f"{name}_raw{z}", [P, PACK, H], F32, at)
+        def load_weight(name, w, z, tag=None):
+            raw[name, z] = buffer(f"{name}_raw{z}", [P, PACK, H], F32, tag=tag)
             rows = w[z * K_PASS : (z + 1) * K_PASS, :]
             nc.sync.dma_start(raw[name, z][:], rows.rearrange("(p j) c -> p j c", j=PACK))
 
         scale_table = keep.tile([P, T], U8, name="scale_table")
-        nc.vector.memset(scale_table[:].bitcast(I32), 0)
+        nc.sync.dma_start(
+            scale_table[:SCALE_ROWS, :].bitcast(I32), x_scales.rearrange("z q c -> (z q) c").bitcast(I32)
+        )
+        nc.vector.memset(scale_table[SCALE_ROWS : P // 2, :].bitcast(I32), 0)
+        nc.vector.memset(scale_table[P // 2 :, :].bitcast(I32), 0)
+        x_scale = [buffer(f"x_scale{z}", [P, S], U8) for z in range(PASSES)]
+        for plane in x_scale:
+            nc.gpsimd.memset(plane[:].bitcast(I32), 0)
 
-        x_table = [load_words(0)]
         offs_t = load_list("offs_t", offs)
-        for q in range(4):
-            nc.sync.dma_start(
-                scale_table[32 * q : 32 * q + 4 * PASSES, :].bitcast(I32),
-                x_scales[:, 4 * q : 4 * q + 4, :].bitcast(I32),
-            )
-        load_weight("w2", w2, 0)
-        x_table.append(load_words(1))
-        load_weight("w2", w2, 1)
+        x_table = [load_words(0)]
         pos1_t = load_list("pos1_t", pos1)
         pos2_t = load_list("pos2_t", pos2)
+        cen_t = load_list("cen_t", cen)
+        load_weight("w2", w2, 0)
+        x_table.append(load_words(1))
+
+        picked_scale = buffer("picked_scale", [P, S], U8)
+        nc.vector.tensor_copy(picked_scale[:], scale_table[:].indirect(offs_t[:]))
+
+        def place_scales(queue, z):
+            for q in range(4):
+                queue.dma_start(
+                    x_scale[z][32 * q : 32 * q + 4, :].bitcast(I32),
+                    picked_scale[16 * z + 4 * q : 16 * z + 4 * q + 4, :].bitcast(I32),
+                )
+
+        place_scales(nc.sync, 0)
+        load_weight("w2", w2, 1)
+        place_scales(nc.sync, 1)
         load_weight("w1", w1, 0)
         load_weight("w1", w1, 1)
-        cen_t = load_list("cen_t", cen)
         w3_raw = buffer("w3_raw", [P, PACK, N], F32)
         w3_rows = w3.rearrange("(a t b) n -> t a b n", t=TILES, b=RUN)
         for t in range(TILES):
@@ -151,7 +167,7 @@ def tile_picked_edgecv_relu_p_kernel(
                     lhsT=codes.bitcast(FP8X4),
                     lhsT_scale=scales,
                     rhs=x_code[z][:, cols].bitcast(FP8X4),
-                    rhs_scale=x_scale[4 * z : P, cols],
+                    rhs_scale=x_scale[z][:, cols],
                     start=(z == 0),
                     stop=(z == PASSES - 1),
                 )
@@ -175,17 +191,18 @@ def tile_picked_edgecv_relu_p_kernel(
                 nc.scalar.activation(dst, window, ACT.Copy)
 
         pick_words(0)
-        x_scale = buffer("x_scale", [P, S], U8)
-        nc.vector.tensor_copy(x_scale[:], scale_table[:].indirect(offs_t[:]))
-        early = buffer("early_bf", [P, 3 * K_PASS], BF16)
-        for t in range(3):
+        early = buffer("early_bf", [P, TILES * K_PASS], BF16)
+        for t in range(2):
             cast("scalar", early, t, "w2", 0, t)
-        quantize_units("early", early, "w2", [(0, t) for t in range(3)])
+        nc.vector.tensor_copy(
+            early[:].rearrange("p (t a i j) -> p t a j i", t=TILES, i=RUN, j=PACK)[:, 2:],
+            raw["w2", 0][:].rearrange("p j (a t i) -> p t a j i", t=TILES, i=RUN)[:, 2:],
+        )
+        quantize_units("early", early, "w2", [(0, t) for t in range(TILES)])
         for t in range(3):
             multiply("w2", 0, t)
-        mixed = buffer("mixed_bf", [P, 2 * K_PASS], BF16)
-        cast("scalar", mixed, 0, "w2", 0, 3)
         pick_words(1, "w2_raw0")
+        mixed = buffer("mixed_bf", [P, K_PASS], BF16)
         lead = buffer("lead_bf", [P, K_PASS], BF16)
         cast("scalar", lead, 0, "w2", 1, 0, last=LEAD_SPLIT)
         cast("gpsimd", lead, 0, "w2", 1, 0, first=LEAD_SPLIT)
@@ -193,8 +210,8 @@ def tile_picked_edgecv_relu_p_kernel(
         multiply("w2", 1, 0)
         third = buffer("third_bf", [P, 2 * K_PASS], BF16, tag="lead_bf")
         cast("vector", third, 1, "w2", 1, 3)
-        cast("scalar", mixed, 1, "w2", 1, 1)
-        quantize_units("mixed", mixed, "w2", [(0, 3), (1, 1)])
+        cast("scalar", mixed, 0, "w2", 1, 1)
+        quantize_units("mixed", mixed, "w2", [(1, 1)])
         cast("scalar", third, 0, "w2", 1, 2)
         empty("w2", 0, "vector")
         quantize_units("third", third, "w2", [(1, 2), (1, 3)], at=MIXED_CODES)

@@ -33,7 +33,7 @@ FIRST_BANK = {"w2": (0, 2, 4, 2), "w1": (6, 0, 4, 2)}
 LEAD_PIECES = ((0, 512, 0), (512, 768, 1), (768, 1024, 6))
 OUT_BANK = (6, 7, 0, 4)
 
-PAIR_STAGE, BEST = 0, 4032
+PAIR_STAGE, BEST, W1_FIRST = 0, 4032, 6080
 REST_STAGE, MIXED_CODES, PAIR_CODES = 14208, 17216, 17280
 
 
@@ -65,8 +65,8 @@ def tile_picked_edgecv_relu_p_kernel(
 
         raw = {}
 
-        def load_weight(name, w, z, tag=None):
-            raw[name, z] = buffer(f"{name}_raw{z}", [P, PACK, H], F32, tag=tag)
+        def load_weight(name, w, z, at=None):
+            raw[name, z] = buffer(f"{name}_raw{z}", [P, PACK, H], F32, at)
             rows = w[z * K_PASS : (z + 1) * K_PASS, :]
             nc.sync.dma_start(raw[name, z][:], rows.rearrange("(p j) c -> p j c", j=PACK))
 
@@ -101,7 +101,7 @@ def tile_picked_edgecv_relu_p_kernel(
         place_scales(nc.sync, 0)
         load_weight("w2", w2, 1)
         place_scales(nc.sync, 1)
-        load_weight("w1", w1, 0)
+        load_weight("w1", w1, 0, W1_FIRST)
         load_weight("w1", w1, 1)
         w3_raw = buffer("w3_raw", [P, PACK, N], F32)
         w3_rows = w3.rearrange("(a t b) n -> t a b n", t=TILES, b=RUN)
@@ -231,9 +231,10 @@ def tile_picked_edgecv_relu_p_kernel(
 
         pair = buffer("pair_bf", [P, 4 * K_PASS], BF16, PAIR_STAGE)
         single = buffer("single_bf", [P, K_PASS], BF16)
-        for t in range(TILES):
-            cast("gpsimd", pair, t, "w1", 0, t)
-        cast("gpsimd", single, 0, "w1", 1, 0)
+        pair_units = [(0, 0), (0, 1), (0, 2), (1, 0)]
+        for slot, (z, t) in enumerate(pair_units):
+            cast("gpsimd", pair, slot, "w1", z, t)
+        cast("gpsimd", single, 0, "w1", 0, 3)
         w3_bf = [buffer("w3_bf0", [P, K_PASS], BF16)]
         nc.gpsimd.tensor_scalar(
             w3_bf[0][:].rearrange("p (c j) -> p c j", j=PACK),
@@ -243,13 +244,13 @@ def tile_picked_edgecv_relu_p_kernel(
             ALU.mult,
             ALU.add,
         )
+        quantize_units("pair", pair, "w1", pair_units, at=PAIR_CODES)
         rest = buffer("rest_bf", [P, 3 * K_PASS], BF16, REST_STAGE)
         nc.vector.tensor_copy(
             rest[:].rearrange("p (t a i j) -> p a t j i", t=3, i=RUN, j=PACK),
             raw["w1", 1][:].rearrange("p j (a t i) -> p a t j i", t=TILES, i=RUN)[:, :, 1:],
         )
-        quantize_units("pair", pair, "w1", [(0, t) for t in range(TILES)], at=PAIR_CODES)
-        quantize_units("single", single, "w1", [(1, 0)], scale_tag="third_scale")
+        quantize_units("single", single, "w1", [(0, 3)], scale_tag="third_scale")
         quantize_units("rest", rest, "w1", [(1, 1), (1, 2), (1, 3)])
         for t in range(TILES):
             for h in range(HALVES):
@@ -262,7 +263,7 @@ def tile_picked_edgecv_relu_p_kernel(
         w3_parts = [quantize("w3_0", w3_bf[0])]
         nc.vector.tensor_tensor(best[:, 2:, :], near[:, 2:, :], far[:, 2:, :], ALU.max)
 
-        w3_bf.append(buffer("w3_bf1", [P, K_PASS], BF16, tag="near"))
+        w3_bf.append(buffer("w3_bf1", [P, K_PASS], BF16, tag="rest_code"))
         nc.scalar.activation(
             w3_bf[1][:].rearrange("p (a i j) -> p a j i", i=RUN, j=PACK),
             w3_raw[:, :, P:].rearrange("p j (a i) -> p a j i", i=RUN),

@@ -82,9 +82,6 @@ def tile_picked_edgecv_relu_p_kernel(
 
         offs_t = load_list("offs_t", offs)
         x_table = [load_words(0)]
-        pos1_t = load_list("pos1_t", pos1)
-        pos2_t = load_list("pos2_t", pos2)
-        cen_t = load_list("cen_t", cen)
         load_weight("w2", w2, 0)
         x_table.append(load_words(1))
 
@@ -101,8 +98,11 @@ def tile_picked_edgecv_relu_p_kernel(
         place_scales(nc.sync, 0)
         load_weight("w2", w2, 1)
         place_scales(nc.sync, 1)
+        pos1_t = load_list("pos1_t", pos1)
+        pos2_t = load_list("pos2_t", pos2)
         load_weight("w1", w1, 0, W1_FIRST)
         load_weight("w1", w1, 1)
+        cen_t = load_list("cen_t", cen)
         w3_raw = buffer("w3_raw", [P, PACK, N], F32)
         w3_rows = w3.rearrange("(a t b) n -> t a b n", t=TILES, b=RUN)
         for t in range(TILES):

@@ -33,7 +33,7 @@ FIRST_BANK = {"w2": (0, 2, 4, 2), "w1": (6, 0, 4, 2)}
 LEAD_PIECES = ((0, 512, 0), (512, 768, 1), (768, 1024, 6))
 OUT_BANK = (6, 7, 0, 4)
 
-PAIR_STAGE, BEST, W1_FIRST = 0, 4032, 6080
+PAIR_STAGE, BEST = 0, 4032
 REST_STAGE, MIXED_CODES, PAIR_CODES = 14208, 17216, 17280
 
 
@@ -88,19 +88,20 @@ def tile_picked_edgecv_relu_p_kernel(
         picked_scale = buffer("picked_scale", [P, S], U8)
         nc.vector.tensor_copy(picked_scale[:], scale_table[:].indirect(offs_t[:]))
 
-        def place_scales(queue, z):
-            for q in range(4):
+        def place_scales(queue, z, quadrants):
+            for q in quadrants:
                 queue.dma_start(
                     x_scale[z][32 * q : 32 * q + 4, :].bitcast(I32),
                     picked_scale[16 * z + 4 * q : 16 * z + 4 * q + 4, :].bitcast(I32),
                 )
 
-        place_scales(nc.sync, 0)
+        place_scales(nc.scalar, 0, range(4))
+        place_scales(nc.scalar, 1, range(2))
         load_weight("w2", w2, 1)
-        place_scales(nc.sync, 1)
+        place_scales(nc.sync, 1, range(2, 4))
         pos1_t = load_list("pos1_t", pos1)
+        load_weight("w1", w1, 0)
         pos2_t = load_list("pos2_t", pos2)
-        load_weight("w1", w1, 0, W1_FIRST)
         load_weight("w1", w1, 1)
         cen_t = load_list("cen_t", cen)
         w3_raw = buffer("w3_raw", [P, PACK, N], F32)
@@ -192,11 +193,10 @@ def tile_picked_edgecv_relu_p_kernel(
 
         pick_words(0)
         early = buffer("early_bf", [P, TILES * K_PASS], BF16)
-        for t in range(2):
-            cast("scalar", early, t, "w2", 0, t)
+        cast("scalar", early, 0, "w2", 0, 0)
         nc.vector.tensor_copy(
-            early[:].rearrange("p (t a i j) -> p t a j i", t=TILES, i=RUN, j=PACK)[:, 2:],
-            raw["w2", 0][:].rearrange("p j (a t i) -> p t a j i", t=TILES, i=RUN)[:, 2:],
+            early[:].rearrange("p (t a i j) -> p a t j i", t=TILES, i=RUN, j=PACK)[:, :, 1:],
+            raw["w2", 0][:].rearrange("p j (a t i) -> p a t j i", t=TILES, i=RUN)[:, :, 1:],
         )
         quantize_units("early", early, "w2", [(0, t) for t in range(TILES)])
         for t in range(3):
@@ -244,12 +244,12 @@ def tile_picked_edgecv_relu_p_kernel(
             ALU.mult,
             ALU.add,
         )
-        quantize_units("pair", pair, "w1", pair_units, at=PAIR_CODES)
         rest = buffer("rest_bf", [P, 3 * K_PASS], BF16, REST_STAGE)
         nc.vector.tensor_copy(
             rest[:].rearrange("p (t a i j) -> p a t j i", t=3, i=RUN, j=PACK),
             raw["w1", 1][:].rearrange("p j (a t i) -> p a t j i", t=TILES, i=RUN)[:, :, 1:],
         )
+        quantize_units("pair", pair, "w1", pair_units, at=PAIR_CODES)
         quantize_units("single", single, "w1", [(0, 3)], scale_tag="third_scale")
         quantize_units("rest", rest, "w1", [(1, 1), (1, 2), (1, 3)])
         for t in range(TILES):

@@ -235,19 +235,15 @@ def tile_picked_edgecv_relu_p_kernel(
         for slot, (z, t) in enumerate(pair_units):
             cast("gpsimd", pair, slot, "w1", z, t)
         cast("gpsimd", single, 0, "w1", 0, 3)
-        w3_bf = [buffer("w3_bf0", [P, K_PASS], BF16)]
-        nc.gpsimd.tensor_scalar(
-            w3_bf[0][:].rearrange("p (c j) -> p c j", j=PACK),
-            w3_raw[:, :, :P].rearrange("p j c -> p c j"),
-            1.0,
-            0.0,
-            ALU.mult,
-            ALU.add,
-        )
         rest = buffer("rest_bf", [P, 3 * K_PASS], BF16, REST_STAGE)
         nc.vector.tensor_copy(
             rest[:].rearrange("p (t a i j) -> p a t j i", t=3, i=RUN, j=PACK),
             raw["w1", 1][:].rearrange("p j (a t i) -> p a t j i", t=TILES, i=RUN)[:, :, 1:],
+        )
+        w3_bf = [buffer("w3_bf0", [P, K_PASS], BF16, tag="w1_raw1")]
+        nc.vector.tensor_copy(
+            w3_bf[0][:].rearrange("p (a i j) -> p a j i", i=RUN, j=PACK),
+            w3_raw[:, :, :P].rearrange("p j (a i) -> p a j i", i=RUN),
         )
         quantize_units("pair", pair, "w1", pair_units, at=PAIR_CODES)
         quantize_units("single", single, "w1", [(0, 3)], scale_tag="third_scale")

@@ -192,13 +192,15 @@ def tile_picked_edgecv_relu_p_kernel(
                 nc.scalar.activation(dst, window, ACT.Copy)
 
         pick_words(0)
-        early = buffer("early_bf", [P, TILES * K_PASS], BF16)
-        cast("scalar", early, 0, "w2", 0, 0)
+        early = [buffer(f"early_bf{n}", [P, 2 * K_PASS], BF16) for n in range(2)]
         nc.vector.tensor_copy(
-            early[:].rearrange("p (t a i j) -> p a t j i", t=TILES, i=RUN, j=PACK)[:, :, 1:],
-            raw["w2", 0][:].rearrange("p j (a t i) -> p a t j i", t=TILES, i=RUN)[:, :, 1:],
+            early[0][:].rearrange("p (t a i j) -> p a t j i", t=2, i=RUN, j=PACK),
+            raw["w2", 0][:].rearrange("p j (a t i) -> p a t j i", t=TILES, i=RUN)[:, :, :2],
         )
-        quantize_units("early", early, "w2", [(0, t) for t in range(TILES)])
+        cast("vector", early[1], 0, "w2", 0, 2)
+        cast("scalar", early[1], 1, "w2", 0, 3)
+        for n in range(2):
+            quantize_units(f"early{n}", early[n], "w2", [(0, 2 * n), (0, 2 * n + 1)])
         for t in range(3):
             multiply("w2", 0, t)
         pick_words(1, "w2_raw0")

@@ -28,6 +28,7 @@ RUN = 4
 RUNS = P // RUN
 LEAD_SPLIT = 20
 CHUNK = 128
+WARM_PASSES = 4
 
 FIRST_BANK = {"w2": (0, 2, 4, 2), "w1": (6, 0, 4, 2)}
 LEAD_PIECES = ((0, 512, 0), (512, 768, 1), (768, 1024, 6))
@@ -134,10 +135,11 @@ def tile_picked_edgecv_relu_p_kernel(
             nc.vector.quantize_mx(out=codes[:].bitcast(FP8X4), scales=scales[:], in_=stage[:])
             return codes, scales
 
-        quantized = {}
+        quantized, whole = {}, {}
 
         def quantize_units(label, stage, name, units, at=None, scale_tag=None):
             codes, scales = quantize(label, stage, at, None, scale_tag)
+            whole[label] = (codes, scales)
             for slot, (z, t) in enumerate(units):
                 cols = slice(slot * P, (slot + 1) * P)
                 quantized[name, z, t] = (codes[:, cols], scales[:, cols])
@@ -201,6 +203,17 @@ def tile_picked_edgecv_relu_p_kernel(
         cast("scalar", early[1], 1, "w2", 0, 3)
         for n in range(2):
             quantize_units(f"early{n}", early[n], "w2", [(0, 2 * n), (0, 2 * n + 1)])
+        warm = psum.tile([P, 2 * P], F32, name="warm", tag="bank7")
+        for n in range(WARM_PASSES):
+            nc.tensor.matmul_mx(
+                out=warm[:],
+                lhsT=quantized["w2", 0, 0][0].bitcast(FP8X4),
+                lhsT_scale=quantized["w2", 0, 0][1],
+                rhs=whole["early0"][0][:].bitcast(FP8X4),
+                rhs_scale=whole["early0"][1][:],
+                start=True,
+                stop=True,
+            )
         for t in range(3):
             multiply("w2", 0, t)
         pick_words(1, "w2_raw0")

@@ -177,11 +177,11 @@ def tile_picked_edgecv_relu_p_kernel(
 
         rows = {}
 
-        def empty(name, t, first="scalar"):
+        def empty(name, t, on_vector=None):
             rows[name, t] = buffer(f"{name}_rows{t}", [P, S], F32)
             for h, (a, b, bank) in enumerate(pieces(name, t)):
                 dst = rows[name, t][:, a:b]
-                if h == 0 and first == "vector":
+                if h == on_vector:
                     nc.vector.tensor_copy(dst, banks[name, t, h][:])
                 else:
                     nc.scalar.activation(dst, banks[name, t, h][:], ACT.Copy)
@@ -228,7 +228,7 @@ def tile_picked_edgecv_relu_p_kernel(
         cast("scalar", mixed, 0, "w2", 1, 1)
         quantize_units("mixed", mixed, "w2", [(1, 1)])
         cast("scalar", third, 0, "w2", 1, 2)
-        empty("w2", 0, "vector")
+        empty("w2", 0, 0)
         quantize_units("third", third, "w2", [(1, 2), (1, 3)], at=MIXED_CODES)
         multiply("w2", 1, 1)
         multiply("w2", 1, 2)
@@ -238,7 +238,7 @@ def tile_picked_edgecv_relu_p_kernel(
         near = buffer("near", [P, TILES, V], F32)
         far = buffer("far", [P, TILES, V], F32)
         for t in range(1, TILES):
-            empty("w2", t)
+            empty("w2", t, 1 if t == 2 else None)
         for t in range(TILES):
             engine = "vector" if t < 2 else "scalar"
             fetch(engine, near[:, t, :], t, pos1_t)
@@ -255,11 +255,6 @@ def tile_picked_edgecv_relu_p_kernel(
             rest[:].rearrange("p (t a i j) -> p a t j i", t=3, i=RUN, j=PACK),
             raw["w1", 1][:].rearrange("p j (a t i) -> p a t j i", t=TILES, i=RUN)[:, :, 1:],
         )
-        w3_bf = [buffer("w3_bf0", [P, K_PASS], BF16, tag="w1_raw1")]
-        nc.vector.tensor_copy(
-            w3_bf[0][:].rearrange("p (a i j) -> p a j i", i=RUN, j=PACK),
-            w3_raw[:, :, :P].rearrange("p j (a i) -> p a j i", i=RUN),
-        )
         quantize_units("pair", pair, "w1", pair_units, at=PAIR_CODES)
         quantize_units("single", single, "w1", [(0, 3)], scale_tag="third_scale")
         quantize_units("rest", rest, "w1", [(1, 1), (1, 2), (1, 3)])
@@ -271,13 +266,12 @@ def tile_picked_edgecv_relu_p_kernel(
 
         best = buffer("best", [P, TILES, V], F32, BEST)
         nc.vector.tensor_tensor(best[:, :2, :], near[:, :2, :], far[:, :2, :], ALU.max)
-        w3_parts = [quantize("w3_0", w3_bf[0])]
         nc.vector.tensor_tensor(best[:, 2:, :], near[:, 2:, :], far[:, 2:, :], ALU.max)
 
-        w3_bf.append(buffer("w3_bf1", [P, K_PASS], BF16, tag="rest_code"))
+        w3_bf = buffer("w3_bf", [P, 2 * K_PASS], BF16, tag="rest_code")
         nc.scalar.activation(
-            w3_bf[1][:].rearrange("p (a i j) -> p a j i", i=RUN, j=PACK),
-            w3_raw[:, :, P:].rearrange("p j (a i) -> p a j i", i=RUN),
+            w3_bf[:].rearrange("p (a i j) -> p a j i", i=RUN, j=PACK),
+            w3_raw[:].rearrange("p j (a i) -> p a j i", i=RUN),
             ACT.Copy,
         )
         sums = buffer("sums", [P, TILES * V], F32)
@@ -311,8 +305,8 @@ def tile_picked_edgecv_relu_p_kernel(
             for u in range(N // P):
                 nc.tensor.matmul_mx(
                     out=acc[u],
-                    lhsT=w3_parts[u][0][:].bitcast(FP8X4),
-                    lhsT_scale=w3_parts[u][1][:],
+                    lhsT=w3_code[:, u * P : (u + 1) * P].bitcast(FP8X4),
+                    lhsT_scale=w3_scale[:, u * P : (u + 1) * P],
                     rhs=z_code[:].bitcast(FP8X4),
                     rhs_scale=z_scale[:],
                     start=True,
@@ -336,7 +330,7 @@ def tile_picked_edgecv_relu_p_kernel(
             add_centres(t, 0, V)
         for c in range(V // CHUNK):
             add_centres(TILES - 1, c * CHUNK, (c + 1) * CHUNK)
-        w3_parts.append(quantize("w3_1", w3_bf[1]))
+        w3_code, w3_scale = quantize("w3", w3_bf)
         for c in range(3):
             weave(c, ("scalar",))
         codes = [quantize(f"z{c}", z_bf[c]) for c in range(1)]

@@ -238,7 +238,7 @@ def tile_picked_edgecv_relu_p_kernel(
         near = buffer("near", [P, TILES, V], F32)
         far = buffer("far", [P, TILES, V], F32)
         for t in range(1, TILES):
-            empty("w2", t, 1 if t == 2 else None)
+            empty("w2", t)
         for t in range(TILES):
             engine = "vector" if t < 2 else "scalar"
             fetch(engine, near[:, t, :], t, pos1_t)

@@ -28,7 +28,7 @@ RUN = 4
 RUNS = P // RUN
 LEAD_SPLIT = 20
 CHUNK = 128
-WARM_PASSES = 4
+WARM_PASSES = (2, 4)
 
 FIRST_BANK = {"w2": (0, 2, 4, 2), "w1": (6, 0, 4, 2)}
 LEAD_PIECES = ((0, 512, 0), (512, 768, 1), (768, 1024, 6))
@@ -203,17 +203,20 @@ def tile_picked_edgecv_relu_p_kernel(
         cast("scalar", early[1], 1, "w2", 0, 3)
         for n in range(2):
             quantize_units(f"early{n}", early[n], "w2", [(0, 2 * n), (0, 2 * n + 1)])
-        warm = psum.tile([P, 2 * P], F32, name="warm", tag="bank7")
-        for n in range(WARM_PASSES):
-            nc.tensor.matmul_mx(
-                out=warm[:],
-                lhsT=quantized["w2", 0, 0][0].bitcast(FP8X4),
-                lhsT_scale=quantized["w2", 0, 0][1],
-                rhs=whole["early0"][0][:].bitcast(FP8X4),
-                rhs_scale=whole["early0"][1][:],
-                start=True,
-                stop=True,
-            )
+        def warm_up(name, bank, passes):
+            warm = psum.tile([P, 2 * P], F32, name=name, tag=f"bank{bank}")
+            for n in range(passes):
+                nc.tensor.matmul_mx(
+                    out=warm[:],
+                    lhsT=quantized["w2", 0, 0][0].bitcast(FP8X4),
+                    lhsT_scale=quantized["w2", 0, 0][1],
+                    rhs=whole["early0"][0][:].bitcast(FP8X4),
+                    rhs_scale=whole["early0"][1][:],
+                    start=True,
+                    stop=True,
+                )
+
+        warm_up("warm_head", 7, WARM_PASSES[0])
         for t in range(3):
             multiply("w2", 0, t)
         pick_words(1, "w2_raw0")
@@ -239,6 +242,7 @@ def tile_picked_edgecv_relu_p_kernel(
         far = buffer("far", [P, TILES, V], F32)
         for t in range(1, TILES):
             empty("w2", t)
+        warm_up("warm_middle", 3, WARM_PASSES[1])
         for t in range(TILES):
             engine = "vector" if t < 2 else "scalar"
             fetch(engine, near[:, t, :], t, pos1_t)

@@ -28,7 +28,8 @@ RUN = 4
 RUNS = P // RUN
 LEAD_SPLIT = 20
 CHUNK = 128
-WARM_PASSES = (2, 4)
+WARM_PASSES = (2, 2, 4)
+NARROW = 32
 
 FIRST_BANK = {"w2": (0, 2, 4, 2), "w1": (6, 0, 4, 2)}
 LEAD_PIECES = ((0, 512, 0), (512, 768, 1), (768, 1024, 6))
@@ -216,6 +217,19 @@ def tile_picked_edgecv_relu_p_kernel(
                     stop=True,
                 )
 
+        def warm_up_narrow(name, bank, passes):
+            warm = psum.tile([NARROW, BANK], F32, name=name, tag=f"bank{bank}")
+            for n in range(passes):
+                nc.tensor.matmul_mx(
+                    out=warm[:],
+                    lhsT=quantized["w2", 0, 0][0][:, :NARROW].bitcast(FP8X4),
+                    lhsT_scale=quantized["w2", 0, 0][1][:, :NARROW],
+                    rhs=x_code[0][:, :BANK].bitcast(FP8X4),
+                    rhs_scale=x_scale[0][:, :BANK],
+                    start=True,
+                    stop=True,
+                )
+
         warm_up("warm_head", 7, WARM_PASSES[0])
         for t in range(3):
             multiply("w2", 0, t)
@@ -242,7 +256,7 @@ def tile_picked_edgecv_relu_p_kernel(
         far = buffer("far", [P, TILES, V], F32)
         for t in range(1, TILES):
             empty("w2", t)
-        warm_up("warm_middle", 3, WARM_PASSES[1])
+        warm_up_narrow("warm_middle", 3, WARM_PASSES[1])
         for t in range(TILES):
             engine = "vector" if t < 2 else "scalar"
             fetch(engine, near[:, t, :], t, pos1_t)
@@ -267,6 +281,7 @@ def tile_picked_edgecv_relu_p_kernel(
                 for z in range(PASSES):
                     multiply("w1", z, t, h)
             empty("w1", t)
+        warm_up_narrow("warm_tail", 3, WARM_PASSES[2])
 
         best = buffer("best", [P, TILES, V], F32, BEST)
         nc.vector.tensor_tensor(best[:, :2, :], near[:, :2, :], far[:, :2, :], ALU.max)

from contextlib import ExitStack

import concourse.mybir as mybir

K, T, S, V, H, N = 1024, 2048, 1024, 512, 512, 256
FLOPS = 2 * (2 * K * H * S + H * N * V)

F32 = mybir.dt.float32
BF16 = mybir.dt.bfloat16
I32 = mybir.dt.int32
U32 = mybir.dt.uint32
U16 = mybir.dt.uint16
U8 = mybir.dt.uint8
FP8X4 = mybir.dt.float8_e4m3fn_x4
ACT = mybir.ActivationFunctionType
ALU = mybir.AluOpType

P = 128
PACK = 4
K_PASS = P * PACK
PASSES = K // K_PASS
BANK = 512
HALVES = S // BANK
LIST_ROWS = 16
SCALE_ROWS = 32
TILES = H // P
RUN = 4
RUNS = P // RUN
LEAD_SPLIT = 20
CHUNK = 128
WARM_PASSES = (2, 2, 4)
NARROW = 32

FIRST_BANK = {"w2": (0, 2, 4, 2), "w1": (6, 0, 4, 2)}
LEAD_PIECES = ((0, 512, 0), (512, 768, 1), (768, 1024, 6))
OUT_BANK = (6, 7, 0, 4)

PAIR_STAGE, BEST = 0, 4032
REST_STAGE, MIXED_CODES, PAIR_CODES = 14208, 17216, 17280


def tile_picked_edgecv_relu_p_kernel(
    tc, x_words, x_scales, w1, w2, w3, offs, cen, pos1, pos2, out
):
    nc = tc.nc
    with ExitStack() as ctx:
        keep = ctx.enter_context(tc.tile_pool(name="keep", bufs=1))
        lane = ctx.enter_context(tc.tile_pool(name="lane", bufs=1))
        psum = ctx.enter_context(tc.psum_pool(name="psum", bufs=1))

        def buffer(name, shape, dtype, at=None, tag=None):
            if at is None:
                return keep.tile(shape, dtype, name=name, tag=tag or name, align_bytes=64)
            return lane.tile(shape, dtype, name=name, offset=at, align_bytes=64)

        def load_list(name, src):
            lst = keep.tile(list(src.shape), U16, name=name)
            nc.sync.dma_start(lst[:], src)
            return lst

        def load_words(z):
            table = buffer(f"x_table{z}", [P, T], U32)
            nc.sync.dma_start(
                table[:].bitcast(I32), x_words[z].rearrange("p c r -> p (c r)").bitcast(I32)
            )
            return table

        raw = {}

        def load_weight(name, w, z, at=None):
            raw[name, z] = buffer(f"{name}_raw{z}", [P, PACK, H], F32, at)
            rows = w[z * K_PASS : (z + 1) * K_PASS, :]
            nc.sync.dma_start(raw[name, z][:], rows.rearrange("(p j) c -> p j c", j=PACK))

        scale_table = keep.tile([P, T], U8, name="scale_table")
        nc.sync.dma_start(
            scale_table[:SCALE_ROWS, :].bitcast(I32), x_scales.rearrange("z q c -> (z q) c").bitcast(I32)
        )
        nc.vector.memset(scale_table[SCALE_ROWS : P // 2, :].bitcast(I32), 0)
        nc.vector.memset(scale_table[P // 2 :, :].bitcast(I32), 0)
        x_scale = [buffer(f"x_scale{z}", [P, S], U8) for z in range(PASSES)]
        for plane in x_scale:
            nc.gpsimd.memset(plane[:].bitcast(I32), 0)

        offs_t = load_list("offs_t", offs)
        x_table = [load_words(0)]
        load_weight("w2", w2, 0)
        x_table.append(load_words(1))

        picked_scale = buffer("picked_scale", [P, S], U8)
        nc.vector.tensor_copy(picked_scale[:], scale_table[:].indirect(offs_t[:]))

        def place_scales(queue, z, quadrants):
            for q in quadrants:
                queue.dma_start(
                    x_scale[z][32 * q : 32 * q + 4, :].bitcast(I32),
                    picked_scale[16 * z + 4 * q : 16 * z + 4 * q + 4, :].bitcast(I32),
                )

        place_scales(nc.scalar, 0, range(4))
        place_scales(nc.scalar, 1, range(2))
        load_weight("w2", w2, 1)
        place_scales(nc.sync, 1, range(2, 4))
        pos1_t = load_list("pos1_t", pos1)
        load_weight("w1", w1, 0)
        pos2_t = load_list("pos2_t", pos2)
        load_weight("w1", w1, 1)
        cen_t = load_list("cen_t", cen)
        w3_raw = buffer("w3_raw", [P, PACK, N], F32)
        w3_rows = w3.rearrange("(a t b) n -> t a b n", t=TILES, b=RUN)
        for t in range(TILES):
            nc.sync.dma_start(w3_raw[:, t, :], w3_rows[t])

        def cast(engine, stage, slot, name, z, t, first=0, last=RUNS):
            step = RUN * PACK
            dst = stage[:, slot * K_PASS + first * step : slot * K_PASS + last * step]
            src = raw[name, z][:].rearrange("p j (a t i) -> p t a j i", t=TILES, i=RUN)[:, t, first:last]
            if engine == "gpsimd":
                nc.gpsimd.tensor_scalar(
                    dst.rearrange("p (a i j) -> p a i j", i=RUN, j=PACK),
                    src.rearrange("p a j i -> p a i j"),
                    1.0,
                    0.0,
                    ALU.mult,
                    ALU.add,
                )
            elif engine == "vector":
                nc.vector.tensor_copy(dst.rearrange("p (a i j) -> p a j i", i=RUN, j=PACK), src)
            else:
                nc.scalar.activation(dst.rearrange("p (a i j) -> p a j i", i=RUN, j=PACK), src, ACT.Copy)

        def quantize(name, stage, at=None, tag=None, scale_tag=None):
            width = stage.shape[1] // PACK
            codes = buffer(f"{name}_code", [P, width], U32, at, tag)
            scales = buffer(f"{name}_scale", [P, width], U8, tag=scale_tag)
            nc.vector.quantize_mx(out=codes[:].bitcast(FP8X4), scales=scales[:], in_=stage[:])
            return codes, scales

        quantized, whole = {}, {}

        def quantize_units(label, stage, name, units, at=None, scale_tag=None):
            codes, scales = quantize(label, stage, at, None, scale_tag)
            whole[label] = (codes, scales)
            for slot, (z, t) in enumerate(units):
                cols = slice(slot * P, (slot + 1) * P)
                quantized[name, z, t] = (codes[:, cols], scales[:, cols])

        x_code = {}

        def pick_words(z, tag=None):
            x_code[z] = buffer(f"x_code{z}", [P, S], U32, tag=tag)
            nc.vector.tensor_copy(x_code[z][:], x_table[z][:].indirect(offs_t[:]))

        banks = {}

        def pieces(name, t):
            if (name, t) == ("w2", 0):
                return LEAD_PIECES
            return [(h * BANK, (h + 1) * BANK, FIRST_BANK[name][t] + h) for h in range(HALVES)]

        def multiply(name, z, t, only=None):
            codes, scales = quantized[name, z, t]
            for h, (a, b, bank) in enumerate(pieces(name, t)):
                if only not in (None, h):
                    continue
                if z == 0:
                    banks[name, t, h] = psum.tile([P, b - a], F32, name=f"{name}_acc{t}{h}", tag=f"bank{bank}")
                cols = slice(a, b)
                nc.tensor.matmul_mx(
                    out=banks[name, t, h][:],
                    lhsT=codes.bitcast(FP8X4),
                    lhsT_scale=scales,
                    rhs=x_code[z][:, cols].bitcast(FP8X4),
                    rhs_scale=x_scale[z][:, cols],
                    start=(z == 0),
                    stop=(z == PASSES - 1),
                )

        rows = {}

        def empty(name, t, on_vector=None):
            rows[name, t] = buffer(f"{name}_rows{t}", [P, S], F32)
            for h, (a, b, bank) in enumerate(pieces(name, t)):
                dst = rows[name, t][:, a:b]
                if h == on_vector:
                    nc.vector.tensor_copy(dst, banks[name, t, h][:])
                else:
                    nc.scalar.activation(dst, banks[name, t, h][:], ACT.Copy)

        def fetch(engine, dst, t, lst):
            window = rows["w2", t][:].indirect(lst[:])
            if engine == "vector":
                nc.vector.tensor_copy(dst, window)
            else:
                nc.scalar.activation(dst, window, ACT.Copy)

        pick_words(0)
        early = [buffer(f"early_bf{n}", [P, 2 * K_PASS], BF16) for n in range(2)]
        nc.vector.tensor_copy(
            early[0][:].rearrange("p (t a i j) -> p a t j i", t=2, i=RUN, j=PACK),
            raw["w2", 0][:].rearrange("p j (a t i) -> p a t j i", t=TILES, i=RUN)[:, :, :2],
        )
        cast("vector", early[1], 0, "w2", 0, 2)
        cast("scalar", early[1], 1, "w2", 0, 3)
        for n in range(2):
            quantize_units(f"early{n}", early[n], "w2", [(0, 2 * n), (0, 2 * n + 1)])
        def warm_up(name, bank, passes):
            warm = psum.tile([P, 2 * P], F32, name=name, tag=f"bank{bank}")
            for n in range(passes):
                nc.tensor.matmul_mx(
                    out=warm[:],
                    lhsT=quantized["w2", 0, 0][0].bitcast(FP8X4),
                    lhsT_scale=quantized["w2", 0, 0][1],
                    rhs=whole["early0"][0][:].bitcast(FP8X4),
                    rhs_scale=whole["early0"][1][:],
                    start=True,
                    stop=True,
                )

        def warm_up_narrow(name, bank, passes):
            warm = psum.tile([NARROW, BANK], F32, name=name, tag=f"bank{bank}")
            for n in range(passes):
                nc.tensor.matmul_mx(
                    out=warm[:],
                    lhsT=quantized["w2", 0, 0][0][:, :NARROW].bitcast(FP8X4),
                    lhsT_scale=quantized["w2", 0, 0][1][:, :NARROW],
                    rhs=x_code[0][:, :BANK].bitcast(FP8X4),
                    rhs_scale=x_scale[0][:, :BANK],
                    start=True,
                    stop=True,
                )

        warm_up("warm_head", 7, WARM_PASSES[0])
        for t in range(3):
            multiply("w2", 0, t)
        pick_words(1, "w2_raw0")
        mixed = buffer("mixed_bf", [P, K_PASS], BF16)
        lead = buffer("lead_bf", [P, K_PASS], BF16)
        cast("scalar", lead, 0, "w2", 1, 0, last=LEAD_SPLIT)
        cast("gpsimd", lead, 0, "w2", 1, 0, first=LEAD_SPLIT)
        quantize_units("lead", lead, "w2", [(1, 0)])
        multiply("w2", 1, 0)
        third = buffer("third_bf", [P, 2 * K_PASS], BF16, tag="lead_bf")
        cast("vector", third, 1, "w2", 1, 3)
        cast("scalar", mixed, 0, "w2", 1, 1)
        quantize_units("mixed", mixed, "w2", [(1, 1)])
        cast("scalar", third, 0, "w2", 1, 2)
        empty("w2", 0, 0)
        quantize_units("third", third, "w2", [(1, 2), (1, 3)], at=MIXED_CODES)
        multiply("w2", 1, 1)
        multiply("w2", 1, 2)
        multiply("w2", 0, 3)
        multiply("w2", 1, 3)

        near = buffer("near", [P, TILES, V], F32)
        far = buffer("far", [P, TILES, V], F32)
        for t in range(1, TILES):
            empty("w2", t)
        warm_up_narrow("warm_middle", 3, WARM_PASSES[1])
        for t in range(TILES):
            engine = "vector" if t < 2 else "scalar"
            fetch(engine, near[:, t, :], t, pos1_t)
            fetch(engine, far[:, t, :], t, pos2_t)

        pair = buffer("pair_bf", [P, 4 * K_PASS], BF16, PAIR_STAGE)
        single = buffer("single_bf", [P, K_PASS], BF16)
        pair_units = [(0, 0), (0, 1), (0, 2), (1, 0)]
        for slot, (z, t) in enumerate(pair_units):
            cast("gpsimd", pair, slot, "w1", z, t)
        cast("gpsimd", single, 0, "w1", 0, 3)
        rest = buffer("rest_bf", [P, 3 * K_PASS], BF16, REST_STAGE)
        nc.vector.tensor_copy(
            rest[:].rearrange("p (t a i j) -> p a t j i", t=3, i=RUN, j=PACK),
            raw["w1", 1][:].rearrange("p j (a t i) -> p a t j i", t=TILES, i=RUN)[:, :, 1:],
        )
        quantize_units("pair", pair, "w1", pair_units, at=PAIR_CODES)
        quantize_units("single", single, "w1", [(0, 3)], scale_tag="third_scale")
        quantize_units("rest", rest, "w1", [(1, 1), (1, 2), (1, 3)])
        for t in range(TILES):
            for h in range(HALVES):
                for z in range(PASSES):
                    multiply("w1", z, t, h)
            empty("w1", t)
        warm_up_narrow("warm_tail", 3, WARM_PASSES[2])

        best = buffer("best", [P, TILES, V], F32, BEST)
        nc.vector.tensor_tensor(best[:, :2, :], near[:, :2, :], far[:, :2, :], ALU.max)
        nc.vector.tensor_tensor(best[:, 2:, :], near[:, 2:, :], far[:, 2:, :], ALU.max)

        w3_bf = buffer("w3_bf", [P, 2 * K_PASS], BF16, tag="rest_code")
        nc.scalar.activation(
            w3_bf[:].rearrange("p (a i j) -> p a j i", i=RUN, j=PACK),
            w3_raw[:].rearrange("p j (a i) -> p a j i", i=RUN),
            ACT.Copy,
        )
        sums = buffer("sums", [P, TILES * V], F32)

        def add_centres(t, a, b):
            centres = cen_t[:, a // LIST_ROWS : b // LIST_ROWS]
            nc.vector.tensor_tensor(sums[:, t * V + a : t * V + b], rows["w1", t][:].indirect(centres), best[:, t, a:b], ALU.add)

        out_view = out.rearrange("(u p) v -> p u v", p=P)
        z_bf = {}

        def weave(c, engines):
            z_bf[c] = buffer(f"z_bf{c}", [P, CHUNK * PACK], BF16, tag=f"z_bf{(0, 1, 2, 0)[c]}")
            dst = z_bf[c][:].rearrange("p (a i t) -> p a t i", i=RUN, t=TILES)
            src = sums[:].rearrange("p (t c a i) -> p c a t i", t=TILES, c=V // CHUNK, i=RUN)[:, c]
            share = CHUNK // RUN // len(engines)
            for n, engine in enumerate(engines):
                part = slice(n * share, (n + 1) * share)
                if engine == "vector":
                    nc.vector.tensor_scalar_max(dst[:, part], src[:, part], 0.0)
                else:
                    nc.scalar.activation(dst[:, part], src[:, part], ACT.Relu)

        def project(c, engines):
            z_code, z_scale = codes[c]
            if len(engines) > 1:
                acc = [psum.tile([P, CHUNK], F32, name=f"out_acc{c}{u}", tag=f"bank{OUT_BANK[c] + u}")[:] for u in range(N // P)]
            else:
                both = psum.tile([P, N // P, CHUNK], F32, name=f"out_acc{c}", tag=f"bank{OUT_BANK[c]}")
                acc = [both[:, u, :] for u in range(N // P)]
            for u in range(N // P):
                nc.tensor.matmul_mx(
                    out=acc[u],
                    lhsT=w3_code[:, u * P : (u + 1) * P].bitcast(FP8X4),
                    lhsT_scale=w3_scale[:, u * P : (u + 1) * P],
                    rhs=z_code[:].bitcast(FP8X4),
                    rhs_scale=z_scale[:],
                    start=True,
                    stop=True,
                )
            result = buffer(f"result{c}", [P, N // P, CHUNK], F32)
            parts = [(result[:, u, :], acc[u]) for u in range(N // P)] if len(engines) > 1 else [(result[:], both[:])]
            for engine, (dst, src) in zip(engines, parts):
                if engine == "vector":
                    nc.vector.tensor_copy(dst, src)
                else:
                    nc.scalar.activation(dst, src, ACT.Copy)
            cols = slice(c * CHUNK, (c + 1) * CHUNK)
            if len(engines) > 1:
                nc.scalar.dma_start(out_view[:, 0, cols], result[:, 0, :])
                nc.sync.dma_start(out_view[:, 1, cols], result[:, 1, :])
            else:
                nc.sync.dma_start(out_view[:, :, cols], result[:])

        for t in range(TILES - 1):
            add_centres(t, 0, V)
        for c in range(V // CHUNK):
            add_centres(TILES - 1, c * CHUNK, (c + 1) * CHUNK)
        w3_code, w3_scale = quantize("w3", w3_bf)
        for c in range(3):
            weave(c, ("scalar",))
        codes = [quantize(f"z{c}", z_bf[c]) for c in range(1)]
        weave(3, ("vector",))
        codes.extend(quantize(f"z{c}", z_bf[c]) for c in range(1, 4))
        for c, engines in enumerate((("scalar",), ("scalar",), ("scalar", "vector"), ("scalar", "vector"))):
            project(c, engines)
